import numpy as np
import ml_dtypes


def mxq(x, axis, fmt="e4m3"):
    dtype, down = {"e4m3": (ml_dtypes.float8_e4m3fn, 7), "e5m2": (ml_dtypes.float8_e5m2, 14)}[fmt]
    v = np.moveaxis(np.asarray(x, np.float32).astype(ml_dtypes.bfloat16).astype(np.float64), axis, -1)
    blocks = v.reshape(v.shape[:-1] + (-1, 32))
    amax = np.abs(blocks).max(-1, keepdims=True)
    byte = np.maximum(np.where(amax > 0, np.frexp(amax)[1] - 1 + 127, 0) - down, 1)
    scale = np.exp2(byte - 127.0)
    codes = (blocks / scale).astype(np.float32).astype(dtype).astype(np.float64)
    return np.moveaxis((codes * scale).reshape(v.shape), -1, axis)


WIDE = False


def mx_kscale(k):
    if not WIDE:
        return np.ones(k)
    levels = np.array([10, -10, 5, -5, 0])
    if k % 512:
        return np.exp2(np.random.permutation(np.resize(levels, k // 32))).repeat(32)
    a = np.empty((k // 512, 16))
    for p in range(k // 512):
        a[p, :8] = np.random.permutation(np.resize(levels, 8))
        for g in range(8):
            far = levels[np.abs(levels - a[p, g]) >= 10]
            a[p, g + 8] = far[np.random.randint(len(far))]
    return np.exp2(a.ravel()).repeat(32)


def f64(x):
    return np.asarray(x).astype(np.float64)


def striped(idx):
    return np.tile(idx.reshape(-1, 16).T, (8, 1)).astype(np.uint16)


def unstriped(offs):
    return offs[:16].T.reshape(-1).astype(np.int64)


def striped8(idx):
    return np.concatenate([x.reshape(-1, 16).T for x in idx]).astype(np.uint16)


def runs(offs, k):
    lists = np.stack([offs[16 * r : 16 * r + 16].T.reshape(-1) for r in range(8)]).astype(np.int64)
    return lists[np.arange(k) % 512 // 64]


def pack_weight(w):
    k, n = w.shape
    w = f64(np.asarray(w, np.float32).astype(ml_dtypes.bfloat16)).reshape(k // 32, 32, n)
    amax = np.abs(w).max(1)
    byte = np.clip(np.where(amax > 0, np.frexp(amax)[1] - 1 + 127 - 7, 1), 1, 254)
    scaled = (w * np.exp2(127.0 - byte)[:, None, :]).reshape(k, n).astype(np.float32)
    words = np.ascontiguousarray(scaled.reshape(k // 512, 128, 4, n).transpose(0, 1, 3, 2)).astype(ml_dtypes.float8_e4m3fn).view(np.uint8)
    return words, np.ascontiguousarray(byte.astype(np.uint8).reshape(k // 512, 16, n))


def unpack_weight(words, scales):
    g, p, n, _ = words.shape
    vals = np.ascontiguousarray(words).view(ml_dtypes.float8_e4m3fn).astype(np.float64) * np.repeat(np.exp2(scales.astype(np.float64) - 127.0), 8, axis=1)[..., None]
    return vals.transpose(0, 1, 3, 2).reshape(g * 512, n)


K, T, S, N, H, U = 512, 2048, 512, 512, 512, 512


def setup_inputs():
    n = np.random.standard_normal
    s = mx_kscale(K)[:, None]
    u = mx_kscale(H)
    packed_xT = pack_weight(n((K, T)) * s)
    return {
        "x_words": packed_xT[0],
        "x_scales": packed_xT[1],
        "w1": (n((K, H)) / np.sqrt(K) / s * u).astype(np.float32),
        "rin": np.random.uniform(0.5, 1.5, (H, U)).astype(np.float32),
        "w2": (n((H, N)) / np.sqrt(H) / u[:, None]).astype(np.float32),
        "so": np.random.uniform(0.5, 1.5, (N, U)).astype(np.float32),
        "offs": striped(np.random.permutation(T)[:S]),
        "mem": striped8(np.stack([np.random.permutation(U)[(U * np.random.uniform(0, 1, S) ** 4).astype(np.int64)] for _ in range(8)])),
    }


def reference(x_words, x_scales, w1, rin, w2, so, offs, mem):
    xq = unpack_weight(x_words, x_scales)[:, unstriped(offs)]
    h = mxq(f64(w1), 0, "e4m3").T @ xq
    z = h * (f64(rin)[np.arange(H)[:, None], runs(mem, H)])
    o = mxq(f64(w2), 0, "e4m3").T @ mxq(z, 0, "e4m3")
    return o * (f64(so)[np.arange(N)[:, None], runs(mem, N)])

@@ -1,0 +1,165 @@
+from contextlib import ExitStack
+
+import concourse.mybir as mybir
+
+K, T, S, H, N, U = 512, 2048, 512, 512, 512, 512
+FLOPS = 2 * K * H * S + 2 * H * N * S
+
+F32 = mybir.dt.float32
+BF16 = mybir.dt.bfloat16
+I32 = mybir.dt.int32
+U32 = mybir.dt.uint32
+U16 = mybir.dt.uint16
+U8 = mybir.dt.uint8
+FP8X4 = mybir.dt.float8_e4m3fn_x4
+MULT = mybir.AluOpType.mult
+
+P = 128
+PACK = 4
+HALF = 256
+QUARTER = 128
+LIST_ROWS = 16
+
+
+def plane_rows(table, t):
+    return table.rearrange("(q t r) u -> t q r u", t=PACK, r=8)[t]
+
+
+def cast_weight_plane(nc, raw, grouped, t):
+    nc.scalar.copy(
+        out=grouped[:].rearrange("p (t q r i j) -> p t q r j i", t=PACK, r=4, i=2, j=PACK)[:, t],
+        in_=raw[:].rearrange("p j (q t r i) -> p t q r j i", t=PACK, r=4, i=2)[:, t],
+    )
+
+
+def quantize_weight_plane(nc, grouped, codes, scales, t):
+    cols = slice(t * P, (t + 1) * P)
+    nc.vector.quantize_mx(
+        out=codes[:, cols].bitcast(FP8X4),
+        scales=scales[:, cols],
+        in_=grouped[:, t * P * PACK : (t + 1) * P * PACK],
+    )
+
+
+def tile_picked_bens8_none_p_kernel(tc, x_words, x_scales, w1, rin, w2, so, offs, mem, out):
+    nc = tc.nc
+    with ExitStack() as ctx:
+        keep = ctx.enter_context(tc.tile_pool(name="keep", bufs=1))
+        psum = ctx.enter_context(tc.psum_pool(name="psum", bufs=1))
+
+        mem_sb = keep.tile([P, S // LIST_ROWS], U16, name="mem_sb")
+        offs_sb = keep.tile([P, S // LIST_ROWS], U16, name="offs_sb")
+        rin_sb = [keep.tile([P, U], F32, name=f"rin_sb{t}") for t in range(PACK)]
+        so_sb = [keep.tile([P, U], F32, name=f"so_sb{t}") for t in range(PACK)]
+        xw_sb = keep.tile([P, T], I32, name="xw_sb")
+        xs_sb = keep.tile([P, T], U8, name="xs_sb")
+        w1_raw = keep.tile([P, PACK, H], F32, name="w1_raw")
+        w2_raw = keep.tile([P, PACK, N], F32, name="w2_raw")
+
+        nc.vector.memset(xs_sb[:].bitcast(I32), 0)
+
+        nc.sync.dma_start(mem_sb[:], mem)
+        nc.sync.dma_start(rin_sb[0][:], plane_rows(rin, 0))
+        for quad in range(4):
+            nc.sync.dma_start(
+                xs_sb[32 * quad : 32 * quad + 4, :].bitcast(I32),
+                x_scales[0, 4 * quad : 4 * quad + 4, :].bitcast(I32),
+            )
+        for t in range(1, PACK):
+            nc.sync.dma_start(rin_sb[t][:], plane_rows(rin, t))
+        nc.sync.dma_start(offs_sb[:], offs)
+        nc.sync.dma_start(w1_raw[:], w1.rearrange("(p j) c -> p j c", j=PACK))
+        nc.sync.dma_start(xw_sb[:], x_words[0].rearrange("p n r -> p (n r)").bitcast(I32))
+        for j in range(PACK):
+            nc.sync.dma_start(w2_raw[:, j, :], plane_rows(w2, j))
+        for t in range(PACK):
+            nc.sync.dma_start(so_sb[t][:], plane_rows(so, t))
+
+        def list_half(list_sb, c):
+            return list_sb[:, c * HALF // LIST_ROWS : (c + 1) * HALF // LIST_ROWS]
+
+        rin_picked = [keep.tile([P, PACK, HALF], F32, name=f"rin_picked{c}") for c in range(2)]
+        for t in range(PACK):
+            for c in range(2):
+                nc.vector.tensor_copy(rin_picked[c][:, t, :], rin_sb[t][:].indirect(list_half(mem_sb, c)))
+
+        x_scale_picked = keep.tile([P, S], U8, name="x_scale_picked", align_bytes=64)
+        nc.vector.tensor_copy(x_scale_picked[:], xs_sb[:].indirect(offs_sb[:]))
+
+        w1_grouped = keep.tile([P, PACK * H], BF16, name="w1_grouped", align_bytes=64)
+        w1_codes = keep.tile([P, H], U32, name="w1_codes", align_bytes=64)
+        w1_scales = keep.tile([P, H], U8, name="w1_scales", align_bytes=64)
+        for t in range(PACK):
+            cast_weight_plane(nc, w1_raw, w1_grouped, t)
+            quantize_weight_plane(nc, w1_grouped, w1_codes, w1_scales, t)
+
+        x_picked = [keep.tile([P, HALF], U32, name=f"x_picked{c}", align_bytes=64) for c in range(2)]
+        for c in range(2):
+            nc.vector.tensor_copy(x_picked[c][:], xw_sb[:].bitcast(U32).indirect(list_half(offs_sb, c)))
+
+        w2_grouped = keep.tile([P, PACK * N], BF16, name="w2_grouped", align_bytes=64)
+        w2_codes = keep.tile([P, N], U32, name="w2_codes", align_bytes=64)
+        w2_scales = keep.tile([P, N], U8, name="w2_scales", align_bytes=64)
+
+        z_grouped = [keep.tile([P, PACK * HALF], BF16, name=f"z_grouped{c}", align_bytes=64) for c in range(2)]
+        z_codes = [keep.tile([P, HALF], U32, name=f"z_codes{c}", align_bytes=64) for c in range(2)]
+        z_scales = [keep.tile([P, HALF], U8, name=f"z_scales{c}", align_bytes=64) for c in range(2)]
+
+        def hidden_quarter(c, s):
+            cols = slice(s * QUARTER, (s + 1) * QUARTER)
+            all_cols = slice(c * HALF + s * QUARTER, c * HALF + (s + 1) * QUARTER)
+            h_bank = psum.tile([P, PACK, QUARTER], F32, name=f"h_bank{c}{s}")
+            for t in range(PACK):
+                nc.tensor.matmul_mx(
+                    out=h_bank[:, t, :],
+                    lhsT=w1_codes[:, t * P : (t + 1) * P].bitcast(FP8X4),
+                    lhsT_scale=w1_scales[:, t * P : (t + 1) * P],
+                    rhs=x_picked[c][:, cols].bitcast(FP8X4),
+                    rhs_scale=x_scale_picked[:, all_cols],
+                    start=True,
+                    stop=True,
+                )
+            nc.vector.tensor_tensor(
+                z_grouped[c][:, s * QUARTER * PACK : (s + 1) * QUARTER * PACK].rearrange(
+                    "p (c i t) -> p c t i", i=2, t=PACK
+                ),
+                h_bank[:].rearrange("p t (c i) -> p c t i", i=2),
+                rin_picked[c][:, :, cols].rearrange("p t (c i) -> p c t i", i=2),
+                MULT,
+            )
+
+        def quantize_z(c):
+            nc.vector.quantize_mx(out=z_codes[c][:].bitcast(FP8X4), scales=z_scales[c][:], in_=z_grouped[c][:])
+
+        hidden_quarter(0, 0)
+        hidden_quarter(0, 1)
+        hidden_quarter(1, 0)
+        quantize_z(0)
+        for t in range(PACK):
+            cast_weight_plane(nc, w2_raw, w2_grouped, t)
+            quantize_weight_plane(nc, w2_grouped, w2_codes, w2_scales, t)
+        hidden_quarter(1, 1)
+        quantize_z(1)
+
+        out_rows = out.rearrange("(q t r) s -> t q r s", t=PACK, r=8)
+        for c in range(2):
+            for pair in range(2):
+                o_bank = psum.tile([P, 2, HALF], F32, name=f"o_bank{c}{pair}")
+                for e in range(2):
+                    t = 2 * pair + e
+                    nc.tensor.matmul_mx(
+                        out=o_bank[:, e, :],
+                        lhsT=w2_codes[:, t * P : (t + 1) * P].bitcast(FP8X4),
+                        lhsT_scale=w2_scales[:, t * P : (t + 1) * P],
+                        rhs=z_codes[c][:].bitcast(FP8X4),
+                        rhs_scale=z_scales[c][:],
+                        start=True,
+                        stop=True,
+                    )
+                for e in range(2):
+                    t = 2 * pair + e
+                    o_sb = keep.tile([P, HALF], F32, name=f"o_sb{c}{t}")
+                    result = keep.tile([P, HALF], F32, name=f"result{c}{t}")
+                    nc.scalar.copy(out=o_sb[:], in_=o_bank[:, e, :])
+                    nc.vector.tensor_tensor(result[:], so_sb[t][:].indirect(list_half(mem_sb, c)), o_sb[:], MULT)
+                    nc.sync.dma_start(out_rows[t][:, :, c * HALF : (c + 1) * HALF], result[:])

@@ -27,17 +27,17 @@ def plane_rows(table, t):
 
 def cast_weight_plane(nc, raw, grouped, t):
     nc.scalar.copy(
-        out=grouped[:].rearrange("p (t q r i j) -> p t q r j i", t=PACK, r=4, i=2, j=PACK)[:, t],
+        out=grouped.rearrange("p (t q r i j) -> p t q r j i", t=PACK, r=4, i=2, j=PACK)[:, t],
         in_=raw[:].rearrange("p j (q t r i) -> p t q r j i", t=PACK, r=4, i=2)[:, t],
     )
 
 
-def quantize_weight_plane(nc, grouped, codes, scales, t):
-    cols = slice(t * P, (t + 1) * P)
+def quantize_weight_pair(nc, grouped, codes, scales, pair):
+    cols = slice(2 * pair * P, 2 * (pair + 1) * P)
     nc.vector.quantize_mx(
         out=codes[:, cols].bitcast(FP8X4),
         scales=scales[:, cols],
-        in_=grouped[:, t * P * PACK : (t + 1) * P * PACK],
+        in_=grouped[:, 2 * pair * P * PACK : 2 * (pair + 1) * P * PACK],
     )
 
 
@@ -49,7 +49,7 @@ def tile_picked_bens8_none_p_kernel(tc, x_words, x_scales, w1, rin, w2, so, offs
 
         mem_sb = keep.tile([P, S // LIST_ROWS], U16, name="mem_sb")
         offs_sb = keep.tile([P, S // LIST_ROWS], U16, name="offs_sb")
-        rin_sb = [keep.tile([P, U], F32, name=f"rin_sb{t}") for t in range(PACK)]
+        rin_sb = [keep.tile([P, 2 * U], F32, name=f"rin_sb{t}") for t in range(PACK)]
         so_sb = [keep.tile([P, U], F32, name=f"so_sb{t}") for t in range(PACK)]
         xw_sb = keep.tile([P, T], I32, name="xw_sb")
         xs_sb = keep.tile([P, T], U8, name="xs_sb")
@@ -59,16 +59,17 @@ def tile_picked_bens8_none_p_kernel(tc, x_words, x_scales, w1, rin, w2, so, offs
         nc.vector.memset(xs_sb[:].bitcast(I32), 0)
 
         nc.sync.dma_start(mem_sb[:], mem)
-        nc.sync.dma_start(rin_sb[0][:], plane_rows(rin, 0))
+        nc.sync.dma_start(rin_sb[0][:, :U], plane_rows(rin, 0))
         for quad in range(4):
             nc.sync.dma_start(
                 xs_sb[32 * quad : 32 * quad + 4, :].bitcast(I32),
                 x_scales[0, 4 * quad : 4 * quad + 4, :].bitcast(I32),
             )
-        for t in range(1, PACK):
-            nc.sync.dma_start(rin_sb[t][:], plane_rows(rin, t))
+        nc.sync.dma_start(rin_sb[1][:, :U], plane_rows(rin, 1))
         nc.sync.dma_start(offs_sb[:], offs)
+        nc.sync.dma_start(rin_sb[2][:, :U], plane_rows(rin, 2))
         nc.sync.dma_start(w1_raw[:], w1.rearrange("(p j) c -> p j c", j=PACK))
+        nc.sync.dma_start(rin_sb[3][:, :U], plane_rows(rin, 3))
         nc.sync.dma_start(xw_sb[:], x_words[0].rearrange("p n r -> p (n r)").bitcast(I32))
         for j in range(PACK):
             nc.sync.dma_start(w2_raw[:, j, :], plane_rows(w2, j))
@@ -78,10 +79,9 @@ def tile_picked_bens8_none_p_kernel(tc, x_words, x_scales, w1, rin, w2, so, offs
         def list_half(list_sb, c):
             return list_sb[:, c * HALF // LIST_ROWS : (c + 1) * HALF // LIST_ROWS]
 
-        rin_picked = [keep.tile([P, PACK, HALF], F32, name=f"rin_picked{c}") for c in range(2)]
+        rin_picked = keep.tile([P, PACK, S], F32, name="rin_picked")
         for t in range(PACK):
-            for c in range(2):
-                nc.vector.tensor_copy(rin_picked[c][:, t, :], rin_sb[t][:].indirect(list_half(mem_sb, c)))
+            nc.vector.tensor_copy(rin_picked[:, t, :], rin_sb[t][:].indirect(mem_sb[:]))
 
         x_scale_picked = keep.tile([P, S], U8, name="x_scale_picked", align_bytes=64)
         nc.vector.tensor_copy(x_scale_picked[:], xs_sb[:].indirect(offs_sb[:]))
@@ -89,19 +89,29 @@ def tile_picked_bens8_none_p_kernel(tc, x_words, x_scales, w1, rin, w2, so, offs
         w1_grouped = keep.tile([P, PACK * H], BF16, name="w1_grouped", align_bytes=64)
         w1_codes = keep.tile([P, H], U32, name="w1_codes", align_bytes=64)
         w1_scales = keep.tile([P, H], U8, name="w1_scales", align_bytes=64)
-        for t in range(PACK):
-            cast_weight_plane(nc, w1_raw, w1_grouped, t)
-            quantize_weight_plane(nc, w1_grouped, w1_codes, w1_scales, t)
+        for pair in range(2):
+            cast_weight_plane(nc, w1_raw, w1_grouped[:], 2 * pair)
+            cast_weight_plane(nc, w1_raw, w1_grouped[:], 2 * pair + 1)
+            quantize_weight_pair(nc, w1_grouped[:], w1_codes, w1_scales, pair)
+
+        rin_grouped = [keep.tile([P, PACK * QUARTER], F32, name=f"rin_grouped{k}") for k in range(4)]
+        for k in range(4):
+            nc.scalar.copy(
+                out=rin_grouped[k][:].rearrange("p (c i t) -> p c t i", i=2, t=PACK),
+                in_=rin_picked[:, :, k * QUARTER : (k + 1) * QUARTER].rearrange("p t (c i) -> p c t i", i=2),
+            )
 
         x_picked = [keep.tile([P, HALF], U32, name=f"x_picked{c}", align_bytes=64) for c in range(2)]
         for c in range(2):
             nc.vector.tensor_copy(x_picked[c][:], xw_sb[:].bitcast(U32).indirect(list_half(offs_sb, c)))
 
-        w2_grouped = keep.tile([P, PACK * N], BF16, name="w2_grouped", align_bytes=64)
+        late_grouped = keep.tile([P, PACK * QUARTER + PACK * N], BF16, name="late_grouped", align_bytes=64)
+        w2_grouped = late_grouped[:, PACK * QUARTER :]
         w2_codes = keep.tile([P, N], U32, name="w2_codes", align_bytes=64)
         w2_scales = keep.tile([P, N], U8, name="w2_scales", align_bytes=64)
 
-        z_grouped = [keep.tile([P, PACK * HALF], BF16, name=f"z_grouped{c}", align_bytes=64) for c in range(2)]
+        z_first = keep.tile([P, PACK * HALF], BF16, name="z_first", align_bytes=64)
+        z_grouped = [z_first[:], late_grouped[:, : PACK * HALF]]
         z_codes = [keep.tile([P, HALF], U32, name=f"z_codes{c}", align_bytes=64) for c in range(2)]
         z_scales = [keep.tile([P, HALF], U8, name=f"z_scales{c}", align_bytes=64) for c in range(2)]
 
@@ -120,16 +130,14 @@ def tile_picked_bens8_none_p_kernel(tc, x_words, x_scales, w1, rin, w2, so, offs
                     stop=True,
                 )
             nc.vector.tensor_tensor(
-                z_grouped[c][:, s * QUARTER * PACK : (s + 1) * QUARTER * PACK].rearrange(
-                    "p (c i t) -> p c t i", i=2, t=PACK
-                ),
-                h_bank[:].rearrange("p t (c i) -> p c t i", i=2),
-                rin_picked[c][:, :, cols].rearrange("p t (c i) -> p c t i", i=2),
+                z_grouped[c][:, s * QUARTER * PACK : (s + 1) * QUARTER * PACK].rearrange("p (n t) -> p n t", t=PACK),
+                h_bank[:].rearrange("p t n -> p n t"),
+                rin_grouped[2 * c + s][:].rearrange("p (n t) -> p n t", t=PACK),
                 MULT,
             )
 
         def quantize_z(c):
-            nc.vector.quantize_mx(out=z_codes[c][:].bitcast(FP8X4), scales=z_scales[c][:], in_=z_grouped[c][:])
+            nc.vector.quantize_mx(out=z_codes[c][:].bitcast(FP8X4), scales=z_scales[c][:], in_=z_grouped[c])
 
         hidden_quarter(0, 0)
         hidden_quarter(0, 1)
@@ -137,8 +145,9 @@ def tile_picked_bens8_none_p_kernel(tc, x_words, x_scales, w1, rin, w2, so, offs
         quantize_z(0)
         for t in range(PACK):
             cast_weight_plane(nc, w2_raw, w2_grouped, t)
-            quantize_weight_plane(nc, w2_grouped, w2_codes, w2_scales, t)
+        quantize_weight_pair(nc, w2_grouped, w2_codes, w2_scales, 0)
         hidden_quarter(1, 1)
+        quantize_weight_pair(nc, w2_grouped, w2_codes, w2_scales, 1)
         quantize_z(1)
 
         out_rows = out.rearrange("(q t r) s -> t q r s", t=PACK, r=8)

@@ -32,12 +32,12 @@ def cast_weight_plane(nc, raw, grouped, t):
     )
 
 
-def quantize_weight_pair(nc, grouped, codes, scales, pair):
-    cols = slice(2 * pair * P, 2 * (pair + 1) * P)
+def quantize_weight_planes(nc, grouped, codes, scales, first, count):
+    cols = slice(first * P, (first + count) * P)
     nc.vector.quantize_mx(
         out=codes[:, cols].bitcast(FP8X4),
         scales=scales[:, cols],
-        in_=grouped[:, 2 * pair * P * PACK : 2 * (pair + 1) * P * PACK],
+        in_=grouped[:, first * P * PACK : (first + count) * P * PACK],
     )
 
 
@@ -58,17 +58,14 @@ def tile_picked_bens8_none_p_kernel(tc, x_words, x_scales, w1, rin, w2, so, offs
 
         nc.vector.memset(xs_sb[:].bitcast(I32), 0)
 
-        nc.sync.dma_start(mem_sb[:], mem)
         nc.sync.dma_start(rin_sb[0][:, :U], plane_rows(rin, 0))
-        for quad in range(4):
-            nc.sync.dma_start(
-                xs_sb[32 * quad : 32 * quad + 4, :].bitcast(I32),
-                x_scales[0, 4 * quad : 4 * quad + 4, :].bitcast(I32),
-            )
+        nc.sync.dma_start(mem_sb[:], mem)
         nc.sync.dma_start(rin_sb[1][:, :U], plane_rows(rin, 1))
         nc.sync.dma_start(offs_sb[:], offs)
         nc.sync.dma_start(rin_sb[2][:, :U], plane_rows(rin, 2))
         nc.sync.dma_start(w1_raw[:], w1.rearrange("(p j) c -> p j c", j=PACK))
+        for r in range(4):
+            nc.sync.dma_start(xs_sb[r:P:32, :].bitcast(I32), x_scales[0, r:16:4, :].bitcast(I32))
         nc.sync.dma_start(rin_sb[3][:, :U], plane_rows(rin, 3))
         nc.sync.dma_start(xw_sb[:], x_words[0].rearrange("p n r -> p (n r)").bitcast(I32))
         for j in range(PACK):
@@ -92,14 +89,7 @@ def tile_picked_bens8_none_p_kernel(tc, x_words, x_scales, w1, rin, w2, so, offs
         for pair in range(2):
             cast_weight_plane(nc, w1_raw, w1_grouped[:], 2 * pair)
             cast_weight_plane(nc, w1_raw, w1_grouped[:], 2 * pair + 1)
-            quantize_weight_pair(nc, w1_grouped[:], w1_codes, w1_scales, pair)
-
-        rin_grouped = [keep.tile([P, PACK * QUARTER], F32, name=f"rin_grouped{k}") for k in range(4)]
-        for k in range(4):
-            nc.scalar.copy(
-                out=rin_grouped[k][:].rearrange("p (c i t) -> p c t i", i=2, t=PACK),
-                in_=rin_picked[:, :, k * QUARTER : (k + 1) * QUARTER].rearrange("p t (c i) -> p c t i", i=2),
-            )
+            quantize_weight_planes(nc, w1_grouped[:], w1_codes, w1_scales, 2 * pair, 2)
 
         x_picked = [keep.tile([P, HALF], U32, name=f"x_picked{c}", align_bytes=64) for c in range(2)]
         for c in range(2):
@@ -130,45 +120,51 @@ def tile_picked_bens8_none_p_kernel(tc, x_words, x_scales, w1, rin, w2, so, offs
                     stop=True,
                 )
             nc.vector.tensor_tensor(
-                z_grouped[c][:, s * QUARTER * PACK : (s + 1) * QUARTER * PACK].rearrange("p (n t) -> p n t", t=PACK),
-                h_bank[:].rearrange("p t n -> p n t"),
-                rin_grouped[2 * c + s][:].rearrange("p (n t) -> p n t", t=PACK),
+                z_grouped[c][:, s * QUARTER * PACK : (s + 1) * QUARTER * PACK].rearrange("p (n i t) -> p n t i", i=2, t=PACK),
+                h_bank[:].rearrange("p t (n i) -> p n t i", i=2),
+                rin_picked[:, :, all_cols].rearrange("p t (n i) -> p n t i", i=2),
                 MULT,
             )
 
         def quantize_z(c):
             nc.vector.quantize_mx(out=z_codes[c][:].bitcast(FP8X4), scales=z_scales[c][:], in_=z_grouped[c])
 
+        out_rows = out.rearrange("(q t r) s -> t q r s", t=PACK, r=8)
+
+        def prepare_w2_plane(t):
+            cast_weight_plane(nc, w2_raw, w2_grouped, t)
+            quantize_weight_planes(nc, w2_grouped, w2_codes, w2_scales, t, 1)
+
+        def output_tile(c, t):
+            o_bank = psum.tile([P, HALF], F32, name=f"o_bank{t}")
+            nc.tensor.matmul_mx(
+                out=o_bank[:],
+                lhsT=w2_codes[:, t * P : (t + 1) * P].bitcast(FP8X4),
+                lhsT_scale=w2_scales[:, t * P : (t + 1) * P],
+                rhs=z_codes[c][:].bitcast(FP8X4),
+                rhs_scale=z_scales[c][:],
+                start=True,
+                stop=True,
+            )
+            o_sb = keep.tile([P, HALF], F32, name=f"o_sb{c}{t}")
+            result = keep.tile([P, HALF], F32, name=f"result{c}{t}")
+            nc.scalar.copy(out=o_sb[:], in_=o_bank[:])
+            nc.vector.tensor_tensor(result[:], so_sb[t][:].indirect(list_half(mem_sb, c)), o_sb[:], MULT)
+            nc.sync.dma_start(out_rows[t][:, :, c * HALF : (c + 1) * HALF], result[:])
+
         hidden_quarter(0, 0)
         hidden_quarter(0, 1)
         hidden_quarter(1, 0)
         quantize_z(0)
-        for t in range(PACK):
-            cast_weight_plane(nc, w2_raw, w2_grouped, t)
-        quantize_weight_pair(nc, w2_grouped, w2_codes, w2_scales, 0)
+        prepare_w2_plane(0)
         hidden_quarter(1, 1)
-        quantize_weight_pair(nc, w2_grouped, w2_codes, w2_scales, 1)
+        prepare_w2_plane(1)
         quantize_z(1)
-
-        out_rows = out.rearrange("(q t r) s -> t q r s", t=PACK, r=8)
-        for c in range(2):
-            for pair in range(2):
-                o_bank = psum.tile([P, 2, HALF], F32, name=f"o_bank{c}{pair}")
-                for e in range(2):
-                    t = 2 * pair + e
-                    nc.tensor.matmul_mx(
-                        out=o_bank[:, e, :],
-                        lhsT=w2_codes[:, t * P : (t + 1) * P].bitcast(FP8X4),
-                        lhsT_scale=w2_scales[:, t * P : (t + 1) * P],
-                        rhs=z_codes[c][:].bitcast(FP8X4),
-                        rhs_scale=z_scales[c][:],
-                        start=True,
-                        stop=True,
-                    )
-                for e in range(2):
-                    t = 2 * pair + e
-                    o_sb = keep.tile([P, HALF], F32, name=f"o_sb{c}{t}")
-                    result = keep.tile([P, HALF], F32, name=f"result{c}{t}")
-                    nc.scalar.copy(out=o_sb[:], in_=o_bank[:, e, :])
-                    nc.vector.tensor_tensor(result[:], so_sb[t][:].indirect(list_half(mem_sb, c)), o_sb[:], MULT)
-                    nc.sync.dma_start(out_rows[t][:, :, c * HALF : (c + 1) * HALF], result[:])
+        output_tile(0, 0)
+        prepare_w2_plane(2)
+        output_tile(0, 1)
+        prepare_w2_plane(3)
+        output_tile(0, 2)
+        output_tile(0, 3)
+        for t in range(PACK):
+            output_tile(1, t)

@@ -22,13 +22,13 @@ LIST_ROWS = 16
 
 
 def plane_rows(table, t):
-    return table.rearrange("(q t r) u -> t q r u", t=PACK, r=8)[t]
+    return table.rearrange("(p t) u -> t p u", t=PACK)[t]
 
 
-def cast_weight_plane(nc, raw, grouped, t):
+def cast_weight_pair(nc, raw, grouped, u):
     nc.scalar.copy(
-        out=grouped.rearrange("p (t q r i j) -> p t q r j i", t=PACK, r=4, i=2, j=PACK)[:, t],
-        in_=raw[:].rearrange("p j (q t r i) -> p t q r j i", t=PACK, r=4, i=2)[:, t],
+        out=grouped.rearrange("p (u i m j) -> p u m j i", u=2, i=2, j=PACK)[:, u],
+        in_=raw[:].rearrange("p j (m u i) -> p u m j i", u=2, i=2)[:, u],
     )
 
 
@@ -68,8 +68,7 @@ def tile_picked_bens8_none_p_kernel(tc, x_words, x_scales, w1, rin, w2, so, offs
             nc.sync.dma_start(xs_sb[r:P:32, :].bitcast(I32), x_scales[0, r:16:4, :].bitcast(I32))
         nc.sync.dma_start(rin_sb[3][:, :U], plane_rows(rin, 3))
         nc.sync.dma_start(xw_sb[:], x_words[0].rearrange("p n r -> p (n r)").bitcast(I32))
-        for j in range(PACK):
-            nc.sync.dma_start(w2_raw[:, j, :], plane_rows(w2, j))
+        nc.sync.dma_start(w2_raw[:], w2.rearrange("(p j) c -> p j c", j=PACK))
         for t in range(PACK):
             nc.sync.dma_start(so_sb[t][:], plane_rows(so, t))
 
@@ -87,8 +86,7 @@ def tile_picked_bens8_none_p_kernel(tc, x_words, x_scales, w1, rin, w2, so, offs
         w1_codes = keep.tile([P, H], U32, name="w1_codes", align_bytes=64)
         w1_scales = keep.tile([P, H], U8, name="w1_scales", align_bytes=64)
         for pair in range(2):
-            cast_weight_plane(nc, w1_raw, w1_grouped[:], 2 * pair)
-            cast_weight_plane(nc, w1_raw, w1_grouped[:], 2 * pair + 1)
+            cast_weight_pair(nc, w1_raw, w1_grouped[:], pair)
             quantize_weight_planes(nc, w1_grouped[:], w1_codes, w1_scales, 2 * pair, 2)
 
         x_picked = [keep.tile([P, HALF], U32, name=f"x_picked{c}", align_bytes=64) for c in range(2)]
@@ -129,11 +127,11 @@ def tile_picked_bens8_none_p_kernel(tc, x_words, x_scales, w1, rin, w2, so, offs
         def quantize_z(c):
             nc.vector.quantize_mx(out=z_codes[c][:].bitcast(FP8X4), scales=z_scales[c][:], in_=z_grouped[c])
 
-        out_rows = out.rearrange("(q t r) s -> t q r s", t=PACK, r=8)
+        out_rows = out.rearrange("(p t) s -> t p s", t=PACK)
 
-        def prepare_w2_plane(t):
-            cast_weight_plane(nc, w2_raw, w2_grouped, t)
-            quantize_weight_planes(nc, w2_grouped, w2_codes, w2_scales, t, 1)
+        def prepare_w2_pair(u):
+            cast_weight_pair(nc, w2_raw, w2_grouped, u)
+            quantize_weight_planes(nc, w2_grouped, w2_codes, w2_scales, 2 * u, 2)
 
         def output_tile(c, t):
             o_bank = psum.tile([P, HALF], F32, name=f"o_bank{t}")
@@ -150,21 +148,20 @@ def tile_picked_bens8_none_p_kernel(tc, x_words, x_scales, w1, rin, w2, so, offs
             result = keep.tile([P, HALF], F32, name=f"result{c}{t}")
             nc.scalar.copy(out=o_sb[:], in_=o_bank[:])
             nc.vector.tensor_tensor(result[:], so_sb[t][:].indirect(list_half(mem_sb, c)), o_sb[:], MULT)
-            nc.sync.dma_start(out_rows[t][:, :, c * HALF : (c + 1) * HALF], result[:])
+            nc.sync.dma_start(out_rows[t][:, c * HALF : (c + 1) * HALF], result[:])
 
         hidden_quarter(0, 0)
         hidden_quarter(0, 1)
         hidden_quarter(1, 0)
         quantize_z(0)
-        prepare_w2_plane(0)
+        prepare_w2_pair(0)
         hidden_quarter(1, 1)
-        prepare_w2_plane(1)
         quantize_z(1)
         output_tile(0, 0)
-        prepare_w2_plane(2)
         output_tile(0, 1)
-        prepare_w2_plane(3)
-        output_tile(0, 2)
-        output_tile(0, 3)
-        for t in range(PACK):
-            output_tile(1, t)
+        prepare_w2_pair(1)
+        output_tile(1, 0)
+        output_tile(1, 1)
+        for c in range(2):
+            output_tile(c, 2)
+            output_tile(c, 3)

@@ -25,11 +25,13 @@ def plane_rows(table, t):
     return table.rearrange("(p t) u -> t p u", t=PACK)[t]
 
 
-def cast_weight_pair(nc, raw, grouped, u):
-    nc.scalar.copy(
-        out=grouped.rearrange("p (u i m j) -> p u m j i", u=2, i=2, j=PACK)[:, u],
-        in_=raw[:].rearrange("p j (m u i) -> p u m j i", u=2, i=2)[:, u],
-    )
+def cast_weight_pair(nc, raw, grouped, u, pieces=1):
+    for piece in range(pieces):
+        rows = slice(piece * P // pieces, (piece + 1) * P // pieces)
+        nc.scalar.copy(
+            out=grouped.rearrange("p (u i m j) -> p u m j i", u=2, i=2, j=PACK)[:, u, rows],
+            in_=raw[:].rearrange("p j (m u i) -> p u m j i", u=2, i=2)[:, u, rows],
+        )
 
 
 def quantize_weight_planes(nc, grouped, codes, scales, first, count):
@@ -49,38 +51,37 @@ def tile_picked_bens8_none_p_kernel(tc, x_words, x_scales, w1, rin, w2, so, offs
 
         mem_sb = keep.tile([P, S // LIST_ROWS], U16, name="mem_sb")
         offs_sb = keep.tile([P, S // LIST_ROWS], U16, name="offs_sb")
-        rin_sb = [keep.tile([P, 2 * U], F32, name=f"rin_sb{t}") for t in range(PACK)]
-        so_sb = [keep.tile([P, U], F32, name=f"so_sb{t}") for t in range(PACK)]
-        xw_sb = keep.tile([P, T], I32, name="xw_sb")
-        xs_sb = keep.tile([P, T], U8, name="xs_sb")
-        w1_raw = keep.tile([P, PACK, H], F32, name="w1_raw")
-        w2_raw = keep.tile([P, PACK, N], F32, name="w2_raw")
+        rin_sb = [keep.tile([P, 2 * U], F32, name=f"rin_sb{t}", tag=f"slot{t}") for t in range(PACK)]
+        xs_sb = keep.tile([P, T], U8, name="xs_sb", tag="x")
+        w1_raw = keep.tile([P, PACK, H], F32, name="w1_raw", tag="slot4")
 
-        nc.vector.memset(xs_sb[:].bitcast(I32), 0)
+        nc.vector.memset(xs_sb[:112, :].bitcast(I32), 0)
 
+        nc.sync.dma_start(xs_sb[112:P, :].bitcast(I32), x_scales[0].bitcast(I32))
+        nc.sync.dma_start(offs_sb[:], offs)
         nc.sync.dma_start(rin_sb[0][:, :U], plane_rows(rin, 0))
         nc.sync.dma_start(mem_sb[:], mem)
         nc.sync.dma_start(rin_sb[1][:, :U], plane_rows(rin, 1))
-        nc.sync.dma_start(offs_sb[:], offs)
-        nc.sync.dma_start(rin_sb[2][:, :U], plane_rows(rin, 2))
         nc.sync.dma_start(w1_raw[:], w1.rearrange("(p j) c -> p j c", j=PACK))
-        for r in range(4):
-            nc.sync.dma_start(xs_sb[r:P:32, :].bitcast(I32), x_scales[0, r:16:4, :].bitcast(I32))
+        nc.sync.dma_start(rin_sb[2][:, :U], plane_rows(rin, 2))
         nc.sync.dma_start(rin_sb[3][:, :U], plane_rows(rin, 3))
-        nc.sync.dma_start(xw_sb[:], x_words[0].rearrange("p n r -> p (n r)").bitcast(I32))
-        nc.sync.dma_start(w2_raw[:], w2.rearrange("(p j) c -> p j c", j=PACK))
-        for t in range(PACK):
-            nc.sync.dma_start(so_sb[t][:], plane_rows(so, t))
 
         def list_half(list_sb, c):
             return list_sb[:, c * HALF // LIST_ROWS : (c + 1) * HALF // LIST_ROWS]
 
+        x_scale_spread = keep.tile([P, S], U8, name="x_scale_spread", align_bytes=64)
+        nc.vector.tensor_copy(x_scale_spread[:], xs_sb[:].indirect(offs_sb[:]))
+        x_scale_picked = keep.tile([P, S], U8, name="x_scale_picked", align_bytes=64)
+        nc.gpsimd.memset(x_scale_picked[:].bitcast(I32), 0)
+        for r in range(4):
+            nc.sync.dma_start(x_scale_picked[r:P:32, :].bitcast(I32), x_scale_spread[112 + r : P : 4, :].bitcast(I32))
+
+        xw_sb = keep.tile([P, T], I32, name="xw_sb", tag="x")
+        nc.sync.dma_start(xw_sb[:], x_words[0].rearrange("p n r -> p (n r)").bitcast(I32))
+
         rin_picked = keep.tile([P, PACK, S], F32, name="rin_picked")
         for t in range(PACK):
             nc.vector.tensor_copy(rin_picked[:, t, :], rin_sb[t][:].indirect(mem_sb[:]))
-
-        x_scale_picked = keep.tile([P, S], U8, name="x_scale_picked", align_bytes=64)
-        nc.vector.tensor_copy(x_scale_picked[:], xs_sb[:].indirect(offs_sb[:]))
 
         w1_grouped = keep.tile([P, PACK * H], BF16, name="w1_grouped", align_bytes=64)
         w1_codes = keep.tile([P, H], U32, name="w1_codes", align_bytes=64)
@@ -89,9 +90,18 @@ def tile_picked_bens8_none_p_kernel(tc, x_words, x_scales, w1, rin, w2, so, offs
             cast_weight_pair(nc, w1_raw, w1_grouped[:], pair)
             quantize_weight_planes(nc, w1_grouped[:], w1_codes, w1_scales, 2 * pair, 2)
 
+        w2_raw = keep.tile([P, PACK, N], F32, name="w2_raw", tag="slot1")
+        nc.sync.dma_start(w2_raw[:], w2.rearrange("(p j) c -> p j c", j=PACK))
+        so_sb = [keep.tile([P, U], F32, name=f"so_sb{t}", tag=f"slot{t + 2}") for t in range(PACK - 1)]
+        for t in range(PACK - 1):
+            nc.sync.dma_start(so_sb[t][:], plane_rows(so, t))
+
         x_picked = [keep.tile([P, HALF], U32, name=f"x_picked{c}", align_bytes=64) for c in range(2)]
         for c in range(2):
             nc.vector.tensor_copy(x_picked[c][:], xw_sb[:].bitcast(U32).indirect(list_half(offs_sb, c)))
+
+        so_sb.append(keep.tile([P, U], F32, name="so_sb3", tag="x"))
+        nc.sync.dma_start(so_sb[3][:], plane_rows(so, 3))
 
         late_grouped = keep.tile([P, PACK * QUARTER + PACK * N], BF16, name="late_grouped", align_bytes=64)
         w2_grouped = late_grouped[:, PACK * QUARTER :]
@@ -130,7 +140,7 @@ def tile_picked_bens8_none_p_kernel(tc, x_words, x_scales, w1, rin, w2, so, offs
         out_rows = out.rearrange("(p t) s -> t p s", t=PACK)
 
         def prepare_w2_pair(u):
-            cast_weight_pair(nc, w2_raw, w2_grouped, u)
+            cast_weight_pair(nc, w2_raw, w2_grouped, u, 1 + 3 * u)
             quantize_weight_planes(nc, w2_grouped, w2_codes, w2_scales, 2 * u, 2)
 
         def output_tile(c, t):

@@ -13,12 +13,14 @@ U16 = mybir.dt.uint16
 U8 = mybir.dt.uint8
 FP8X4 = mybir.dt.float8_e4m3fn_x4
 MULT = mybir.AluOpType.mult
+ADD = mybir.AluOpType.add
 
 P = 128
 PACK = 4
 HALF = 256
 QUARTER = 128
 LIST_ROWS = 16
+SCALAR_ROWS = 80
 
 
 def plane_rows(table, t):
@@ -140,7 +142,21 @@ def tile_picked_bens8_none_p_kernel(tc, x_words, x_scales, w1, rin, w2, so, offs
         out_rows = out.rearrange("(p t) s -> t p s", t=PACK)
 
         def prepare_w2_pair(u):
-            cast_weight_pair(nc, w2_raw, w2_grouped, u, 1 + 3 * u)
+            if u == 0:
+                nc.scalar.copy(
+                    out=w2_grouped.rearrange("p (u i m j) -> p u m j i", u=2, i=2, j=PACK)[:, 0, :SCALAR_ROWS],
+                    in_=w2_raw[:].rearrange("p j (m u i) -> p u m j i", u=2, i=2)[:, 0, :SCALAR_ROWS],
+                )
+                nc.gpsimd.tensor_scalar(
+                    w2_grouped.rearrange("p (u i m j) -> p u i m j", u=2, i=2, j=PACK)[:, 0, :, SCALAR_ROWS:],
+                    w2_raw[:].rearrange("p j (m u i) -> p u i m j", u=2, i=2)[:, 0, :, SCALAR_ROWS:],
+                    1.0,
+                    0.0,
+                    MULT,
+                    ADD,
+                )
+            else:
+                cast_weight_pair(nc, w2_raw, w2_grouped, u, 4)
             quantize_weight_planes(nc, w2_grouped, w2_codes, w2_scales, 2 * u, 2)
 
         def output_tile(c, t):
@@ -157,8 +173,12 @@ def tile_picked_bens8_none_p_kernel(tc, x_words, x_scales, w1, rin, w2, so, offs
             o_sb = keep.tile([P, HALF], F32, name=f"o_sb{c}{t}")
             result = keep.tile([P, HALF], F32, name=f"result{c}{t}")
             nc.scalar.copy(out=o_sb[:], in_=o_bank[:])
-            nc.vector.tensor_tensor(result[:], so_sb[t][:].indirect(list_half(mem_sb, c)), o_sb[:], MULT)
-            nc.sync.dma_start(out_rows[t][:, c * HALF : (c + 1) * HALF], result[:])
+            width = QUARTER if (c, t) == (1, PACK - 1) else HALF
+            for first in range(0, HALF, width):
+                token = c * HALF + first
+                offsets = mem_sb[:, token // LIST_ROWS : (token + width) // LIST_ROWS]
+                nc.vector.tensor_tensor(result[:, first : first + width], so_sb[t][:].indirect(offsets), o_sb[:, first : first + width], MULT)
+                nc.sync.dma_start(out_rows[t][:, token : token + width], result[:, first : first + width])
 
         hidden_quarter(0, 0)
         hidden_quarter(0, 1)

@@ -13,14 +13,12 @@ U16 = mybir.dt.uint16
 U8 = mybir.dt.uint8
 FP8X4 = mybir.dt.float8_e4m3fn_x4
 MULT = mybir.AluOpType.mult
-ADD = mybir.AluOpType.add
 
 P = 128
 PACK = 4
 HALF = 256
 QUARTER = 128
 LIST_ROWS = 16
-SCALAR_ROWS = 80
 
 
 def plane_rows(table, t):
@@ -53,9 +51,13 @@ def tile_picked_bens8_none_p_kernel(tc, x_words, x_scales, w1, rin, w2, so, offs
 
         mem_sb = keep.tile([P, S // LIST_ROWS], U16, name="mem_sb")
         offs_sb = keep.tile([P, S // LIST_ROWS], U16, name="offs_sb")
-        rin_sb = [keep.tile([P, 2 * U], F32, name=f"rin_sb{t}", tag=f"slot{t}") for t in range(PACK)]
-        xs_sb = keep.tile([P, T], U8, name="xs_sb", tag="x")
+        rin_sb = [keep.tile([P, 2 * U], F32, name=f"rin_sb{t}", tag=f"slot{t}") for t in range(PACK - 1)]
+        xs_sb = keep.tile([P, T], U8, name="xs_sb")
         w1_raw = keep.tile([P, PACK, H], F32, name="w1_raw", tag="slot4")
+
+        warm = keep.tile([P, 16], F32, name="warm")
+        nc.gpsimd.memset(warm[:, 0:1], 0.0)
+        nc.scalar.copy(out=warm[:, 8:9], in_=warm[:, 0:1])
 
         nc.vector.memset(xs_sb[:112, :].bitcast(I32), 0)
 
@@ -66,7 +68,9 @@ def tile_picked_bens8_none_p_kernel(tc, x_words, x_scales, w1, rin, w2, so, offs
         nc.sync.dma_start(rin_sb[1][:, :U], plane_rows(rin, 1))
         nc.sync.dma_start(w1_raw[:], w1.rearrange("(p j) c -> p j c", j=PACK))
         nc.sync.dma_start(rin_sb[2][:, :U], plane_rows(rin, 2))
-        nc.sync.dma_start(rin_sb[3][:, :U], plane_rows(rin, 3))
+
+        xw_sb = keep.tile([P, T], I32, name="xw_sb", tag="x")
+        nc.sync.dma_start(xw_sb[:], x_words[0].rearrange("p n r -> p (n r)").bitcast(I32))
 
         def list_half(list_sb, c):
             return list_sb[:, c * HALF // LIST_ROWS : (c + 1) * HALF // LIST_ROWS]
@@ -78,12 +82,11 @@ def tile_picked_bens8_none_p_kernel(tc, x_words, x_scales, w1, rin, w2, so, offs
         for r in range(4):
             nc.sync.dma_start(x_scale_picked[r:P:32, :].bitcast(I32), x_scale_spread[112 + r : P : 4, :].bitcast(I32))
 
-        xw_sb = keep.tile([P, T], I32, name="xw_sb", tag="x")
-        nc.sync.dma_start(xw_sb[:], x_words[0].rearrange("p n r -> p (n r)").bitcast(I32))
-
         rin_picked = keep.tile([P, PACK, S], F32, name="rin_picked")
-        for t in range(PACK):
+        for t in range(PACK - 1):
             nc.vector.tensor_copy(rin_picked[:, t, :], rin_sb[t][:].indirect(mem_sb[:]))
+        rin_last = keep.tile([P, 2 * U], F32, name="rin_last", tag="slot0")
+        nc.sync.dma_start(rin_last[:, :U], plane_rows(rin, PACK - 1))
 
         w1_grouped = keep.tile([P, PACK * H], BF16, name="w1_grouped", align_bytes=64)
         w1_codes = keep.tile([P, H], U32, name="w1_codes", align_bytes=64)
@@ -94,16 +97,20 @@ def tile_picked_bens8_none_p_kernel(tc, x_words, x_scales, w1, rin, w2, so, offs
 
         w2_raw = keep.tile([P, PACK, N], F32, name="w2_raw", tag="slot1")
         nc.sync.dma_start(w2_raw[:], w2.rearrange("(p j) c -> p j c", j=PACK))
-        so_sb = [keep.tile([P, U], F32, name=f"so_sb{t}", tag=f"slot{t + 2}") for t in range(PACK - 1)]
-        for t in range(PACK - 1):
+        so_sb = [keep.tile([P, U], F32, name=f"so_sb{t}", tag=f"slot{2 * t + 2}") for t in range(2)]
+        for t in range(2):
             nc.sync.dma_start(so_sb[t][:], plane_rows(so, t))
 
         x_picked = [keep.tile([P, HALF], U32, name=f"x_picked{c}", align_bytes=64) for c in range(2)]
         for c in range(2):
             nc.vector.tensor_copy(x_picked[c][:], xw_sb[:].bitcast(U32).indirect(list_half(offs_sb, c)))
 
-        so_sb.append(keep.tile([P, U], F32, name="so_sb3", tag="x"))
-        nc.sync.dma_start(so_sb[3][:], plane_rows(so, 3))
+        nc.vector.tensor_copy(rin_picked[:, PACK - 1, :], rin_last[:].indirect(mem_sb[:]))
+
+        so_sb.append(keep.tile([P, U], F32, name="so_sb2", tag="x"))
+        so_sb.append(keep.tile([P, U], F32, name="so_sb3", tag="slot0"))
+        for t in range(2, PACK):
+            nc.sync.dma_start(so_sb[t][:], plane_rows(so, t))
 
         late_grouped = keep.tile([P, PACK * QUARTER + PACK * N], BF16, name="late_grouped", align_bytes=64)
         w2_grouped = late_grouped[:, PACK * QUARTER :]
@@ -142,21 +149,7 @@ def tile_picked_bens8_none_p_kernel(tc, x_words, x_scales, w1, rin, w2, so, offs
         out_rows = out.rearrange("(p t) s -> t p s", t=PACK)
 
         def prepare_w2_pair(u):
-            if u == 0:
-                nc.scalar.copy(
-                    out=w2_grouped.rearrange("p (u i m j) -> p u m j i", u=2, i=2, j=PACK)[:, 0, :SCALAR_ROWS],
-                    in_=w2_raw[:].rearrange("p j (m u i) -> p u m j i", u=2, i=2)[:, 0, :SCALAR_ROWS],
-                )
-                nc.gpsimd.tensor_scalar(
-                    w2_grouped.rearrange("p (u i m j) -> p u i m j", u=2, i=2, j=PACK)[:, 0, :, SCALAR_ROWS:],
-                    w2_raw[:].rearrange("p j (m u i) -> p u i m j", u=2, i=2)[:, 0, :, SCALAR_ROWS:],
-                    1.0,
-                    0.0,
-                    MULT,
-                    ADD,
-                )
-            else:
-                cast_weight_pair(nc, w2_raw, w2_grouped, u, 4)
+            cast_weight_pair(nc, w2_raw, w2_grouped, u, 1 + 3 * u)
             quantize_weight_planes(nc, w2_grouped, w2_codes, w2_scales, 2 * u, 2)
 
         def output_tile(c, t):

@@ -19,6 +19,7 @@ PACK = 4
 HALF = 256
 QUARTER = 128
 LIST_ROWS = 16
+SHARE = 80
 
 
 def plane_rows(table, t):
@@ -52,12 +53,8 @@ def tile_picked_bens8_none_p_kernel(tc, x_words, x_scales, w1, rin, w2, so, offs
         mem_sb = keep.tile([P, S // LIST_ROWS], U16, name="mem_sb")
         offs_sb = keep.tile([P, S // LIST_ROWS], U16, name="offs_sb")
         rin_sb = [keep.tile([P, 2 * U], F32, name=f"rin_sb{t}", tag=f"slot{t}") for t in range(PACK - 1)]
-        xs_sb = keep.tile([P, T], U8, name="xs_sb")
+        xs_sb = keep.tile([P, T], U8, name="xs_sb", tag="x")
         w1_raw = keep.tile([P, PACK, H], F32, name="w1_raw", tag="slot4")
-
-        warm = keep.tile([P, 16], F32, name="warm")
-        nc.gpsimd.memset(warm[:, 0:1], 0.0)
-        nc.scalar.copy(out=warm[:, 8:9], in_=warm[:, 0:1])
 
         nc.vector.memset(xs_sb[:112, :].bitcast(I32), 0)
 
@@ -69,9 +66,6 @@ def tile_picked_bens8_none_p_kernel(tc, x_words, x_scales, w1, rin, w2, so, offs
         nc.sync.dma_start(w1_raw[:], w1.rearrange("(p j) c -> p j c", j=PACK))
         nc.sync.dma_start(rin_sb[2][:, :U], plane_rows(rin, 2))
 
-        xw_sb = keep.tile([P, T], I32, name="xw_sb", tag="x")
-        nc.sync.dma_start(xw_sb[:], x_words[0].rearrange("p n r -> p (n r)").bitcast(I32))
-
         def list_half(list_sb, c):
             return list_sb[:, c * HALF // LIST_ROWS : (c + 1) * HALF // LIST_ROWS]
 
@@ -82,11 +76,14 @@ def tile_picked_bens8_none_p_kernel(tc, x_words, x_scales, w1, rin, w2, so, offs
         for r in range(4):
             nc.sync.dma_start(x_scale_picked[r:P:32, :].bitcast(I32), x_scale_spread[112 + r : P : 4, :].bitcast(I32))
 
+        xw_sb = keep.tile([P, T], I32, name="xw_sb", tag="x")
+        nc.sync.dma_start(xw_sb[:], x_words[0].rearrange("p n r -> p (n r)").bitcast(I32))
+
         rin_picked = keep.tile([P, PACK, S], F32, name="rin_picked")
         for t in range(PACK - 1):
             nc.vector.tensor_copy(rin_picked[:, t, :], rin_sb[t][:].indirect(mem_sb[:]))
-        rin_last = keep.tile([P, 2 * U], F32, name="rin_last", tag="slot0")
-        nc.sync.dma_start(rin_last[:, :U], plane_rows(rin, PACK - 1))
+        rin_last = keep.tile([P, U], F32, name="rin_last", tag="slot0")
+        nc.sync.dma_start(rin_last[:], plane_rows(rin, PACK - 1))
 
         w1_grouped = keep.tile([P, PACK * H], BF16, name="w1_grouped", align_bytes=64)
         w1_codes = keep.tile([P, H], U32, name="w1_codes", align_bytes=64)
@@ -105,7 +102,8 @@ def tile_picked_bens8_none_p_kernel(tc, x_words, x_scales, w1, rin, w2, so, offs
         for c in range(2):
             nc.vector.tensor_copy(x_picked[c][:], xw_sb[:].bitcast(U32).indirect(list_half(offs_sb, c)))
 
-        nc.vector.tensor_copy(rin_picked[:, PACK - 1, :], rin_last[:].indirect(mem_sb[:]))
+        for c in range(2):
+            nc.vector.tensor_copy(rin_picked[:, PACK - 1, c * HALF : (c + 1) * HALF], rin_last[:].indirect(list_half(mem_sb, c)))
 
         so_sb.append(keep.tile([P, U], F32, name="so_sb2", tag="x"))
         so_sb.append(keep.tile([P, U], F32, name="so_sb3", tag="slot0"))
@@ -136,6 +134,22 @@ def tile_picked_bens8_none_p_kernel(tc, x_words, x_scales, w1, rin, w2, so, offs
                     start=True,
                     stop=True,
                 )
+            if (c, s) == (0, 0):
+                h_woven = keep.tile([P, SHARE, PACK], F32, name="h_woven")
+                nc.scalar.copy(out=h_woven[:], in_=h_bank[:, :, :SHARE].rearrange("p t n -> p n t"))
+                nc.gpsimd.tensor_tensor(
+                    z_grouped[c][:, : SHARE * PACK].rearrange("p (n t) -> p n t", t=PACK),
+                    h_woven[:],
+                    rin_picked[:, :, :SHARE].rearrange("p t n -> p n t"),
+                    MULT,
+                )
+                nc.vector.tensor_tensor(
+                    z_grouped[c][:, SHARE * PACK : QUARTER * PACK].rearrange("p (n i t) -> p n t i", i=2, t=PACK),
+                    h_bank[:, :, SHARE:].rearrange("p t (n i) -> p n t i", i=2),
+                    rin_picked[:, :, SHARE:QUARTER].rearrange("p t (n i) -> p n t i", i=2),
+                    MULT,
+                )
+                return
             nc.vector.tensor_tensor(
                 z_grouped[c][:, s * QUARTER * PACK : (s + 1) * QUARTER * PACK].rearrange("p (n i t) -> p n t i", i=2, t=PACK),
                 h_bank[:].rearrange("p t (n i) -> p n t i", i=2),

@@ -19,20 +19,22 @@ PACK = 4
 HALF = 256
 QUARTER = 128
 LIST_ROWS = 16
-SHARE = 80
 
 
 def plane_rows(table, t):
     return table.rearrange("(p t) u -> t p u", t=PACK)[t]
 
 
-def cast_weight_pair(nc, raw, grouped, u, pieces=1):
-    for piece in range(pieces):
-        rows = slice(piece * P // pieces, (piece + 1) * P // pieces)
-        nc.scalar.copy(
-            out=grouped.rearrange("p (u i m j) -> p u m j i", u=2, i=2, j=PACK)[:, u, rows],
-            in_=raw[:].rearrange("p j (m u i) -> p u m j i", u=2, i=2)[:, u, rows],
-        )
+def weight_half(w, a):
+    return w.rearrange("(p j) c -> p j c", j=PACK)[:, :, a * HALF : (a + 1) * HALF]
+
+
+def cast_weight_half(nc, raw, grouped, a, pairs):
+    rows = slice(a * P // 2, (a + 1) * P // 2)
+    nc.scalar.copy(
+        out=grouped.rearrange("p (u i m j) -> p u m j i", u=2, i=2, j=PACK)[:, pairs, rows],
+        in_=raw.rearrange("p j (m u i) -> p u m j i", u=2, i=2)[:, pairs],
+    )
 
 
 def quantize_weight_planes(nc, grouped, codes, scales, first, count):
@@ -53,8 +55,9 @@ def tile_picked_bens8_none_p_kernel(tc, x_words, x_scales, w1, rin, w2, so, offs
         mem_sb = keep.tile([P, S // LIST_ROWS], U16, name="mem_sb")
         offs_sb = keep.tile([P, S // LIST_ROWS], U16, name="offs_sb")
         rin_sb = [keep.tile([P, 2 * U], F32, name=f"rin_sb{t}", tag=f"slot{t}") for t in range(PACK - 1)]
-        xs_sb = keep.tile([P, T], U8, name="xs_sb", tag="x")
-        w1_raw = keep.tile([P, PACK, H], F32, name="w1_raw", tag="slot4")
+        xs_sb = keep.tile([P, T], U8, name="xs_sb", tag="xs")
+        w1_raw = [keep.tile([P, PACK, HALF], F32, name=f"w1_raw{a}", tag=f"slot{a + 3}") for a in range(2)]
+        xw_sb = keep.tile([P, T], I32, name="xw_sb", tag="x")
 
         nc.vector.memset(xs_sb[:112, :].bitcast(I32), 0)
 
@@ -62,9 +65,11 @@ def tile_picked_bens8_none_p_kernel(tc, x_words, x_scales, w1, rin, w2, so, offs
         nc.sync.dma_start(offs_sb[:], offs)
         nc.sync.dma_start(rin_sb[0][:, :U], plane_rows(rin, 0))
         nc.sync.dma_start(mem_sb[:], mem)
+        nc.sync.dma_start(w1_raw[0][:], weight_half(w1, 0))
         nc.sync.dma_start(rin_sb[1][:, :U], plane_rows(rin, 1))
-        nc.sync.dma_start(w1_raw[:], w1.rearrange("(p j) c -> p j c", j=PACK))
+        nc.sync.dma_start(w1_raw[1][:], weight_half(w1, 1))
         nc.sync.dma_start(rin_sb[2][:, :U], plane_rows(rin, 2))
+        nc.sync.dma_start(xw_sb[:], x_words[0].rearrange("p n r -> p (n r)").bitcast(I32))
 
         def list_half(list_sb, c):
             return list_sb[:, c * HALF // LIST_ROWS : (c + 1) * HALF // LIST_ROWS]
@@ -72,29 +77,28 @@ def tile_picked_bens8_none_p_kernel(tc, x_words, x_scales, w1, rin, w2, so, offs
         x_scale_spread = keep.tile([P, S], U8, name="x_scale_spread", align_bytes=64)
         nc.vector.tensor_copy(x_scale_spread[:], xs_sb[:].indirect(offs_sb[:]))
         x_scale_picked = keep.tile([P, S], U8, name="x_scale_picked", align_bytes=64)
-        nc.gpsimd.memset(x_scale_picked[:].bitcast(I32), 0)
+        nc.vector.memset(x_scale_picked[:].bitcast(I32), 0)
         for r in range(4):
             nc.sync.dma_start(x_scale_picked[r:P:32, :].bitcast(I32), x_scale_spread[112 + r : P : 4, :].bitcast(I32))
 
-        xw_sb = keep.tile([P, T], I32, name="xw_sb", tag="x")
-        nc.sync.dma_start(xw_sb[:], x_words[0].rearrange("p n r -> p (n r)").bitcast(I32))
+        rin_last = keep.tile([P, U], F32, name="rin_last", tag="xs")
+        nc.sync.dma_start(rin_last[:], plane_rows(rin, PACK - 1))
 
         rin_picked = keep.tile([P, PACK, S], F32, name="rin_picked")
         for t in range(PACK - 1):
             nc.vector.tensor_copy(rin_picked[:, t, :], rin_sb[t][:].indirect(mem_sb[:]))
-        rin_last = keep.tile([P, U], F32, name="rin_last", tag="slot0")
-        nc.sync.dma_start(rin_last[:], plane_rows(rin, PACK - 1))
 
         w1_grouped = keep.tile([P, PACK * H], BF16, name="w1_grouped", align_bytes=64)
         w1_codes = keep.tile([P, H], U32, name="w1_codes", align_bytes=64)
         w1_scales = keep.tile([P, H], U8, name="w1_scales", align_bytes=64)
-        for pair in range(2):
-            cast_weight_pair(nc, w1_raw, w1_grouped[:], pair)
-            quantize_weight_planes(nc, w1_grouped[:], w1_codes, w1_scales, 2 * pair, 2)
+        for a in range(2):
+            cast_weight_half(nc, w1_raw[a][:], w1_grouped[:], a, slice(0, 2))
+        quantize_weight_planes(nc, w1_grouped[:], w1_codes, w1_scales, 0, PACK)
 
-        w2_raw = keep.tile([P, PACK, N], F32, name="w2_raw", tag="slot1")
-        nc.sync.dma_start(w2_raw[:], w2.rearrange("(p j) c -> p j c", j=PACK))
-        so_sb = [keep.tile([P, U], F32, name=f"so_sb{t}", tag=f"slot{2 * t + 2}") for t in range(2)]
+        w2_raw = keep.tile([P, 2, PACK, HALF], F32, name="w2_raw", tag="slot0")
+        for a in range(2):
+            nc.sync.dma_start(w2_raw[:, a], weight_half(w2, a))
+        so_sb = [keep.tile([P, U], F32, name=f"so_sb{t}", tag=f"slot{t + 1}") for t in range(2)]
         for t in range(2):
             nc.sync.dma_start(so_sb[t][:], plane_rows(so, t))
 
@@ -106,7 +110,7 @@ def tile_picked_bens8_none_p_kernel(tc, x_words, x_scales, w1, rin, w2, so, offs
             nc.vector.tensor_copy(rin_picked[:, PACK - 1, c * HALF : (c + 1) * HALF], rin_last[:].indirect(list_half(mem_sb, c)))
 
         so_sb.append(keep.tile([P, U], F32, name="so_sb2", tag="x"))
-        so_sb.append(keep.tile([P, U], F32, name="so_sb3", tag="slot0"))
+        so_sb.append(keep.tile([P, U], F32, name="so_sb3", tag="xs"))
         for t in range(2, PACK):
             nc.sync.dma_start(so_sb[t][:], plane_rows(so, t))
 
@@ -118,62 +122,74 @@ def tile_picked_bens8_none_p_kernel(tc, x_words, x_scales, w1, rin, w2, so, offs
         z_first = keep.tile([P, PACK * HALF], BF16, name="z_first", align_bytes=64)
         z_grouped = [z_first[:], late_grouped[:, : PACK * HALF]]
         z_codes = [keep.tile([P, HALF], U32, name=f"z_codes{c}", align_bytes=64) for c in range(2)]
-        z_scales = [keep.tile([P, HALF], U8, name=f"z_scales{c}", align_bytes=64) for c in range(2)]
+        z_scales_second = keep.tile([P, HALF], U8, name="z_scales_second", align_bytes=64)
+        z_scales = [w2_scales[4:P, :HALF], z_scales_second[:]]
 
-        def hidden_quarter(c, s):
+        def hidden_product(c, s, t, target):
             cols = slice(s * QUARTER, (s + 1) * QUARTER)
             all_cols = slice(c * HALF + s * QUARTER, c * HALF + (s + 1) * QUARTER)
-            h_bank = psum.tile([P, PACK, QUARTER], F32, name=f"h_bank{c}{s}")
-            for t in range(PACK):
-                nc.tensor.matmul_mx(
-                    out=h_bank[:, t, :],
-                    lhsT=w1_codes[:, t * P : (t + 1) * P].bitcast(FP8X4),
-                    lhsT_scale=w1_scales[:, t * P : (t + 1) * P],
-                    rhs=x_picked[c][:, cols].bitcast(FP8X4),
-                    rhs_scale=x_scale_picked[:, all_cols],
-                    start=True,
-                    stop=True,
-                )
-            if (c, s) == (0, 0):
-                h_woven = keep.tile([P, SHARE, PACK], F32, name="h_woven")
-                nc.scalar.copy(out=h_woven[:], in_=h_bank[:, :, :SHARE].rearrange("p t n -> p n t"))
-                nc.gpsimd.tensor_tensor(
-                    z_grouped[c][:, : SHARE * PACK].rearrange("p (n t) -> p n t", t=PACK),
-                    h_woven[:],
-                    rin_picked[:, :, :SHARE].rearrange("p t n -> p n t"),
-                    MULT,
-                )
-                nc.vector.tensor_tensor(
-                    z_grouped[c][:, SHARE * PACK : QUARTER * PACK].rearrange("p (n i t) -> p n t i", i=2, t=PACK),
-                    h_bank[:, :, SHARE:].rearrange("p t (n i) -> p n t i", i=2),
-                    rin_picked[:, :, SHARE:QUARTER].rearrange("p t (n i) -> p n t i", i=2),
-                    MULT,
-                )
-                return
-            nc.vector.tensor_tensor(
+            nc.tensor.matmul_mx(
+                out=target,
+                lhsT=w1_codes[:, t * P : (t + 1) * P].bitcast(FP8X4),
+                lhsT_scale=w1_scales[:, t * P : (t + 1) * P],
+                rhs=x_picked[c][:, cols].bitcast(FP8X4),
+                rhs_scale=x_scale_picked[:, all_cols],
+                start=True,
+                stop=True,
+            )
+
+        def scale_quarter(engine, c, s, h_planes):
+            all_cols = slice(c * HALF + s * QUARTER, c * HALF + (s + 1) * QUARTER)
+            engine.tensor_tensor(
                 z_grouped[c][:, s * QUARTER * PACK : (s + 1) * QUARTER * PACK].rearrange("p (n i t) -> p n t i", i=2, t=PACK),
-                h_bank[:].rearrange("p t (n i) -> p n t i", i=2),
+                h_planes.rearrange("p t (n i) -> p n t i", i=2),
                 rin_picked[:, :, all_cols].rearrange("p t (n i) -> p n t i", i=2),
                 MULT,
             )
 
+        def hidden_quarter(c, s):
+            if (c, s) == (0, 0):
+                h_sb = keep.tile([P, PACK, QUARTER], F32, name="h_sb")
+                for u in range(2):
+                    h_pair = psum.tile([P, 2, QUARTER], F32, name=f"h_pair{u}", tag=f"o_bank{u + 2}")
+                    for i in range(2):
+                        hidden_product(c, s, 2 * u + i, h_pair[:, i, :])
+                    nc.scalar.copy(out=h_sb[:, 2 * u : 2 * u + 2, :], in_=h_pair[:])
+                scale_quarter(nc.gpsimd, c, s, h_sb[:])
+                return
+            h_bank = psum.tile([P, PACK, QUARTER], F32, name=f"h_bank{c}{s}")
+            for t in range(PACK):
+                hidden_product(c, s, t, h_bank[:, t, :])
+            scale_quarter(nc.vector, c, s, h_bank[:])
+
         def quantize_z(c):
-            nc.vector.quantize_mx(out=z_codes[c][:].bitcast(FP8X4), scales=z_scales[c][:], in_=z_grouped[c])
+            nc.vector.quantize_mx(out=z_codes[c][:].bitcast(FP8X4), scales=z_scales[c], in_=z_grouped[c])
 
         out_rows = out.rearrange("(p t) s -> t p s", t=PACK)
 
         def prepare_w2_pair(u):
-            cast_weight_pair(nc, w2_raw, w2_grouped, u, 1 + 3 * u)
-            quantize_weight_planes(nc, w2_grouped, w2_codes, w2_scales, 2 * u, 2)
+            if u == 0:
+                for a in range(2):
+                    cast_weight_half(nc, w2_raw[:, a], w2_grouped, a, slice(u, u + 1))
+                for t in range(2):
+                    quantize_weight_planes(nc, w2_grouped, w2_codes, w2_scales, t, 1)
+            else:
+                for piece in range(4):
+                    rows = slice(16 * piece, 16 * piece + 16)
+                    nc.scalar.copy(
+                        out=w2_grouped.rearrange("p (u i a m j) -> p u a m j i", u=2, i=2, a=2, j=PACK)[:, u, :, rows],
+                        in_=w2_raw[:].rearrange("p a j (m u i) -> p u a m j i", u=2, i=2)[:, u, :, rows],
+                    )
+                quantize_weight_planes(nc, w2_grouped, w2_codes, w2_scales, 2 * u, 2)
 
         def output_tile(c, t):
-            o_bank = psum.tile([P, HALF], F32, name=f"o_bank{t}")
+            o_bank = psum.tile([P, HALF], F32, name=f"o_bank{t}", tag=f"o_bank{t}")
             nc.tensor.matmul_mx(
                 out=o_bank[:],
                 lhsT=w2_codes[:, t * P : (t + 1) * P].bitcast(FP8X4),
                 lhsT_scale=w2_scales[:, t * P : (t + 1) * P],
                 rhs=z_codes[c][:].bitcast(FP8X4),
-                rhs_scale=z_scales[c][:],
+                rhs_scale=z_scales[c],
                 start=True,
                 stop=True,
             )
@@ -190,9 +206,9 @@ def tile_picked_bens8_none_p_kernel(tc, x_words, x_scales, w1, rin, w2, so, offs
         hidden_quarter(0, 0)
         hidden_quarter(0, 1)
         hidden_quarter(1, 0)
-        quantize_z(0)
         prepare_w2_pair(0)
         hidden_quarter(1, 1)
+        quantize_z(0)
         quantize_z(1)
         output_tile(0, 0)
         output_tile(0, 1)

@@ -25,16 +25,13 @@ def plane_rows(table, t):
     return table.rearrange("(p t) u -> t p u", t=PACK)[t]
 
 
-def weight_half(w, a):
-    return w.rearrange("(p j) c -> p j c", j=PACK)[:, :, a * HALF : (a + 1) * HALF]
-
-
-def cast_weight_half(nc, raw, grouped, a, pairs):
-    rows = slice(a * P // 2, (a + 1) * P // 2)
-    nc.scalar.copy(
-        out=grouped.rearrange("p (u i m j) -> p u m j i", u=2, i=2, j=PACK)[:, pairs, rows],
-        in_=raw.rearrange("p j (m u i) -> p u m j i", u=2, i=2)[:, pairs],
-    )
+def cast_weight_pair(nc, raw, grouped, u, pieces=1):
+    for piece in range(pieces):
+        rows = slice(piece * P // pieces, (piece + 1) * P // pieces)
+        nc.scalar.copy(
+            out=grouped.rearrange("p (i m j) -> p m j i", i=2, j=PACK)[:, rows],
+            in_=raw[:].rearrange("p j (m u i) -> p u m j i", u=2, i=2)[:, u, rows],
+        )
 
 
 def quantize_weight_planes(nc, grouped, codes, scales, first, count):
@@ -42,7 +39,7 @@ def quantize_weight_planes(nc, grouped, codes, scales, first, count):
     nc.vector.quantize_mx(
         out=codes[:, cols].bitcast(FP8X4),
         scales=scales[:, cols],
-        in_=grouped[:, first * P * PACK : (first + count) * P * PACK],
+        in_=grouped,
     )
 
 
@@ -55,9 +52,8 @@ def tile_picked_bens8_none_p_kernel(tc, x_words, x_scales, w1, rin, w2, so, offs
         mem_sb = keep.tile([P, S // LIST_ROWS], U16, name="mem_sb")
         offs_sb = keep.tile([P, S // LIST_ROWS], U16, name="offs_sb")
         rin_sb = [keep.tile([P, 2 * U], F32, name=f"rin_sb{t}", tag=f"slot{t}") for t in range(PACK - 1)]
-        xs_sb = keep.tile([P, T], U8, name="xs_sb", tag="xs")
-        w1_raw = [keep.tile([P, PACK, HALF], F32, name=f"w1_raw{a}", tag=f"slot{a + 3}") for a in range(2)]
-        xw_sb = keep.tile([P, T], I32, name="xw_sb", tag="x")
+        xs_sb = keep.tile([P, T], U8, name="xs_sb", tag="x")
+        w1_raw = keep.tile([P, PACK, H], F32, name="w1_raw", tag="slot3")
 
         nc.vector.memset(xs_sb[:112, :].bitcast(I32), 0)
 
@@ -65,11 +61,9 @@ def tile_picked_bens8_none_p_kernel(tc, x_words, x_scales, w1, rin, w2, so, offs
         nc.sync.dma_start(offs_sb[:], offs)
         nc.sync.dma_start(rin_sb[0][:, :U], plane_rows(rin, 0))
         nc.sync.dma_start(mem_sb[:], mem)
-        nc.sync.dma_start(w1_raw[0][:], weight_half(w1, 0))
         nc.sync.dma_start(rin_sb[1][:, :U], plane_rows(rin, 1))
-        nc.sync.dma_start(w1_raw[1][:], weight_half(w1, 1))
+        nc.sync.dma_start(w1_raw[:], w1.rearrange("(p j) c -> p j c", j=PACK))
         nc.sync.dma_start(rin_sb[2][:, :U], plane_rows(rin, 2))
-        nc.sync.dma_start(xw_sb[:], x_words[0].rearrange("p n r -> p (n r)").bitcast(I32))
 
         def list_half(list_sb, c):
             return list_sb[:, c * HALF // LIST_ROWS : (c + 1) * HALF // LIST_ROWS]
@@ -81,28 +75,30 @@ def tile_picked_bens8_none_p_kernel(tc, x_words, x_scales, w1, rin, w2, so, offs
         for r in range(4):
             nc.sync.dma_start(x_scale_picked[r:P:32, :].bitcast(I32), x_scale_spread[112 + r : P : 4, :].bitcast(I32))
 
-        rin_last = keep.tile([P, U], F32, name="rin_last", tag="xs")
-        nc.sync.dma_start(rin_last[:], plane_rows(rin, PACK - 1))
+        xw_sb = keep.tile([P, T], I32, name="xw_sb", tag="x")
+        nc.sync.dma_start(xw_sb[:], x_words[0].rearrange("p n r -> p (n r)").bitcast(I32))
 
         rin_picked = keep.tile([P, PACK, S], F32, name="rin_picked")
         for t in range(PACK - 1):
             nc.vector.tensor_copy(rin_picked[:, t, :], rin_sb[t][:].indirect(mem_sb[:]))
+        rin_last = keep.tile([P, U], F32, name="rin_last", tag="slot0")
+        nc.sync.dma_start(rin_last[:], plane_rows(rin, PACK - 1))
 
         w1_grouped = keep.tile([P, PACK * H], BF16, name="w1_grouped", align_bytes=64)
         w1_codes = keep.tile([P, H], U32, name="w1_codes", align_bytes=64)
         w1_scales = keep.tile([P, H], U8, name="w1_scales", align_bytes=64)
-        for a in range(2):
-            cast_weight_half(nc, w1_raw[a][:], w1_grouped[:], a, slice(0, 2))
-        quantize_weight_planes(nc, w1_grouped[:], w1_codes, w1_scales, 0, PACK)
+        for u in range(2):
+            pair = w1_grouped[:, u * 2 * H : (u + 1) * 2 * H]
+            cast_weight_pair(nc, w1_raw, pair, u)
+            quantize_weight_planes(nc, pair, w1_codes, w1_scales, 2 * u, 2)
 
-        w2_raw = keep.tile([P, 2, PACK, HALF], F32, name="w2_raw", tag="slot0")
-        for a in range(2):
-            nc.sync.dma_start(w2_raw[:, a], weight_half(w2, a))
-        so_sb = [keep.tile([P, U], F32, name=f"so_sb{t}", tag=f"slot{t + 1}") for t in range(2)]
+        w2_raw = keep.tile([P, PACK, N], F32, name="w2_raw", tag="slot1")
+        nc.sync.dma_start(w2_raw[:], w2.rearrange("(p j) c -> p j c", j=PACK))
+        so_sb = [keep.tile([P, U], F32, name=f"so_sb{t}", tag=f"slot{t + 2}") for t in range(2)]
         for t in range(2):
             nc.sync.dma_start(so_sb[t][:], plane_rows(so, t))
 
-        x_picked = [keep.tile([P, HALF], U32, name=f"x_picked{c}", align_bytes=64) for c in range(2)]
+        x_picked = [keep.tile([P, HALF], U32, name=f"x_picked{c}", tag=f"late{3 * c}", align_bytes=64) for c in range(2)]
         for c in range(2):
             nc.vector.tensor_copy(x_picked[c][:], xw_sb[:].bitcast(U32).indirect(list_half(offs_sb, c)))
 
@@ -110,20 +106,15 @@ def tile_picked_bens8_none_p_kernel(tc, x_words, x_scales, w1, rin, w2, so, offs
             nc.vector.tensor_copy(rin_picked[:, PACK - 1, c * HALF : (c + 1) * HALF], rin_last[:].indirect(list_half(mem_sb, c)))
 
         so_sb.append(keep.tile([P, U], F32, name="so_sb2", tag="x"))
-        so_sb.append(keep.tile([P, U], F32, name="so_sb3", tag="xs"))
+        so_sb.append(keep.tile([P, U], F32, name="so_sb3", tag="slot0"))
         for t in range(2, PACK):
             nc.sync.dma_start(so_sb[t][:], plane_rows(so, t))
 
-        late_grouped = keep.tile([P, PACK * QUARTER + PACK * N], BF16, name="late_grouped", align_bytes=64)
-        w2_grouped = late_grouped[:, PACK * QUARTER :]
         w2_codes = keep.tile([P, N], U32, name="w2_codes", align_bytes=64)
         w2_scales = keep.tile([P, N], U8, name="w2_scales", align_bytes=64)
-
-        z_first = keep.tile([P, PACK * HALF], BF16, name="z_first", align_bytes=64)
-        z_grouped = [z_first[:], late_grouped[:, : PACK * HALF]]
-        z_codes = [keep.tile([P, HALF], U32, name=f"z_codes{c}", align_bytes=64) for c in range(2)]
-        z_scales_second = keep.tile([P, HALF], U8, name="z_scales_second", align_bytes=64)
-        z_scales = [w2_scales[4:P, :HALF], z_scales_second[:]]
+        z_grouped = [keep.tile([P, PACK * HALF], BF16, name=f"z_grouped{c}", align_bytes=64) for c in range(2)]
+        z_scales = [keep.tile([P, HALF], U8, name=f"z_scales{c}", align_bytes=64) for c in range(2)]
+        z_codes = {}
 
         def hidden_product(c, s, t, target):
             cols = slice(s * QUARTER, (s + 1) * QUARTER)
@@ -138,77 +129,77 @@ def tile_picked_bens8_none_p_kernel(tc, x_words, x_scales, w1, rin, w2, so, offs
                 stop=True,
             )
 
-        def scale_quarter(engine, c, s, h_planes):
-            all_cols = slice(c * HALF + s * QUARTER, c * HALF + (s + 1) * QUARTER)
-            engine.tensor_tensor(
-                z_grouped[c][:, s * QUARTER * PACK : (s + 1) * QUARTER * PACK].rearrange("p (n i t) -> p n t i", i=2, t=PACK),
-                h_planes.rearrange("p t (n i) -> p n t i", i=2),
-                rin_picked[:, :, all_cols].rearrange("p t (n i) -> p n t i", i=2),
-                MULT,
-            )
-
         def hidden_quarter(c, s):
+            all_cols = slice(c * HALF + s * QUARTER, c * HALF + (s + 1) * QUARTER)
+            z_quarter = z_grouped[c][:, s * QUARTER * PACK : (s + 1) * QUARTER * PACK]
             if (c, s) == (0, 0):
-                h_sb = keep.tile([P, PACK, QUARTER], F32, name="h_sb")
+                h_sb = keep.tile([P, 2, QUARTER, 2], F32, name="h_sb")
                 for u in range(2):
                     h_pair = psum.tile([P, 2, QUARTER], F32, name=f"h_pair{u}", tag=f"o_bank{u + 2}")
                     for i in range(2):
                         hidden_product(c, s, 2 * u + i, h_pair[:, i, :])
-                    nc.scalar.copy(out=h_sb[:, 2 * u : 2 * u + 2, :], in_=h_pair[:])
-                scale_quarter(nc.gpsimd, c, s, h_sb[:])
+                    nc.scalar.copy(out=h_sb[:, u], in_=h_pair[:].rearrange("p i n -> p n i"))
+                nc.gpsimd.tensor_tensor(
+                    z_quarter.rearrange("p (n u i) -> p n u i", u=2, i=2),
+                    h_sb[:].rearrange("p u n i -> p n u i"),
+                    rin_picked[:, :, all_cols].rearrange("p (u i) n -> p n u i", u=2),
+                    MULT,
+                )
                 return
             h_bank = psum.tile([P, PACK, QUARTER], F32, name=f"h_bank{c}{s}")
             for t in range(PACK):
                 hidden_product(c, s, t, h_bank[:, t, :])
-            scale_quarter(nc.vector, c, s, h_bank[:])
+            nc.vector.tensor_tensor(
+                z_quarter.rearrange("p (n i t) -> p n t i", i=2, t=PACK),
+                h_bank[:].rearrange("p t (n i) -> p n t i", i=2),
+                rin_picked[:, :, all_cols].rearrange("p t (n i) -> p n t i", i=2),
+                MULT,
+            )
 
         def quantize_z(c):
-            nc.vector.quantize_mx(out=z_codes[c][:].bitcast(FP8X4), scales=z_scales[c], in_=z_grouped[c])
+            z_codes[c] = keep.tile([P, HALF], U32, name=f"z_codes{c}", tag=f"late{1 - c}", align_bytes=64)
+            nc.vector.quantize_mx(out=z_codes[c][:].bitcast(FP8X4), scales=z_scales[c][:], in_=z_grouped[c][:])
 
         out_rows = out.rearrange("(p t) s -> t p s", t=PACK)
 
         def prepare_w2_pair(u):
+            pair = keep.tile([P, 2 * N], BF16, name=f"w2_pair{u}", tag=f"late{2 * u}", align_bytes=64)
+            cast_weight_pair(nc, w2_raw, pair[:], u, 1 + 3 * u)
             if u == 0:
-                for a in range(2):
-                    cast_weight_half(nc, w2_raw[:, a], w2_grouped, a, slice(u, u + 1))
                 for t in range(2):
-                    quantize_weight_planes(nc, w2_grouped, w2_codes, w2_scales, t, 1)
+                    quantize_weight_planes(nc, pair[:, t * N : (t + 1) * N], w2_codes, w2_scales, t, 1)
             else:
-                for piece in range(4):
-                    rows = slice(16 * piece, 16 * piece + 16)
-                    nc.scalar.copy(
-                        out=w2_grouped.rearrange("p (u i a m j) -> p u a m j i", u=2, i=2, a=2, j=PACK)[:, u, :, rows],
-                        in_=w2_raw[:].rearrange("p a j (m u i) -> p u a m j i", u=2, i=2)[:, u, :, rows],
-                    )
-                quantize_weight_planes(nc, w2_grouped, w2_codes, w2_scales, 2 * u, 2)
+                quantize_weight_planes(nc, pair[:], w2_codes, w2_scales, 2 * u, 2)
 
-        def output_tile(c, t):
-            o_bank = psum.tile([P, HALF], F32, name=f"o_bank{t}", tag=f"o_bank{t}")
+        def output_piece(c, t, start, count, width, bank):
+            o_bank = psum.tile([P, count], F32, name=f"o_bank{c}{t}{start}", tag=bank)
             nc.tensor.matmul_mx(
                 out=o_bank[:],
                 lhsT=w2_codes[:, t * P : (t + 1) * P].bitcast(FP8X4),
                 lhsT_scale=w2_scales[:, t * P : (t + 1) * P],
-                rhs=z_codes[c][:].bitcast(FP8X4),
-                rhs_scale=z_scales[c],
+                rhs=z_codes[c][:, start : start + count].bitcast(FP8X4),
+                rhs_scale=z_scales[c][:, start : start + count],
                 start=True,
                 stop=True,
             )
-            o_sb = keep.tile([P, HALF], F32, name=f"o_sb{c}{t}")
-            result = keep.tile([P, HALF], F32, name=f"result{c}{t}")
+            o_sb = keep.tile([P, count], F32, name=f"o_sb{c}{t}{start}")
+            result = keep.tile([P, count], F32, name=f"result{c}{t}{start}")
             nc.scalar.copy(out=o_sb[:], in_=o_bank[:])
-            width = QUARTER if (c, t) == (1, PACK - 1) else HALF
-            for first in range(0, HALF, width):
-                token = c * HALF + first
+            for first in range(0, count, width):
+                token = c * HALF + start + first
                 offsets = mem_sb[:, token // LIST_ROWS : (token + width) // LIST_ROWS]
                 nc.vector.tensor_tensor(result[:, first : first + width], so_sb[t][:].indirect(offsets), o_sb[:, first : first + width], MULT)
                 nc.sync.dma_start(out_rows[t][:, token : token + width], result[:, first : first + width])
 
-        hidden_quarter(0, 0)
-        hidden_quarter(0, 1)
-        hidden_quarter(1, 0)
-        prepare_w2_pair(0)
-        hidden_quarter(1, 1)
+        def output_tile(c, t):
+            width = QUARTER if (c, t) == (1, PACK - 1) else HALF
+            output_piece(c, t, 0, HALF, width, f"o_bank{t}")
+
+        for c in range(2):
+            for s in range(2):
+                hidden_quarter(c, s)
         quantize_z(0)
+        prepare_w2_pair(0)
         quantize_z(1)
         output_tile(0, 0)
         output_tile(0, 1)

@@ -19,27 +19,35 @@ PACK = 4
 HALF = 256
 QUARTER = 128
 LIST_ROWS = 16
+SCALE_ROWS = 16
+GPSIMD_TOKENS = 160
+GPSIMD_FIRST = 64
 
 
 def plane_rows(table, t):
     return table.rearrange("(p t) u -> t p u", t=PACK)[t]
 
 
-def cast_weight_pair(nc, raw, grouped, u, pieces=1):
-    for piece in range(pieces):
-        rows = slice(piece * P // pieces, (piece + 1) * P // pieces)
-        nc.scalar.copy(
-            out=grouped.rearrange("p (i m j) -> p m j i", i=2, j=PACK)[:, rows],
-            in_=raw[:].rearrange("p j (m u i) -> p u m j i", u=2, i=2)[:, u, rows],
-        )
+def cast_weight_pair(nc, raw, grouped, u):
+    nc.scalar.copy(
+        out=grouped.rearrange("p (i m j) -> p m j i", i=2, j=PACK),
+        in_=raw[:].rearrange("p j (m u i) -> p u m j i", u=2, i=2)[:, u],
+    )
 
 
-def quantize_weight_planes(nc, grouped, codes, scales, first, count):
-    cols = slice(first * P, (first + count) * P)
-    nc.vector.quantize_mx(
-        out=codes[:, cols].bitcast(FP8X4),
-        scales=scales[:, cols],
-        in_=grouped,
+def quantize(nc, codes, scales, grouped):
+    nc.vector.quantize_mx(out=codes.bitcast(FP8X4), scales=scales, in_=grouped)
+
+
+def product(nc, target, w_codes, w_scales, t, codes, scales):
+    nc.tensor.matmul_mx(
+        out=target,
+        lhsT=w_codes[:, t * P : (t + 1) * P].bitcast(FP8X4),
+        lhsT_scale=w_scales[:, t * P : (t + 1) * P],
+        rhs=codes.bitcast(FP8X4),
+        rhs_scale=scales,
+        start=True,
+        stop=True,
     )
 
 
@@ -49,40 +57,47 @@ def tile_picked_bens8_none_p_kernel(tc, x_words, x_scales, w1, rin, w2, so, offs
         keep = ctx.enter_context(tc.tile_pool(name="keep", bufs=1))
         psum = ctx.enter_context(tc.psum_pool(name="psum", bufs=1))
 
+        def entries(list_sb, first, count):
+            return list_sb[:, first // LIST_ROWS : (first + count) // LIST_ROWS]
+
         mem_sb = keep.tile([P, S // LIST_ROWS], U16, name="mem_sb")
         offs_sb = keep.tile([P, S // LIST_ROWS], U16, name="offs_sb")
-        rin_sb = [keep.tile([P, 2 * U], F32, name=f"rin_sb{t}", tag=f"slot{t}") for t in range(PACK - 1)]
+        rin_sb = [keep.tile([P, 2 * U], F32, name=f"rin_sb{t}", tag=f"slot{t}") for t in range(PACK)]
         xs_sb = keep.tile([P, T], U8, name="xs_sb", tag="x")
-        w1_raw = keep.tile([P, PACK, H], F32, name="w1_raw", tag="slot3")
+        w1_raw = keep.tile([P, PACK, H], F32, name="w1_raw", tag="w1")
 
-        nc.vector.memset(xs_sb[:112, :].bitcast(I32), 0)
-
-        nc.sync.dma_start(xs_sb[112:P, :].bitcast(I32), x_scales[0].bitcast(I32))
+        first_row = P - SCALE_ROWS
+        nc.vector.memset(xs_sb[:first_row, :].bitcast(I32), 0)
+        nc.sync.dma_start(xs_sb[first_row:, :].bitcast(I32), x_scales[0].bitcast(I32))
         nc.sync.dma_start(offs_sb[:], offs)
         nc.sync.dma_start(rin_sb[0][:, :U], plane_rows(rin, 0))
         nc.sync.dma_start(mem_sb[:], mem)
         nc.sync.dma_start(rin_sb[1][:, :U], plane_rows(rin, 1))
-        nc.sync.dma_start(w1_raw[:], w1.rearrange("(p j) c -> p j c", j=PACK))
         nc.sync.dma_start(rin_sb[2][:, :U], plane_rows(rin, 2))
+        nc.sync.dma_start(w1_raw[:], w1.rearrange("(p j) c -> p j c", j=PACK))
+        nc.sync.dma_start(rin_sb[3][:, :U], plane_rows(rin, 3))
 
-        def list_half(list_sb, c):
-            return list_sb[:, c * HALF // LIST_ROWS : (c + 1) * HALF // LIST_ROWS]
-
-        x_scale_spread = keep.tile([P, S], U8, name="x_scale_spread", align_bytes=64)
-        nc.vector.tensor_copy(x_scale_spread[:], xs_sb[:].indirect(offs_sb[:]))
-        x_scale_picked = keep.tile([P, S], U8, name="x_scale_picked", align_bytes=64)
-        nc.vector.memset(x_scale_picked[:].bitcast(I32), 0)
+        xs_gathered = keep.tile([P, S], U8, name="xs_gathered", align_bytes=64)
+        nc.vector.tensor_copy(xs_gathered[:], xs_sb[:].indirect(offs_sb[:]))
+        xs_picked = keep.tile([P, S], U8, name="xs_picked", align_bytes=64)
+        nc.vector.memset(xs_picked[:].bitcast(I32), 0)
         for r in range(4):
-            nc.sync.dma_start(x_scale_picked[r:P:32, :].bitcast(I32), x_scale_spread[112 + r : P : 4, :].bitcast(I32))
+            nc.sync.dma_start(xs_picked[r:P:32, :].bitcast(I32), xs_gathered[first_row + r : P : 4, :].bitcast(I32))
 
         xw_sb = keep.tile([P, T], I32, name="xw_sb", tag="x")
         nc.sync.dma_start(xw_sb[:], x_words[0].rearrange("p n r -> p (n r)").bitcast(I32))
 
         rin_picked = keep.tile([P, PACK, S], F32, name="rin_picked")
-        for t in range(PACK - 1):
+        for t in range(PACK):
             nc.vector.tensor_copy(rin_picked[:, t, :], rin_sb[t][:].indirect(mem_sb[:]))
-        rin_last = keep.tile([P, U], F32, name="rin_last", tag="slot0")
-        nc.sync.dma_start(rin_last[:], plane_rows(rin, PACK - 1))
+
+        so_sb = [keep.tile([P, 2 * U], F32, name="so_sb0", tag="slot0")]
+        nc.sync.dma_start(so_sb[0][:, :U], plane_rows(so, 0))
+        w2_raw = keep.tile([P, PACK, N], F32, name="w2_raw", tag="slot1")
+        nc.sync.dma_start(w2_raw[:], w2.rearrange("(p j) c -> p j c", j=PACK))
+        for t, tag in ((1, "slot2"), (2, "slot3"), (3, "w1")):
+            so_sb.append(keep.tile([P, 2 * U], F32, name=f"so_sb{t}", tag=tag))
+            nc.sync.dma_start(so_sb[t][:, :U], plane_rows(so, t))
 
         w1_grouped = keep.tile([P, PACK * H], BF16, name="w1_grouped", align_bytes=64)
         w1_codes = keep.tile([P, H], U32, name="w1_codes", align_bytes=64)
@@ -90,122 +105,94 @@ def tile_picked_bens8_none_p_kernel(tc, x_words, x_scales, w1, rin, w2, so, offs
         for u in range(2):
             pair = w1_grouped[:, u * 2 * H : (u + 1) * 2 * H]
             cast_weight_pair(nc, w1_raw, pair, u)
-            quantize_weight_planes(nc, pair, w1_codes, w1_scales, 2 * u, 2)
+            quantize(nc, w1_codes[:, u * HALF : (u + 1) * HALF], w1_scales[:, u * HALF : (u + 1) * HALF], pair)
 
-        w2_raw = keep.tile([P, PACK, N], F32, name="w2_raw", tag="slot1")
-        nc.sync.dma_start(w2_raw[:], w2.rearrange("(p j) c -> p j c", j=PACK))
-        so_sb = [keep.tile([P, U], F32, name=f"so_sb{t}", tag=f"slot{t + 2}") for t in range(2)]
-        for t in range(2):
-            nc.sync.dma_start(so_sb[t][:], plane_rows(so, t))
+        rin_woven = keep.tile([P, GPSIMD_TOKENS, PACK], F32, name="rin_woven")
+        nc.scalar.copy(out=rin_woven[:], in_=rin_picked[:, :, :GPSIMD_TOKENS].rearrange("p t n -> p n t"))
 
         x_picked = [keep.tile([P, HALF], U32, name=f"x_picked{c}", tag=f"late{3 * c}", align_bytes=64) for c in range(2)]
         for c in range(2):
-            nc.vector.tensor_copy(x_picked[c][:], xw_sb[:].bitcast(U32).indirect(list_half(offs_sb, c)))
+            nc.vector.tensor_copy(x_picked[c][:], xw_sb[:].bitcast(U32).indirect(entries(offs_sb, c * HALF, HALF)))
 
-        for c in range(2):
-            nc.vector.tensor_copy(rin_picked[:, PACK - 1, c * HALF : (c + 1) * HALF], rin_last[:].indirect(list_half(mem_sb, c)))
+        so_picked = keep.tile([P, S], F32, name="so_picked")
+        nc.vector.tensor_copy(so_picked[:], so_sb[0][:].indirect(mem_sb[:]))
 
-        so_sb.append(keep.tile([P, U], F32, name="so_sb2", tag="x"))
-        so_sb.append(keep.tile([P, U], F32, name="so_sb3", tag="slot0"))
-        for t in range(2, PACK):
-            nc.sync.dma_start(so_sb[t][:], plane_rows(so, t))
-
-        w2_codes = keep.tile([P, N], U32, name="w2_codes", align_bytes=64)
-        w2_scales = keep.tile([P, N], U8, name="w2_scales", align_bytes=64)
         z_grouped = [keep.tile([P, PACK * HALF], BF16, name=f"z_grouped{c}", align_bytes=64) for c in range(2)]
         z_scales = [keep.tile([P, HALF], U8, name=f"z_scales{c}", align_bytes=64) for c in range(2)]
         z_codes = {}
+        h_woven = keep.tile([P, GPSIMD_TOKENS, PACK], F32, name="h_woven")
 
-        def hidden_product(c, s, t, target):
-            cols = slice(s * QUARTER, (s + 1) * QUARTER)
-            all_cols = slice(c * HALF + s * QUARTER, c * HALF + (s + 1) * QUARTER)
-            nc.tensor.matmul_mx(
-                out=target,
-                lhsT=w1_codes[:, t * P : (t + 1) * P].bitcast(FP8X4),
-                lhsT_scale=w1_scales[:, t * P : (t + 1) * P],
-                rhs=x_picked[c][:, cols].bitcast(FP8X4),
-                rhs_scale=x_scale_picked[:, all_cols],
-                start=True,
-                stop=True,
-            )
+        def weave_h(h_bank, token, start, stop):
+            nc.scalar.copy(out=h_woven[:, start:stop, :], in_=h_bank[:, :, start - token : stop - token].rearrange("p t n -> p n t"))
 
-        def hidden_quarter(c, s):
-            all_cols = slice(c * HALF + s * QUARTER, c * HALF + (s + 1) * QUARTER)
-            z_quarter = z_grouped[c][:, s * QUARTER * PACK : (s + 1) * QUARTER * PACK]
-            if (c, s) == (0, 0):
-                h_sb = keep.tile([P, 2, QUARTER, 2], F32, name="h_sb")
-                for u in range(2):
-                    h_pair = psum.tile([P, 2, QUARTER], F32, name=f"h_pair{u}", tag=f"o_bank{u + 2}")
-                    for i in range(2):
-                        hidden_product(c, s, 2 * u + i, h_pair[:, i, :])
-                    nc.scalar.copy(out=h_sb[:, u], in_=h_pair[:].rearrange("p i n -> p n i"))
-                nc.gpsimd.tensor_tensor(
-                    z_quarter.rearrange("p (n u i) -> p n u i", u=2, i=2),
-                    h_sb[:].rearrange("p u n i -> p n u i"),
-                    rin_picked[:, :, all_cols].rearrange("p (u i) n -> p n u i", u=2),
-                    MULT,
-                )
-                return
-            h_bank = psum.tile([P, PACK, QUARTER], F32, name=f"h_bank{c}{s}")
-            for t in range(PACK):
-                hidden_product(c, s, t, h_bank[:, t, :])
-            nc.vector.tensor_tensor(
-                z_quarter.rearrange("p (n i t) -> p n t i", i=2, t=PACK),
-                h_bank[:].rearrange("p t (n i) -> p n t i", i=2),
-                rin_picked[:, :, all_cols].rearrange("p t (n i) -> p n t i", i=2),
+        def gpsimd_product(start, stop):
+            nc.gpsimd.tensor_tensor(
+                z_grouped[0][:, start * PACK : stop * PACK],
+                h_woven[:, start:stop, :].rearrange("p n t -> p (n t)"),
+                rin_woven[:, start:stop, :].rearrange("p n t -> p (n t)"),
                 MULT,
             )
 
+        def hidden_quarter(q):
+            c, first = divmod(q * QUARTER, HALF)
+            token = q * QUARTER
+            h_bank = psum.tile([P, PACK, QUARTER], F32, name=f"h_bank{q}")
+            for t in range(PACK):
+                product(nc, h_bank[:, t, :], w1_codes, w1_scales, t, x_picked[c][:, first : first + QUARTER], xs_picked[:, token : token + QUARTER])
+            share = min(max(GPSIMD_TOKENS - token, 0), QUARTER)
+            if q == 0:
+                weave_h(h_bank, token, 0, GPSIMD_FIRST)
+                gpsimd_product(0, GPSIMD_FIRST)
+                weave_h(h_bank, token, GPSIMD_FIRST, QUARTER)
+            if q == 1:
+                weave_h(h_bank, token, QUARTER, GPSIMD_TOKENS)
+                gpsimd_product(GPSIMD_FIRST, GPSIMD_TOKENS)
+            if share < QUARTER:
+                nc.vector.tensor_tensor(
+                    z_grouped[c][:, (first + share) * PACK : (first + QUARTER) * PACK].rearrange("p (n i t) -> p n t i", i=2, t=PACK),
+                    h_bank[:, :, share:].rearrange("p t (n i) -> p n t i", i=2),
+                    rin_picked[:, :, token + share : token + QUARTER].rearrange("p t (n i) -> p n t i", i=2),
+                    MULT,
+                )
+
         def quantize_z(c):
             z_codes[c] = keep.tile([P, HALF], U32, name=f"z_codes{c}", tag=f"late{1 - c}", align_bytes=64)
-            nc.vector.quantize_mx(out=z_codes[c][:].bitcast(FP8X4), scales=z_scales[c][:], in_=z_grouped[c][:])
+            quantize(nc, z_codes[c][:], z_scales[c][:], z_grouped[c][:])
 
-        out_rows = out.rearrange("(p t) s -> t p s", t=PACK)
+        w2_codes = keep.tile([P, N], U32, name="w2_codes", align_bytes=64)
+        w2_scales = keep.tile([P, N], U8, name="w2_scales", align_bytes=64)
 
         def prepare_w2_pair(u):
             pair = keep.tile([P, 2 * N], BF16, name=f"w2_pair{u}", tag=f"late{2 * u}", align_bytes=64)
-            cast_weight_pair(nc, w2_raw, pair[:], u, 1 + 3 * u)
-            if u == 0:
-                for t in range(2):
-                    quantize_weight_planes(nc, pair[:, t * N : (t + 1) * N], w2_codes, w2_scales, t, 1)
-            else:
-                quantize_weight_planes(nc, pair[:], w2_codes, w2_scales, 2 * u, 2)
+            cast_weight_pair(nc, w2_raw, pair[:], u)
+            planes = 1 + u
+            for t in range(0, 2, planes):
+                cols = slice((2 * u + t) * P, (2 * u + t + planes) * P)
+                quantize(nc, w2_codes[:, cols], w2_scales[:, cols], pair[:, t * N : (t + planes) * N])
 
-        def output_piece(c, t, start, count, width, bank):
-            o_bank = psum.tile([P, count], F32, name=f"o_bank{c}{t}{start}", tag=bank)
-            nc.tensor.matmul_mx(
-                out=o_bank[:],
-                lhsT=w2_codes[:, t * P : (t + 1) * P].bitcast(FP8X4),
-                lhsT_scale=w2_scales[:, t * P : (t + 1) * P],
-                rhs=z_codes[c][:, start : start + count].bitcast(FP8X4),
-                rhs_scale=z_scales[c][:, start : start + count],
-                start=True,
-                stop=True,
-            )
-            o_sb = keep.tile([P, count], F32, name=f"o_sb{c}{t}{start}")
-            result = keep.tile([P, count], F32, name=f"result{c}{t}{start}")
+        out_rows = out.rearrange("(p t) s -> t p s", t=PACK)
+
+        def output_tile(t, c, width):
+            o_bank = psum.tile([P, HALF], F32, name=f"o_bank{t}{c}", tag=f"o_bank{(2 * t + c) % 4}")
+            product(nc, o_bank[:], w2_codes, w2_scales, t, z_codes[c][:], z_scales[c][:])
+            result = keep.tile([P, HALF], F32, name=f"result{t}{c}")
+            if t == 0:
+                nc.vector.tensor_tensor(result[:], o_bank[:], so_picked[:, c * HALF : (c + 1) * HALF], MULT)
+                nc.sync.dma_start(out_rows[t][:, c * HALF : (c + 1) * HALF], result[:])
+                return
+            o_sb = keep.tile([P, HALF], F32, name=f"o_sb{t}{c}")
             nc.scalar.copy(out=o_sb[:], in_=o_bank[:])
-            for first in range(0, count, width):
-                token = c * HALF + start + first
-                offsets = mem_sb[:, token // LIST_ROWS : (token + width) // LIST_ROWS]
-                nc.vector.tensor_tensor(result[:, first : first + width], so_sb[t][:].indirect(offsets), o_sb[:, first : first + width], MULT)
+            for first in range(0, HALF, width):
+                token = c * HALF + first
+                nc.vector.tensor_tensor(result[:, first : first + width], so_sb[t][:].indirect(entries(mem_sb, token, width)), o_sb[:, first : first + width], MULT)
                 nc.sync.dma_start(out_rows[t][:, token : token + width], result[:, first : first + width])
 
-        def output_tile(c, t):
-            width = QUARTER if (c, t) == (1, PACK - 1) else HALF
-            output_piece(c, t, 0, HALF, width, f"o_bank{t}")
-
-        for c in range(2):
-            for s in range(2):
-                hidden_quarter(c, s)
+        for q in range(S // QUARTER):
+            hidden_quarter(q)
         quantize_z(0)
         prepare_w2_pair(0)
         quantize_z(1)
-        output_tile(0, 0)
-        output_tile(0, 1)
         prepare_w2_pair(1)
-        output_tile(1, 0)
-        output_tile(1, 1)
-        for c in range(2):
-            output_tile(c, 2)
-            output_tile(c, 3)
+        for t in range(PACK):
+            for c in range(2):
+                output_tile(t, c, QUARTER if (t, c) == (PACK - 1, 1) else HALF)

@@ -68,7 +68,7 @@ def tile_picked_bens8_none_p_kernel(tc, x_words, x_scales, w1, rin, w2, so, offs
 
         first_row = P - SCALE_ROWS
         nc.vector.memset(xs_sb[:first_row, :].bitcast(I32), 0)
-        nc.sync.dma_start(xs_sb[first_row:, :].bitcast(I32), x_scales[0].bitcast(I32))
+        nc.scalar.dma_start(xs_sb[first_row:, :].bitcast(I32), x_scales[0].bitcast(I32))
         nc.sync.dma_start(offs_sb[:], offs)
         nc.sync.dma_start(rin_sb[0][:, :U], plane_rows(rin, 0))
         nc.sync.dma_start(mem_sb[:], mem)

@@ -13,6 +13,7 @@ U16 = mybir.dt.uint16
 U8 = mybir.dt.uint8
 FP8X4 = mybir.dt.float8_e4m3fn_x4
 MULT = mybir.AluOpType.mult
+ADD = mybir.AluOpType.add
 
 P = 128
 PACK = 4
@@ -55,6 +56,7 @@ def tile_picked_bens8_none_p_kernel(tc, x_words, x_scales, w1, rin, w2, so, offs
     nc = tc.nc
     with ExitStack() as ctx:
         keep = ctx.enter_context(tc.tile_pool(name="keep", bufs=1))
+        late = ctx.enter_context(tc.tile_pool(name="late", bufs=1))
         psum = ctx.enter_context(tc.psum_pool(name="psum", bufs=1))
 
         def entries(list_sb, first, count):
@@ -63,8 +65,8 @@ def tile_picked_bens8_none_p_kernel(tc, x_words, x_scales, w1, rin, w2, so, offs
         mem_sb = keep.tile([P, S // LIST_ROWS], U16, name="mem_sb")
         offs_sb = keep.tile([P, S // LIST_ROWS], U16, name="offs_sb")
         rin_sb = [keep.tile([P, 2 * U], F32, name=f"rin_sb{t}", tag=f"slot{t}") for t in range(PACK)]
-        xs_sb = keep.tile([P, T], U8, name="xs_sb", tag="x")
-        w1_raw = keep.tile([P, PACK, H], F32, name="w1_raw", tag="w1")
+        xs_sb = keep.tile([P, T], U8, name="xs_sb")
+        w1_raw = late.tile([P, PACK, H], F32, name="w1_raw", offset=0)
 
         first_row = P - SCALE_ROWS
         nc.vector.memset(xs_sb[:first_row, :].bitcast(I32), 0)
@@ -76,6 +78,8 @@ def tile_picked_bens8_none_p_kernel(tc, x_words, x_scales, w1, rin, w2, so, offs
         nc.sync.dma_start(rin_sb[2][:, :U], plane_rows(rin, 2))
         nc.sync.dma_start(w1_raw[:], w1.rearrange("(p j) c -> p j c", j=PACK))
         nc.sync.dma_start(rin_sb[3][:, :U], plane_rows(rin, 3))
+        xw_sb = keep.tile([P, T], I32, name="xw_sb", tag="x")
+        nc.sync.dma_start(xw_sb[:], x_words[0].rearrange("p n r -> p (n r)").bitcast(I32))
 
         xs_gathered = keep.tile([P, S], U8, name="xs_gathered", align_bytes=64)
         nc.vector.tensor_copy(xs_gathered[:], xs_sb[:].indirect(offs_sb[:]))
@@ -83,9 +87,6 @@ def tile_picked_bens8_none_p_kernel(tc, x_words, x_scales, w1, rin, w2, so, offs
         nc.vector.memset(xs_picked[:].bitcast(I32), 0)
         for r in range(4):
             nc.sync.dma_start(xs_picked[r:P:32, :].bitcast(I32), xs_gathered[first_row + r : P : 4, :].bitcast(I32))
-
-        xw_sb = keep.tile([P, T], I32, name="xw_sb", tag="x")
-        nc.sync.dma_start(xw_sb[:], x_words[0].rearrange("p n r -> p (n r)").bitcast(I32))
 
         rin_picked = keep.tile([P, PACK, S], F32, name="rin_picked")
         for t in range(PACK):
@@ -95,7 +96,7 @@ def tile_picked_bens8_none_p_kernel(tc, x_words, x_scales, w1, rin, w2, so, offs
         nc.sync.dma_start(so_sb[0][:, :U], plane_rows(so, 0))
         w2_raw = keep.tile([P, PACK, N], F32, name="w2_raw", tag="slot1")
         nc.sync.dma_start(w2_raw[:], w2.rearrange("(p j) c -> p j c", j=PACK))
-        for t, tag in ((1, "slot2"), (2, "slot3"), (3, "w1")):
+        for t, tag in ((1, "slot2"), (2, "slot3")):
             so_sb.append(keep.tile([P, 2 * U], F32, name=f"so_sb{t}", tag=tag))
             nc.sync.dma_start(so_sb[t][:, :U], plane_rows(so, t))
 
@@ -104,17 +105,29 @@ def tile_picked_bens8_none_p_kernel(tc, x_words, x_scales, w1, rin, w2, so, offs
         w1_scales = keep.tile([P, H], U8, name="w1_scales", align_bytes=64)
         for u in range(2):
             pair = w1_grouped[:, u * 2 * H : (u + 1) * 2 * H]
-            cast_weight_pair(nc, w1_raw, pair, u)
-            quantize(nc, w1_codes[:, u * HALF : (u + 1) * HALF], w1_scales[:, u * HALF : (u + 1) * HALF], pair)
+            if u == 0:
+                cast_weight_pair(nc, w1_raw, pair, u)
+            else:
+                target = pair.rearrange("p (i m j) -> p i m j", i=2, j=PACK)
+                source = w1_raw[:].rearrange("p j (m u i) -> p u i m j", u=2, i=2)[:, u]
+                nc.scalar.copy(
+                    out=target[:, :, : P // 2].rearrange("p i m j -> p m j i"),
+                    in_=source[:, :, : P // 2].rearrange("p i m j -> p m j i"),
+                )
+                for i in range(2):
+                    nc.gpsimd.tensor_scalar(target[:, i, P // 2 :], source[:, i, P // 2 :], 1.0, 0.0, MULT, ADD)
+        quantize(nc, w1_codes[:], w1_scales[:], w1_grouped[:])
 
         rin_woven = keep.tile([P, GPSIMD_TOKENS, PACK], F32, name="rin_woven")
         nc.scalar.copy(out=rin_woven[:], in_=rin_picked[:, :, :GPSIMD_TOKENS].rearrange("p t n -> p n t"))
 
-        x_picked = [keep.tile([P, HALF], U32, name=f"x_picked{c}", tag=f"late{3 * c}", align_bytes=64) for c in range(2)]
+        x_picked = [late.tile([P, HALF], U32, name=f"x_picked{c}", offset=2048 * c, align_bytes=64) for c in range(2)]
         for c in range(2):
             nc.vector.tensor_copy(x_picked[c][:], xw_sb[:].bitcast(U32).indirect(entries(offs_sb, c * HALF, HALF)))
 
-        so_picked = keep.tile([P, S], F32, name="so_picked")
+        so_sb.append(keep.tile([P, 2 * U], F32, name="so_sb3", tag="x"))
+        nc.sync.dma_start(so_sb[3][:, :U], plane_rows(so, 3))
+        so_picked = late.tile([P, S], F32, name="so_picked", offset=4096)
         nc.vector.tensor_copy(so_picked[:], so_sb[0][:].indirect(mem_sb[:]))
 
         z_grouped = [keep.tile([P, PACK * HALF], BF16, name=f"z_grouped{c}", align_bytes=64) for c in range(2)]
@@ -156,14 +169,14 @@ def tile_picked_bens8_none_p_kernel(tc, x_words, x_scales, w1, rin, w2, so, offs
                 )
 
         def quantize_z(c):
-            z_codes[c] = keep.tile([P, HALF], U32, name=f"z_codes{c}", tag=f"late{1 - c}", align_bytes=64)
+            z_codes[c] = late.tile([P, HALF], U32, name=f"z_codes{c}", offset=0 if c else 8192, align_bytes=64)
             quantize(nc, z_codes[c][:], z_scales[c][:], z_grouped[c][:])
 
         w2_codes = keep.tile([P, N], U32, name="w2_codes", align_bytes=64)
         w2_scales = keep.tile([P, N], U8, name="w2_scales", align_bytes=64)
 
         def prepare_w2_pair(u):
-            pair = keep.tile([P, 2 * N], BF16, name=f"w2_pair{u}", tag=f"late{2 * u}", align_bytes=64)
+            pair = late.tile([P, 2 * N], BF16, name=f"w2_pair{u}", offset=2048 * u, align_bytes=64)
             cast_weight_pair(nc, w2_raw, pair[:], u)
             planes = 1 + u
             for t in range(0, 2, planes):

@@ -21,7 +21,7 @@ HALF = 256
 QUARTER = 128
 LIST_ROWS = 16
 SCALE_ROWS = 16
-GPSIMD_TOKENS = 160
+GPSIMD_TOKENS = 128
 GPSIMD_FIRST = 64
 
 
@@ -157,9 +157,7 @@ def tile_picked_bens8_none_p_kernel(tc, x_words, x_scales, w1, rin, w2, so, offs
                 weave_h(h_bank, token, 0, GPSIMD_FIRST)
                 gpsimd_product(0, GPSIMD_FIRST)
                 weave_h(h_bank, token, GPSIMD_FIRST, QUARTER)
-            if q == 1:
-                weave_h(h_bank, token, QUARTER, GPSIMD_TOKENS)
-                gpsimd_product(GPSIMD_FIRST, GPSIMD_TOKENS)
+                gpsimd_product(GPSIMD_FIRST, QUARTER)
             if share < QUARTER:
                 nc.vector.tensor_tensor(
                     z_grouped[c][:, (first + share) * PACK : (first + QUARTER) * PACK].rearrange("p (n i t) -> p n t i", i=2, t=PACK),

@@ -13,7 +13,7 @@ U16 = mybir.dt.uint16
 U8 = mybir.dt.uint8
 FP8X4 = mybir.dt.float8_e4m3fn_x4
 MULT = mybir.AluOpType.mult
-ADD = mybir.AluOpType.add
+COPY = mybir.ActivationFunctionType.Copy
 
 P = 128
 PACK = 4
@@ -21,18 +21,17 @@ HALF = 256
 QUARTER = 128
 LIST_ROWS = 16
 SCALE_ROWS = 16
-GPSIMD_TOKENS = 128
-GPSIMD_FIRST = 64
+PLANE_BYTES = 4 * U
 
 
 def plane_rows(table, t):
     return table.rearrange("(p t) u -> t p u", t=PACK)[t]
 
 
-def cast_weight_pair(nc, raw, grouped, u):
-    nc.scalar.copy(
-        out=grouped.rearrange("p (i m j) -> p m j i", i=2, j=PACK),
-        in_=raw[:].rearrange("p j (m u i) -> p u m j i", u=2, i=2)[:, u],
+def weight_pair_views(raw, grouped, u):
+    return (
+        grouped.rearrange("p (i m j) -> p m j i", i=2, j=PACK),
+        raw[:].rearrange("p j (m u i) -> p u m j i", u=2, i=2)[:, u],
     )
 
 
@@ -64,21 +63,27 @@ def tile_picked_bens8_none_p_kernel(tc, x_words, x_scales, w1, rin, w2, so, offs
 
         mem_sb = keep.tile([P, S // LIST_ROWS], U16, name="mem_sb")
         offs_sb = keep.tile([P, S // LIST_ROWS], U16, name="offs_sb")
-        rin_sb = [keep.tile([P, 2 * U], F32, name=f"rin_sb{t}", tag=f"slot{t}") for t in range(PACK)]
-        xs_sb = keep.tile([P, T], U8, name="xs_sb")
+
+        def fetch_on_scalar(target, window, first, count):
+            nc.scalar.activation(target, window[:].indirect(entries(mem_sb, first, count)), COPY)
+
+        def fetch_on_vector(target, window, first, count):
+            nc.vector.tensor_copy(target, window[:].indirect(entries(mem_sb, first, count)))
+
+        rin_sb = [keep.tile([P, U], F32, name=f"rin_sb{t}", tag=f"slot{t}") for t in range(PACK - 1)]
+        xs_sb = keep.tile([P, T], U8, name="xs_sb", tag="slot3")
         w1_raw = late.tile([P, PACK, H], F32, name="w1_raw", offset=0)
+        xw_sb = keep.tile([P, T], I32, name="xw_sb")
 
         first_row = P - SCALE_ROWS
         nc.vector.memset(xs_sb[:first_row, :].bitcast(I32), 0)
         nc.scalar.dma_start(xs_sb[first_row:, :].bitcast(I32), x_scales[0].bitcast(I32))
         nc.sync.dma_start(offs_sb[:], offs)
-        nc.sync.dma_start(rin_sb[0][:, :U], plane_rows(rin, 0))
+        nc.sync.dma_start(rin_sb[0][:], plane_rows(rin, 0))
         nc.sync.dma_start(mem_sb[:], mem)
-        nc.sync.dma_start(rin_sb[1][:, :U], plane_rows(rin, 1))
-        nc.sync.dma_start(rin_sb[2][:, :U], plane_rows(rin, 2))
+        nc.sync.dma_start(rin_sb[1][:], plane_rows(rin, 1))
         nc.sync.dma_start(w1_raw[:], w1.rearrange("(p j) c -> p j c", j=PACK))
-        nc.sync.dma_start(rin_sb[3][:, :U], plane_rows(rin, 3))
-        xw_sb = keep.tile([P, T], I32, name="xw_sb", tag="x")
+        nc.sync.dma_start(rin_sb[2][:], plane_rows(rin, 2))
         nc.sync.dma_start(xw_sb[:], x_words[0].rearrange("p n r -> p (n r)").bitcast(I32))
 
         xs_gathered = keep.tile([P, S], U8, name="xs_gathered", align_bytes=64)
@@ -87,123 +92,100 @@ def tile_picked_bens8_none_p_kernel(tc, x_words, x_scales, w1, rin, w2, so, offs
         nc.vector.memset(xs_picked[:].bitcast(I32), 0)
         for r in range(4):
             nc.sync.dma_start(xs_picked[r:P:32, :].bitcast(I32), xs_gathered[first_row + r : P : 4, :].bitcast(I32))
+        rin_sb.append(keep.tile([P, U], F32, name="rin_sb3", tag="slot3"))
+        nc.sync.dma_start(rin_sb[3][:], plane_rows(rin, 3))
 
-        rin_picked = keep.tile([P, PACK, S], F32, name="rin_picked")
-        for t in range(PACK):
-            nc.vector.tensor_copy(rin_picked[:, t, :], rin_sb[t][:].indirect(mem_sb[:]))
+        rin_picked = [keep.tile([P, PACK, HALF], F32, name=f"rin_picked{c}") for c in range(2)]
+        for t in range(2):
+            for c in range(2):
+                fetch_on_vector(rin_picked[c][:, t, :], rin_sb[t], c * HALF, HALF)
 
-        so_sb = [keep.tile([P, 2 * U], F32, name="so_sb0", tag="slot0")]
-        nc.sync.dma_start(so_sb[0][:, :U], plane_rows(so, 0))
+        so_sb = [keep.tile([P, U], F32, name="so_sb0", tag="slot0")]
+        nc.sync.dma_start(so_sb[0][:], plane_rows(so, 0))
         w2_raw = keep.tile([P, PACK, N], F32, name="w2_raw", tag="slot1")
         nc.sync.dma_start(w2_raw[:], w2.rearrange("(p j) c -> p j c", j=PACK))
-        for t, tag in ((1, "slot2"), (2, "slot3")):
-            so_sb.append(keep.tile([P, 2 * U], F32, name=f"so_sb{t}", tag=tag))
-            nc.sync.dma_start(so_sb[t][:, :U], plane_rows(so, t))
 
-        w1_grouped = keep.tile([P, PACK * H], BF16, name="w1_grouped", align_bytes=64)
+        def cast_weight(raw, grouped):
+            target, source = weight_pair_views(raw, grouped[0][:], 0)
+            nc.vector.tensor_copy(target, source)
+            target, source = weight_pair_views(raw, grouped[1][:], 1)
+            nc.scalar.copy(out=target, in_=source)
+
+        def quantize_pair(codes, scales, grouped, u):
+            cols = slice(2 * u * P, 2 * (u + 1) * P)
+            quantize(nc, codes[:, cols], scales[:, cols], grouped[u][:])
+
+        w1_grouped = [keep.tile([P, 2 * H], BF16, name=f"w1_grouped{u}", align_bytes=64) for u in range(2)]
         w1_codes = keep.tile([P, H], U32, name="w1_codes", align_bytes=64)
         w1_scales = keep.tile([P, H], U8, name="w1_scales", align_bytes=64)
+        cast_weight(w1_raw, w1_grouped)
         for u in range(2):
-            pair = w1_grouped[:, u * 2 * H : (u + 1) * 2 * H]
-            if u == 0:
-                cast_weight_pair(nc, w1_raw, pair, u)
-            else:
-                target = pair.rearrange("p (i m j) -> p i m j", i=2, j=PACK)
-                source = w1_raw[:].rearrange("p j (m u i) -> p u i m j", u=2, i=2)[:, u]
-                nc.scalar.copy(
-                    out=target[:, :, : P // 2].rearrange("p i m j -> p m j i"),
-                    in_=source[:, :, : P // 2].rearrange("p i m j -> p m j i"),
-                )
-                for i in range(2):
-                    nc.gpsimd.tensor_scalar(target[:, i, P // 2 :], source[:, i, P // 2 :], 1.0, 0.0, MULT, ADD)
-        quantize(nc, w1_codes[:], w1_scales[:], w1_grouped[:])
+            quantize_pair(w1_codes, w1_scales, w1_grouped, u)
 
-        rin_woven = keep.tile([P, GPSIMD_TOKENS, PACK], F32, name="rin_woven")
-        nc.scalar.copy(out=rin_woven[:], in_=rin_picked[:, :, :GPSIMD_TOKENS].rearrange("p t n -> p n t"))
-
-        x_picked = [late.tile([P, HALF], U32, name=f"x_picked{c}", offset=2048 * c, align_bytes=64) for c in range(2)]
         for c in range(2):
-            nc.vector.tensor_copy(x_picked[c][:], xw_sb[:].bitcast(U32).indirect(entries(offs_sb, c * HALF, HALF)))
+            fetch_on_scalar(rin_picked[c][:, 2, :], rin_sb[2], c * HALF, HALF)
 
-        so_sb.append(keep.tile([P, 2 * U], F32, name="so_sb3", tag="x"))
-        nc.sync.dma_start(so_sb[3][:, :U], plane_rows(so, 3))
-        so_picked = late.tile([P, S], F32, name="so_picked", offset=4096)
-        nc.vector.tensor_copy(so_picked[:], so_sb[0][:].indirect(mem_sb[:]))
+        for t in range(1, PACK):
+            so_sb.append(late.tile([P, U], F32, name=f"so_sb{t}", offset=(t - 1) * PLANE_BYTES))
+            nc.sync.dma_start(so_sb[t][:], plane_rows(so, t))
+
+        x_picked = keep.tile([P, S], U32, name="x_picked", align_bytes=64)
+        for first, count in ((0, QUARTER), (QUARTER, QUARTER), (HALF, HALF)):
+            nc.vector.tensor_copy(x_picked[:, first : first + count], xw_sb[:].bitcast(U32).indirect(entries(offs_sb, first, count)))
+        for c in range(2):
+            fetch_on_scalar(rin_picked[c][:, 3, :], rin_sb[3], c * HALF, HALF)
+
+        so_picked = [keep.tile([P, S], F32, name=f"so_picked{t}") for t in range(PACK)]
+        for c in range(2):
+            fetch_on_scalar(so_picked[0][:, c * HALF : (c + 1) * HALF], so_sb[0], c * HALF, HALF)
 
         z_grouped = [keep.tile([P, PACK * HALF], BF16, name=f"z_grouped{c}", align_bytes=64) for c in range(2)]
-        z_scales = [keep.tile([P, HALF], U8, name=f"z_scales{c}", align_bytes=64) for c in range(2)]
-        z_codes = {}
-        h_woven = keep.tile([P, GPSIMD_TOKENS, PACK], F32, name="h_woven")
-
-        def weave_h(h_bank, token, start, stop):
-            nc.scalar.copy(out=h_woven[:, start:stop, :], in_=h_bank[:, :, start - token : stop - token].rearrange("p t n -> p n t"))
-
-        def gpsimd_product(start, stop):
-            nc.gpsimd.tensor_tensor(
-                z_grouped[0][:, start * PACK : stop * PACK],
-                h_woven[:, start:stop, :].rearrange("p n t -> p (n t)"),
-                rin_woven[:, start:stop, :].rearrange("p n t -> p (n t)"),
-                MULT,
-            )
+        z_codes = keep.tile([P, S], U32, name="z_codes", align_bytes=64)
+        z_scales = keep.tile([P, S], U8, name="z_scales", align_bytes=64)
 
         def hidden_quarter(q):
             c, first = divmod(q * QUARTER, HALF)
-            token = q * QUARTER
+            tokens = slice(q * QUARTER, (q + 1) * QUARTER)
             h_bank = psum.tile([P, PACK, QUARTER], F32, name=f"h_bank{q}")
             for t in range(PACK):
-                product(nc, h_bank[:, t, :], w1_codes, w1_scales, t, x_picked[c][:, first : first + QUARTER], xs_picked[:, token : token + QUARTER])
-            share = min(max(GPSIMD_TOKENS - token, 0), QUARTER)
-            if q == 0:
-                weave_h(h_bank, token, 0, GPSIMD_FIRST)
-                gpsimd_product(0, GPSIMD_FIRST)
-                weave_h(h_bank, token, GPSIMD_FIRST, QUARTER)
-                gpsimd_product(GPSIMD_FIRST, QUARTER)
-            if share < QUARTER:
-                nc.vector.tensor_tensor(
-                    z_grouped[c][:, (first + share) * PACK : (first + QUARTER) * PACK].rearrange("p (n i t) -> p n t i", i=2, t=PACK),
-                    h_bank[:, :, share:].rearrange("p t (n i) -> p n t i", i=2),
-                    rin_picked[:, :, token + share : token + QUARTER].rearrange("p t (n i) -> p n t i", i=2),
-                    MULT,
-                )
+                product(nc, h_bank[:, t, :], w1_codes, w1_scales, t, x_picked[:, tokens], xs_picked[:, tokens])
+            nc.vector.tensor_tensor(
+                z_grouped[c][:, first * PACK : (first + QUARTER) * PACK].rearrange("p (n i t) -> p n t i", i=2, t=PACK),
+                h_bank[:].rearrange("p t (n i) -> p n t i", i=2),
+                rin_picked[c][:, :, first : first + QUARTER].rearrange("p t (n i) -> p n t i", i=2),
+                MULT,
+            )
 
         def quantize_z(c):
-            z_codes[c] = late.tile([P, HALF], U32, name=f"z_codes{c}", offset=0 if c else 8192, align_bytes=64)
-            quantize(nc, z_codes[c][:], z_scales[c][:], z_grouped[c][:])
+            cols = slice(c * HALF, (c + 1) * HALF)
+            quantize(nc, z_codes[:, cols], z_scales[:, cols], z_grouped[c][:])
 
-        w2_codes = keep.tile([P, N], U32, name="w2_codes", align_bytes=64)
-        w2_scales = keep.tile([P, N], U8, name="w2_scales", align_bytes=64)
-
-        def prepare_w2_pair(u):
-            pair = late.tile([P, 2 * N], BF16, name=f"w2_pair{u}", offset=2048 * u, align_bytes=64)
-            cast_weight_pair(nc, w2_raw, pair[:], u)
-            planes = 1 + u
-            for t in range(0, 2, planes):
-                cols = slice((2 * u + t) * P, (2 * u + t + planes) * P)
-                quantize(nc, w2_codes[:, cols], w2_scales[:, cols], pair[:, t * N : (t + planes) * N])
-
-        out_rows = out.rearrange("(p t) s -> t p s", t=PACK)
-
-        def output_tile(t, c, width):
-            o_bank = psum.tile([P, HALF], F32, name=f"o_bank{t}{c}", tag=f"o_bank{(2 * t + c) % 4}")
-            product(nc, o_bank[:], w2_codes, w2_scales, t, z_codes[c][:], z_scales[c][:])
-            result = keep.tile([P, HALF], F32, name=f"result{t}{c}")
-            if t == 0:
-                nc.vector.tensor_tensor(result[:], o_bank[:], so_picked[:, c * HALF : (c + 1) * HALF], MULT)
-                nc.sync.dma_start(out_rows[t][:, c * HALF : (c + 1) * HALF], result[:])
-                return
-            o_sb = keep.tile([P, HALF], F32, name=f"o_sb{t}{c}")
-            nc.scalar.copy(out=o_sb[:], in_=o_bank[:])
-            for first in range(0, HALF, width):
-                token = c * HALF + first
-                nc.vector.tensor_tensor(result[:, first : first + width], so_sb[t][:].indirect(entries(mem_sb, token, width)), o_sb[:, first : first + width], MULT)
-                nc.sync.dma_start(out_rows[t][:, token : token + width], result[:, first : first + width])
-
-        for q in range(S // QUARTER):
+        for q in range(3):
             hidden_quarter(q)
         quantize_z(0)
-        prepare_w2_pair(0)
+        hidden_quarter(3)
+
+        w2_grouped = [keep.tile([P, 2 * N], BF16, name=f"w2_grouped{u}", align_bytes=64) for u in range(2)]
+        w2_codes = keep.tile([P, N], U32, name="w2_codes", align_bytes=64)
+        w2_scales = keep.tile([P, N], U8, name="w2_scales", align_bytes=64)
+        cast_weight(w2_raw, w2_grouped)
         quantize_z(1)
-        prepare_w2_pair(1)
-        for t in range(PACK):
+        for u in range(2):
+            quantize_pair(w2_codes, w2_scales, w2_grouped, u)
+
+        fetch_on_scalar(so_picked[1][:, :HALF], so_sb[1], 0, HALF)
+        fetch_on_vector(so_picked[1][:, HALF:], so_sb[1], HALF, HALF)
+        for t in (2, 3):
             for c in range(2):
-                output_tile(t, c, QUARTER if (t, c) == (PACK - 1, 1) else HALF)
+                fetch_on_scalar(so_picked[t][:, c * HALF : (c + 1) * HALF], so_sb[t], c * HALF, HALF)
+
+        out_rows = out.rearrange("(p t) s -> t p s", t=PACK)
+        for t in range(PACK):
+            o_bank = psum.tile([P, S], F32, name=f"o_bank{t}")
+            product(nc, o_bank[:], w2_codes, w2_scales, t, z_codes[:], z_scales[:])
+            result = keep.tile([P, S], F32, name=f"result{t}")
+            width = HALF if t == PACK - 1 else S
+            for first in range(0, S, width):
+                tokens = slice(first, first + width)
+                nc.vector.tensor_tensor(result[:, tokens], o_bank[:, tokens], so_picked[t][:, tokens], MULT)
+                nc.sync.dma_start(out_rows[t][:, tokens], result[:, tokens])

@@ -22,6 +22,9 @@ QUARTER = 128
 LIST_ROWS = 16
 SCALE_ROWS = 16
 PLANE_BYTES = 4 * U
+SCALAR_COLUMNS = 104
+HELD = 8 * PLANE_BYTES
+PICKED = 14 * PLANE_BYTES
 
 
 def plane_rows(table, t):
@@ -70,7 +73,9 @@ def tile_picked_bens8_none_p_kernel(tc, x_words, x_scales, w1, rin, w2, so, offs
         def fetch_on_vector(target, window, first, count):
             nc.vector.tensor_copy(target, window[:].indirect(entries(mem_sb, first, count)))
 
-        rin_sb = [keep.tile([P, U], F32, name=f"rin_sb{t}", tag=f"slot{t}") for t in range(PACK - 1)]
+        rin_raw = keep.tile([P, 3 * U], F32, name="rin_raw")
+        rin_sb = [late.tile([P, U], F32, name="rin_sb0", offset=HELD)]
+        rin_sb.extend(keep.tile([P, U], F32, name=f"rin_sb{t}") for t in (1, 2))
         xs_sb = keep.tile([P, T], U8, name="xs_sb", tag="slot3")
         w1_raw = late.tile([P, PACK, H], F32, name="w1_raw", offset=0)
         xw_sb = keep.tile([P, T], I32, name="xw_sb")
@@ -79,11 +84,9 @@ def tile_picked_bens8_none_p_kernel(tc, x_words, x_scales, w1, rin, w2, so, offs
         nc.vector.memset(xs_sb[:first_row, :].bitcast(I32), 0)
         nc.scalar.dma_start(xs_sb[first_row:, :].bitcast(I32), x_scales[0].bitcast(I32))
         nc.sync.dma_start(offs_sb[:], offs)
-        nc.sync.dma_start(rin_sb[0][:], plane_rows(rin, 0))
+        nc.sync.dma_start(rin_raw[:], rin.rearrange("(p t) u -> p (t u)", t=PACK)[:, : 3 * U])
         nc.sync.dma_start(mem_sb[:], mem)
-        nc.sync.dma_start(rin_sb[1][:], plane_rows(rin, 1))
         nc.sync.dma_start(w1_raw[:], w1.rearrange("(p j) c -> p j c", j=PACK))
-        nc.sync.dma_start(rin_sb[2][:], plane_rows(rin, 2))
         nc.sync.dma_start(xw_sb[:], x_words[0].rearrange("p n r -> p (n r)").bitcast(I32))
 
         xs_gathered = keep.tile([P, S], U8, name="xs_gathered", align_bytes=64)
@@ -95,21 +98,29 @@ def tile_picked_bens8_none_p_kernel(tc, x_words, x_scales, w1, rin, w2, so, offs
         rin_sb.append(keep.tile([P, U], F32, name="rin_sb3", tag="slot3"))
         nc.sync.dma_start(rin_sb[3][:], plane_rows(rin, 3))
 
-        rin_picked = [keep.tile([P, PACK, HALF], F32, name=f"rin_picked{c}") for c in range(2)]
-        for t in range(2):
-            for c in range(2):
-                fetch_on_vector(rin_picked[c][:, t, :], rin_sb[t], c * HALF, HALF)
+        pieces = ((0, QUARTER), (QUARTER, QUARTER), (HALF, HALF))
+        rin_picked = {first: keep.tile([P, PACK, count], F32, name=f"rin_picked{first}") for first, count in pieces}
 
-        so_sb = [keep.tile([P, U], F32, name="so_sb0", tag="slot0")]
-        nc.sync.dma_start(so_sb[0][:], plane_rows(so, 0))
-        w2_raw = keep.tile([P, PACK, N], F32, name="w2_raw", tag="slot1")
+        def fetch_rin(fetch, t):
+            for first, count in pieces:
+                fetch(rin_picked[first][:, t, :], rin_sb[t], first, count)
+
+        nc.vector.tensor_copy(rin_sb[0][:], rin_raw[:, :U])
+        nc.scalar.copy(out=rin_sb[1][:], in_=rin_raw[:, U : 2 * U])
+        nc.scalar.copy(out=rin_sb[2][:], in_=rin_raw[:, 2 * U :])
+        fetch_rin(fetch_on_vector, 0)
+        fetch_rin(fetch_on_scalar, 1)
+
+        so_sb = [late.tile([P, 2 * U], F32, name="so_sb0", offset=HELD - 3 * PLANE_BYTES // 2)]
+        nc.sync.dma_start(so_sb[0][:, :U], plane_rows(so, 0))
+        w2_raw = late.tile([P, PACK, N], F32, name="w2_raw", offset=HELD + PLANE_BYTES // 2)
         nc.sync.dma_start(w2_raw[:], w2.rearrange("(p j) c -> p j c", j=PACK))
 
         def cast_weight(raw, grouped):
             target, source = weight_pair_views(raw, grouped[0][:], 0)
             nc.vector.tensor_copy(target, source)
             target, source = weight_pair_views(raw, grouped[1][:], 1)
-            nc.scalar.copy(out=target, in_=source)
+            nc.vector.tensor_copy(target, source)
 
         def quantize_pair(codes, scales, grouped, u):
             cols = slice(2 * u * P, 2 * (u + 1) * P)
@@ -122,70 +133,85 @@ def tile_picked_bens8_none_p_kernel(tc, x_words, x_scales, w1, rin, w2, so, offs
         for u in range(2):
             quantize_pair(w1_codes, w1_scales, w1_grouped, u)
 
-        for c in range(2):
-            fetch_on_scalar(rin_picked[c][:, 2, :], rin_sb[2], c * HALF, HALF)
+        fetch_rin(fetch_on_scalar, 2)
 
         for t in range(1, PACK):
-            so_sb.append(late.tile([P, U], F32, name=f"so_sb{t}", offset=(t - 1) * PLANE_BYTES))
-            nc.sync.dma_start(so_sb[t][:], plane_rows(so, t))
+            width = U if t == PACK - 1 else 2 * U
+            so_sb.append(late.tile([P, width], F32, name=f"so_sb{t}", offset=(0, 3, 2)[t - 1] * PLANE_BYTES))
+            nc.sync.dma_start(so_sb[t][:, :U], plane_rows(so, t))
 
-        x_picked = keep.tile([P, S], U32, name="x_picked", align_bytes=64)
-        for first, count in ((0, QUARTER), (QUARTER, QUARTER), (HALF, HALF)):
+        x_picked = late.tile([P, S], U32, name="x_picked", offset=PICKED, align_bytes=64)
+        for first, count in pieces:
             nc.vector.tensor_copy(x_picked[:, first : first + count], xw_sb[:].bitcast(U32).indirect(entries(offs_sb, first, count)))
-        for c in range(2):
-            fetch_on_scalar(rin_picked[c][:, 3, :], rin_sb[3], c * HALF, HALF)
+        fetch_rin(fetch_on_scalar, 3)
 
         so_picked = [keep.tile([P, S], F32, name=f"so_picked{t}") for t in range(PACK)]
-        for c in range(2):
-            fetch_on_scalar(so_picked[0][:, c * HALF : (c + 1) * HALF], so_sb[0], c * HALF, HALF)
+        fetch_on_scalar(so_picked[0][:], so_sb[0], 0, S)
 
         z_grouped = [keep.tile([P, PACK * HALF], BF16, name=f"z_grouped{c}", align_bytes=64) for c in range(2)]
-        z_codes = keep.tile([P, S], U32, name="z_codes", align_bytes=64)
-        z_scales = keep.tile([P, S], U8, name="z_scales", align_bytes=64)
+        z_codes = {}
+        z_scales = [keep.tile([P, HALF], U8, name=f"z_scales{c}", align_bytes=64) for c in range(2)]
 
         def hidden_quarter(q):
             c, first = divmod(q * QUARTER, HALF)
             tokens = slice(q * QUARTER, (q + 1) * QUARTER)
+            piece = min(q * QUARTER, HALF)
             h_bank = psum.tile([P, PACK, QUARTER], F32, name=f"h_bank{q}")
             for t in range(PACK):
                 product(nc, h_bank[:, t, :], w1_codes, w1_scales, t, x_picked[:, tokens], xs_picked[:, tokens])
             nc.vector.tensor_tensor(
                 z_grouped[c][:, first * PACK : (first + QUARTER) * PACK].rearrange("p (n i t) -> p n t i", i=2, t=PACK),
                 h_bank[:].rearrange("p t (n i) -> p n t i", i=2),
-                rin_picked[c][:, :, first : first + QUARTER].rearrange("p t (n i) -> p n t i", i=2),
+                rin_picked[piece][:, :, tokens.start - piece : tokens.stop - piece].rearrange("p t (n i) -> p n t i", i=2),
                 MULT,
             )
 
         def quantize_z(c):
-            cols = slice(c * HALF, (c + 1) * HALF)
-            quantize(nc, z_codes[:, cols], z_scales[:, cols], z_grouped[c][:])
+            if c == 0:
+                z_codes[c] = keep.tile([P, HALF], U32, name="z_codes0", align_bytes=64)
+            else:
+                z_codes[c] = late.tile([P, HALF], U32, name="z_codes1", offset=HELD + PLANE_BYTES, align_bytes=64)
+            quantize(nc, z_codes[c][:], z_scales[c][:], z_grouped[c][:])
 
         for q in range(3):
             hidden_quarter(q)
         quantize_z(0)
         hidden_quarter(3)
 
-        w2_grouped = [keep.tile([P, 2 * N], BF16, name=f"w2_grouped{u}", align_bytes=64) for u in range(2)]
+        w2_grouped = [late.tile([P, 2 * N], BF16, name=f"w2_grouped{u}", offset=PICKED + (2 * u - 1) * PLANE_BYTES // 2, align_bytes=64) for u in range(2)]
         w2_codes = keep.tile([P, N], U32, name="w2_codes", align_bytes=64)
         w2_scales = keep.tile([P, N], U8, name="w2_scales", align_bytes=64)
-        cast_weight(w2_raw, w2_grouped)
+        target, source = weight_pair_views(w2_raw, w2_grouped[0][:], 0)
+        nc.vector.tensor_copy(target, source)
+        target, source = weight_pair_views(w2_raw, w2_grouped[1][:], 1)
+        nc.scalar.copy(out=target[:, :SCALAR_COLUMNS], in_=source[:, :SCALAR_COLUMNS])
+        nc.vector.tensor_copy(target[:, SCALAR_COLUMNS:], source[:, SCALAR_COLUMNS:])
+        quantize_pair(w2_codes, w2_scales, w2_grouped, 0)
         quantize_z(1)
-        for u in range(2):
-            quantize_pair(w2_codes, w2_scales, w2_grouped, u)
 
-        fetch_on_scalar(so_picked[1][:, :HALF], so_sb[1], 0, HALF)
-        fetch_on_vector(so_picked[1][:, HALF:], so_sb[1], HALF, HALF)
-        for t in (2, 3):
-            for c in range(2):
-                fetch_on_scalar(so_picked[t][:, c * HALF : (c + 1) * HALF], so_sb[t], c * HALF, HALF)
+        for t in (1, 2):
+            fetch_on_scalar(so_picked[t][:], so_sb[t], 0, S)
+        last_pieces = ((0, HALF), (HALF, HALF))
+        for first, count in last_pieces:
+            fetch_on_scalar(so_picked[3][:, first : first + count], so_sb[3], first, count)
 
         out_rows = out.rearrange("(p t) s -> t p s", t=PACK)
-        for t in range(PACK):
+
+        def output_piece(t, o_bank, bank_first, first, count):
+            tokens = slice(first, first + count)
+            result = keep.tile([P, count], F32, name=f"result{t}_{first}")
+            nc.vector.tensor_tensor(result[:], o_bank[:, first - bank_first : first - bank_first + count], so_picked[t][:, tokens], MULT)
+            nc.sync.dma_start(out_rows[t][:, tokens], result[:])
+
+        for c in range(2):
+            o_half = psum.tile([P, HALF], F32, name=f"o_half{c}", tag=f"h_bank{c}")
+            product(nc, o_half[:], w2_codes, w2_scales, 0, z_codes[c][:], z_scales[c][:])
+            output_piece(0, o_half, c * HALF, c * HALF, HALF)
+            if c == 0:
+                quantize_pair(w2_codes, w2_scales, w2_grouped, 1)
+        for t in range(1, PACK):
             o_bank = psum.tile([P, S], F32, name=f"o_bank{t}")
-            product(nc, o_bank[:], w2_codes, w2_scales, t, z_codes[:], z_scales[:])
-            result = keep.tile([P, S], F32, name=f"result{t}")
-            width = HALF if t == PACK - 1 else S
-            for first in range(0, S, width):
-                tokens = slice(first, first + width)
-                nc.vector.tensor_tensor(result[:, tokens], o_bank[:, tokens], so_picked[t][:, tokens], MULT)
-                nc.sync.dma_start(out_rows[t][:, tokens], result[:, tokens])
+            for c in range(2):
+                product(nc, o_bank[:, c * HALF : (c + 1) * HALF], w2_codes, w2_scales, t, z_codes[c][:], z_scales[c][:])
+            for first, count in last_pieces if t == PACK - 1 else ((0, S),):
+                output_piece(t, o_bank, 0, first, count)

@@ -22,7 +22,7 @@ QUARTER = 128
 LIST_ROWS = 16
 SCALE_ROWS = 16
 PLANE_BYTES = 4 * U
-SCALAR_COLUMNS = 104
+SCALAR_COLUMNS = 56
 HELD = 8 * PLANE_BYTES
 PICKED = 14 * PLANE_BYTES
 
@@ -191,7 +191,7 @@ def tile_picked_bens8_none_p_kernel(tc, x_words, x_scales, w1, rin, w2, so, offs
 
         for t in (1, 2):
             fetch_on_scalar(so_picked[t][:], so_sb[t], 0, S)
-        last_pieces = ((0, HALF), (HALF, HALF))
+        last_pieces = ((0, HALF), (HALF, QUARTER), (HALF + QUARTER, QUARTER))
         for first, count in last_pieces:
             fetch_on_scalar(so_picked[3][:, first : first + count], so_sb[3], first, count)
 
@@ -213,5 +213,10 @@ def tile_picked_bens8_none_p_kernel(tc, x_words, x_scales, w1, rin, w2, so, offs
             o_bank = psum.tile([P, S], F32, name=f"o_bank{t}")
             for c in range(2):
                 product(nc, o_bank[:, c * HALF : (c + 1) * HALF], w2_codes, w2_scales, t, z_codes[c][:], z_scales[c][:])
-            for first, count in last_pieces if t == PACK - 1 else ((0, S),):
-                output_piece(t, o_bank, 0, first, count)
+            if t < PACK - 1:
+                output_piece(t, o_bank, 0, 0, S)
+        output_piece(t, o_bank, 0, 0, HALF)
+        last = keep.tile([P, HALF], F32, name="last")
+        for first, count in last_pieces[1:]:
+            nc.vector.tensor_tensor(last[:, first - HALF : first - HALF + count], o_bank[:, first : first + count], so_picked[t][:, first : first + count], MULT)
+        nc.sync.dma_start(out_rows[t][:, HALF:], last[:])

@@ -22,13 +22,22 @@ QUARTER = 128
 LIST_ROWS = 16
 SCALE_ROWS = 16
 PLANE_BYTES = 4 * U
-SCALAR_COLUMNS = 56
-HELD = 8 * PLANE_BYTES
-PICKED = 14 * PLANE_BYTES
+SCALAR_COLUMNS_W1 = 32
+SCALAR_COLUMNS = 72
+W1_AT = 2 * PLANE_BYTES
+PICKED = W1_AT + PLANE_BYTES // 4
+HELD = 10 * PLANE_BYTES
 
 
 def plane_rows(table, t):
     return table.rearrange("(p t) u -> t p u", t=PACK)[t]
+
+
+def cast_weight(nc, raw, grouped, scalar_columns):
+    target = grouped[:].rearrange("p (t m j) -> p m j t", t=PACK, j=PACK)
+    source = raw[:].rearrange("p j (m t) -> p m j t", t=PACK)
+    nc.vector.tensor_copy(target[:, scalar_columns:], source[:, scalar_columns:])
+    nc.scalar.copy(out=target[:, :scalar_columns], in_=source[:, :scalar_columns])
 
 
 def weight_pair_views(raw, grouped, u):
@@ -75,9 +84,9 @@ def tile_picked_bens8_none_p_kernel(tc, x_words, x_scales, w1, rin, w2, so, offs
 
         rin_raw = keep.tile([P, 3 * U], F32, name="rin_raw")
         rin_sb = [late.tile([P, U], F32, name="rin_sb0", offset=HELD)]
-        rin_sb.extend(keep.tile([P, U], F32, name=f"rin_sb{t}") for t in (1, 2))
+        rin_sb.append(keep.tile([P, U], F32, name="rin_sb1"))
         xs_sb = keep.tile([P, T], U8, name="xs_sb", tag="slot3")
-        w1_raw = late.tile([P, PACK, H], F32, name="w1_raw", offset=0)
+        w1_raw = late.tile([P, PACK, H], F32, name="w1_raw", offset=W1_AT)
         xw_sb = keep.tile([P, T], I32, name="xw_sb")
 
         first_row = P - SCALE_ROWS
@@ -95,8 +104,8 @@ def tile_picked_bens8_none_p_kernel(tc, x_words, x_scales, w1, rin, w2, so, offs
         nc.vector.memset(xs_picked[:].bitcast(I32), 0)
         for r in range(4):
             nc.sync.dma_start(xs_picked[r:P:32, :].bitcast(I32), xs_gathered[first_row + r : P : 4, :].bitcast(I32))
-        rin_sb.append(keep.tile([P, U], F32, name="rin_sb3", tag="slot3"))
-        nc.sync.dma_start(rin_sb[3][:], plane_rows(rin, 3))
+        rin_last = keep.tile([P, U], F32, name="rin_last", tag="slot3")
+        nc.sync.dma_start(rin_last[:], plane_rows(rin, 3))
 
         pieces = ((0, QUARTER), (QUARTER, QUARTER), (HALF, HALF))
         rin_picked = {first: keep.tile([P, PACK, count], F32, name=f"rin_picked{first}") for first, count in pieces}
@@ -107,7 +116,6 @@ def tile_picked_bens8_none_p_kernel(tc, x_words, x_scales, w1, rin, w2, so, offs
 
         nc.vector.tensor_copy(rin_sb[0][:], rin_raw[:, :U])
         nc.scalar.copy(out=rin_sb[1][:], in_=rin_raw[:, U : 2 * U])
-        nc.scalar.copy(out=rin_sb[2][:], in_=rin_raw[:, 2 * U :])
         fetch_rin(fetch_on_vector, 0)
         fetch_rin(fetch_on_scalar, 1)
 
@@ -116,28 +124,23 @@ def tile_picked_bens8_none_p_kernel(tc, x_words, x_scales, w1, rin, w2, so, offs
         w2_raw = late.tile([P, PACK, N], F32, name="w2_raw", offset=HELD + PLANE_BYTES // 2)
         nc.sync.dma_start(w2_raw[:], w2.rearrange("(p j) c -> p j c", j=PACK))
 
-        def cast_weight(raw, grouped):
-            target, source = weight_pair_views(raw, grouped[0][:], 0)
-            nc.vector.tensor_copy(target, source)
-            target, source = weight_pair_views(raw, grouped[1][:], 1)
-            nc.vector.tensor_copy(target, source)
-
         def quantize_pair(codes, scales, grouped, u):
             cols = slice(2 * u * P, 2 * (u + 1) * P)
             quantize(nc, codes[:, cols], scales[:, cols], grouped[u][:])
 
-        w1_grouped = [keep.tile([P, 2 * H], BF16, name=f"w1_grouped{u}", align_bytes=64) for u in range(2)]
+        w1_grouped = keep.tile([P, PACK * H], BF16, name="w1_grouped", align_bytes=64)
         w1_codes = keep.tile([P, H], U32, name="w1_codes", align_bytes=64)
         w1_scales = keep.tile([P, H], U8, name="w1_scales", align_bytes=64)
-        cast_weight(w1_raw, w1_grouped)
-        for u in range(2):
-            quantize_pair(w1_codes, w1_scales, w1_grouped, u)
-
+        cast_weight(nc, w1_raw, w1_grouped, SCALAR_COLUMNS_W1)
+        rin_sb.append(late.tile([P, U], F32, name="rin_sb2", offset=PICKED + PLANE_BYTES))
+        rin_sb.append(rin_last)
+        nc.vector.tensor_copy(rin_sb[2][:], rin_raw[:, 2 * U :])
+        quantize(nc, w1_codes[:], w1_scales[:], w1_grouped[:])
         fetch_rin(fetch_on_scalar, 2)
 
         for t in range(1, PACK):
             width = U if t == PACK - 1 else 2 * U
-            so_sb.append(late.tile([P, width], F32, name=f"so_sb{t}", offset=(0, 3, 2)[t - 1] * PLANE_BYTES))
+            so_sb.append(late.tile([P, width], F32, name=f"so_sb{t}", offset=PICKED + (-2, 3, 2)[t - 1] * PLANE_BYTES))
             nc.sync.dma_start(so_sb[t][:, :U], plane_rows(so, t))
 
         x_picked = late.tile([P, S], U32, name="x_picked", offset=PICKED, align_bytes=64)
@@ -178,7 +181,7 @@ def tile_picked_bens8_none_p_kernel(tc, x_words, x_scales, w1, rin, w2, so, offs
         quantize_z(0)
         hidden_quarter(3)
 
-        w2_grouped = [late.tile([P, 2 * N], BF16, name=f"w2_grouped{u}", offset=PICKED + (2 * u - 1) * PLANE_BYTES // 2, align_bytes=64) for u in range(2)]
+        w2_grouped = [keep.tile([P, 2 * N], BF16, name=f"w2_grouped{u}", align_bytes=64) for u in range(2)]
         w2_codes = keep.tile([P, N], U32, name="w2_codes", align_bytes=64)
         w2_scales = keep.tile([P, N], U8, name="w2_scales", align_bytes=64)
         target, source = weight_pair_views(w2_raw, w2_grouped[0][:], 0)

@@ -22,7 +22,7 @@ QUARTER = 128
 LIST_ROWS = 16
 SCALE_ROWS = 16
 PLANE_BYTES = 4 * U
-SCALAR_COLUMNS_W1 = 32
+SCALAR_COLUMNS_W1 = 16
 SCALAR_COLUMNS = 72
 W1_AT = 2 * PLANE_BYTES
 PICKED = W1_AT + PLANE_BYTES // 4
@@ -82,19 +82,20 @@ def tile_picked_bens8_none_p_kernel(tc, x_words, x_scales, w1, rin, w2, so, offs
         def fetch_on_vector(target, window, first, count):
             nc.vector.tensor_copy(target, window[:].indirect(entries(mem_sb, first, count)))
 
-        rin_raw = keep.tile([P, 3 * U], F32, name="rin_raw")
-        rin_sb = [late.tile([P, U], F32, name="rin_sb0", offset=HELD)]
-        rin_sb.append(keep.tile([P, U], F32, name="rin_sb1"))
+        rin_sb = [keep.tile([P, U], F32, name=f"rin_sb{t}") for t in range(2)]
+        rin_sb.append(late.tile([P, U], F32, name="rin_sb2", offset=HELD))
         xs_sb = keep.tile([P, T], U8, name="xs_sb", tag="slot3")
         w1_raw = late.tile([P, PACK, H], F32, name="w1_raw", offset=W1_AT)
         xw_sb = keep.tile([P, T], I32, name="xw_sb")
 
-        first_row = P - SCALE_ROWS
-        nc.vector.memset(xs_sb[:first_row, :].bitcast(I32), 0)
-        nc.scalar.dma_start(xs_sb[first_row:, :].bitcast(I32), x_scales[0].bitcast(I32))
-        nc.sync.dma_start(offs_sb[:], offs)
-        nc.sync.dma_start(rin_raw[:], rin.rearrange("(p t) u -> p (t u)", t=PACK)[:, : 3 * U])
+        first_row = 32
+        nc.vector.memset(xs_sb[:].bitcast(I32), 0)
+        nc.sync.dma_start(rin_sb[0][:], plane_rows(rin, 0))
         nc.sync.dma_start(mem_sb[:], mem)
+        nc.sync.dma_start(rin_sb[1][:], plane_rows(rin, 1))
+        nc.sync.dma_start(offs_sb[:], offs)
+        nc.sync.dma_start(xs_sb[first_row : first_row + 4 * SCALE_ROWS : 4, :].bitcast(I32), x_scales[0].bitcast(I32))
+        nc.sync.dma_start(rin_sb[2][:], plane_rows(rin, 2))
         nc.sync.dma_start(w1_raw[:], w1.rearrange("(p j) c -> p j c", j=PACK))
         nc.sync.dma_start(xw_sb[:], x_words[0].rearrange("p n r -> p (n r)").bitcast(I32))
 
@@ -103,9 +104,9 @@ def tile_picked_bens8_none_p_kernel(tc, x_words, x_scales, w1, rin, w2, so, offs
         xs_picked = keep.tile([P, S], U8, name="xs_picked", align_bytes=64)
         nc.vector.memset(xs_picked[:].bitcast(I32), 0)
         for r in range(4):
-            nc.sync.dma_start(xs_picked[r:P:32, :].bitcast(I32), xs_gathered[first_row + r : P : 4, :].bitcast(I32))
-        rin_last = keep.tile([P, U], F32, name="rin_last", tag="slot3")
-        nc.sync.dma_start(rin_last[:], plane_rows(rin, 3))
+            nc.sync.dma_start(xs_picked[r:P:32, :].bitcast(I32), xs_gathered[first_row + 4 * r : first_row + 4 * SCALE_ROWS : 16, :].bitcast(I32))
+        rin_sb.append(keep.tile([P, U], F32, name="rin_sb3", tag="slot3"))
+        nc.sync.dma_start(rin_sb[3][:], plane_rows(rin, 3))
 
         pieces = ((0, QUARTER), (QUARTER, QUARTER), (HALF, HALF))
         rin_picked = {first: keep.tile([P, PACK, count], F32, name=f"rin_picked{first}") for first, count in pieces}
@@ -114,10 +115,9 @@ def tile_picked_bens8_none_p_kernel(tc, x_words, x_scales, w1, rin, w2, so, offs
             for first, count in pieces:
                 fetch(rin_picked[first][:, t, :], rin_sb[t], first, count)
 
-        nc.vector.tensor_copy(rin_sb[0][:], rin_raw[:, :U])
-        nc.scalar.copy(out=rin_sb[1][:], in_=rin_raw[:, U : 2 * U])
-        fetch_rin(fetch_on_vector, 0)
+        fetch_rin(fetch_on_scalar, 0)
         fetch_rin(fetch_on_scalar, 1)
+        fetch_rin(fetch_on_vector, 2)
 
         so_sb = [late.tile([P, 2 * U], F32, name="so_sb0", offset=HELD - 3 * PLANE_BYTES // 2)]
         nc.sync.dma_start(so_sb[0][:, :U], plane_rows(so, 0))
@@ -132,11 +132,7 @@ def tile_picked_bens8_none_p_kernel(tc, x_words, x_scales, w1, rin, w2, so, offs
         w1_codes = keep.tile([P, H], U32, name="w1_codes", align_bytes=64)
         w1_scales = keep.tile([P, H], U8, name="w1_scales", align_bytes=64)
         cast_weight(nc, w1_raw, w1_grouped, SCALAR_COLUMNS_W1)
-        rin_sb.append(late.tile([P, U], F32, name="rin_sb2", offset=PICKED + PLANE_BYTES))
-        rin_sb.append(rin_last)
-        nc.vector.tensor_copy(rin_sb[2][:], rin_raw[:, 2 * U :])
         quantize(nc, w1_codes[:], w1_scales[:], w1_grouped[:])
-        fetch_rin(fetch_on_scalar, 2)
 
         for t in range(1, PACK):
             width = U if t == PACK - 1 else 2 * U

@@ -22,7 +22,6 @@ QUARTER = 128
 LIST_ROWS = 16
 SCALE_ROWS = 16
 PLANE_BYTES = 4 * U
-SCALAR_COLUMNS_W1 = 16
 SCALAR_COLUMNS = 72
 W1_AT = 2 * PLANE_BYTES
 PICKED = W1_AT + PLANE_BYTES // 4
@@ -33,11 +32,10 @@ def plane_rows(table, t):
     return table.rearrange("(p t) u -> t p u", t=PACK)[t]
 
 
-def cast_weight(nc, raw, grouped, scalar_columns):
+def cast_weight(nc, raw, grouped):
     target = grouped[:].rearrange("p (t m j) -> p m j t", t=PACK, j=PACK)
     source = raw[:].rearrange("p j (m t) -> p m j t", t=PACK)
-    nc.vector.tensor_copy(target[:, scalar_columns:], source[:, scalar_columns:])
-    nc.scalar.copy(out=target[:, :scalar_columns], in_=source[:, :scalar_columns])
+    nc.vector.tensor_copy(target, source)
 
 
 def weight_pair_views(raw, grouped, u):
@@ -82,21 +80,21 @@ def tile_picked_bens8_none_p_kernel(tc, x_words, x_scales, w1, rin, w2, so, offs
         def fetch_on_vector(target, window, first, count):
             nc.vector.tensor_copy(target, window[:].indirect(entries(mem_sb, first, count)))
 
-        rin_sb = [keep.tile([P, U], F32, name=f"rin_sb{t}") for t in range(2)]
-        rin_sb.append(late.tile([P, U], F32, name="rin_sb2", offset=HELD))
-        xs_sb = keep.tile([P, T], U8, name="xs_sb", tag="slot3")
+        rin_sb = [keep.tile([P, 2 * U], F32, name="rin_sb0")]
+        rin_sb.append(late.tile([P, U], F32, name="rin_sb1", offset=HELD + 3 * PLANE_BYTES))
+        rin_sb.append(keep.tile([P, U], F32, name="rin_sb2"))
+        xs_sb = late.tile([P, T], U8, name="xs_sb", offset=HELD)
         w1_raw = late.tile([P, PACK, H], F32, name="w1_raw", offset=W1_AT)
         xw_sb = keep.tile([P, T], I32, name="xw_sb")
 
         first_row = 32
         nc.vector.memset(xs_sb[:].bitcast(I32), 0)
-        nc.sync.dma_start(rin_sb[0][:], plane_rows(rin, 0))
+        nc.sync.dma_start(rin_sb[0][:], rin.rearrange("(p t) u -> p (t u)", t=PACK)[:, : 2 * U])
         nc.sync.dma_start(mem_sb[:], mem)
-        nc.sync.dma_start(rin_sb[1][:], plane_rows(rin, 1))
         nc.sync.dma_start(offs_sb[:], offs)
         nc.sync.dma_start(xs_sb[first_row : first_row + 4 * SCALE_ROWS : 4, :].bitcast(I32), x_scales[0].bitcast(I32))
-        nc.sync.dma_start(rin_sb[2][:], plane_rows(rin, 2))
         nc.sync.dma_start(w1_raw[:], w1.rearrange("(p j) c -> p j c", j=PACK))
+        nc.sync.dma_start(rin_sb[2][:], plane_rows(rin, 2))
         nc.sync.dma_start(xw_sb[:], x_words[0].rearrange("p n r -> p (n r)").bitcast(I32))
 
         xs_gathered = keep.tile([P, S], U8, name="xs_gathered", align_bytes=64)
@@ -105,23 +103,26 @@ def tile_picked_bens8_none_p_kernel(tc, x_words, x_scales, w1, rin, w2, so, offs
         nc.vector.memset(xs_picked[:].bitcast(I32), 0)
         for r in range(4):
             nc.sync.dma_start(xs_picked[r:P:32, :].bitcast(I32), xs_gathered[first_row + 4 * r : first_row + 4 * SCALE_ROWS : 16, :].bitcast(I32))
-        rin_sb.append(keep.tile([P, U], F32, name="rin_sb3", tag="slot3"))
+        rin_sb.append(late.tile([P, U], F32, name="rin_sb3", offset=HELD + PLANE_BYTES // 2))
         nc.sync.dma_start(rin_sb[3][:], plane_rows(rin, 3))
 
         pieces = ((0, QUARTER), (QUARTER, QUARTER), (HALF, HALF))
-        rin_picked = {first: keep.tile([P, PACK, count], F32, name=f"rin_picked{first}") for first, count in pieces}
+        halves = ((0, HALF), (HALF, HALF))
+        rin_picked = [keep.tile([P, PACK, HALF], F32, name=f"rin_picked{c}") for c in range(2)]
 
-        def fetch_rin(fetch, t):
-            for first, count in pieces:
-                fetch(rin_picked[first][:, t, :], rin_sb[t], first, count)
+        def fetch_rin(fetch, t, cuts):
+            for first, count in cuts:
+                c, column = divmod(first, HALF)
+                fetch(rin_picked[c][:, t, column : column + count], rin_sb[t], first, count)
 
-        fetch_rin(fetch_on_scalar, 0)
-        fetch_rin(fetch_on_scalar, 1)
-        fetch_rin(fetch_on_vector, 2)
+        nc.scalar.copy(out=rin_sb[1][:], in_=rin_sb[0][:, U:])
+        fetch_rin(fetch_on_vector, 0, halves)
+        fetch_rin(fetch_on_scalar, 1, halves)
+        fetch_rin(fetch_on_scalar, 2, halves)
 
         so_sb = [late.tile([P, 2 * U], F32, name="so_sb0", offset=HELD - 3 * PLANE_BYTES // 2)]
         nc.sync.dma_start(so_sb[0][:, :U], plane_rows(so, 0))
-        w2_raw = late.tile([P, PACK, N], F32, name="w2_raw", offset=HELD + PLANE_BYTES // 2)
+        w2_raw = late.tile([P, PACK, N], F32, name="w2_raw", offset=HELD + 3 * PLANE_BYTES)
         nc.sync.dma_start(w2_raw[:], w2.rearrange("(p j) c -> p j c", j=PACK))
 
         def quantize_pair(codes, scales, grouped, u):
@@ -131,7 +132,7 @@ def tile_picked_bens8_none_p_kernel(tc, x_words, x_scales, w1, rin, w2, so, offs
         w1_grouped = keep.tile([P, PACK * H], BF16, name="w1_grouped", align_bytes=64)
         w1_codes = keep.tile([P, H], U32, name="w1_codes", align_bytes=64)
         w1_scales = keep.tile([P, H], U8, name="w1_scales", align_bytes=64)
-        cast_weight(nc, w1_raw, w1_grouped, SCALAR_COLUMNS_W1)
+        cast_weight(nc, w1_raw, w1_grouped)
         quantize(nc, w1_codes[:], w1_scales[:], w1_grouped[:])
 
         for t in range(1, PACK):
@@ -142,7 +143,7 @@ def tile_picked_bens8_none_p_kernel(tc, x_words, x_scales, w1, rin, w2, so, offs
         x_picked = late.tile([P, S], U32, name="x_picked", offset=PICKED, align_bytes=64)
         for first, count in pieces:
             nc.vector.tensor_copy(x_picked[:, first : first + count], xw_sb[:].bitcast(U32).indirect(entries(offs_sb, first, count)))
-        fetch_rin(fetch_on_scalar, 3)
+        fetch_rin(fetch_on_scalar, 3, pieces)
 
         so_picked = [keep.tile([P, S], F32, name=f"so_picked{t}") for t in range(PACK)]
         fetch_on_scalar(so_picked[0][:], so_sb[0], 0, S)
@@ -154,14 +155,13 @@ def tile_picked_bens8_none_p_kernel(tc, x_words, x_scales, w1, rin, w2, so, offs
         def hidden_quarter(q):
             c, first = divmod(q * QUARTER, HALF)
             tokens = slice(q * QUARTER, (q + 1) * QUARTER)
-            piece = min(q * QUARTER, HALF)
             h_bank = psum.tile([P, PACK, QUARTER], F32, name=f"h_bank{q}")
             for t in range(PACK):
                 product(nc, h_bank[:, t, :], w1_codes, w1_scales, t, x_picked[:, tokens], xs_picked[:, tokens])
             nc.vector.tensor_tensor(
                 z_grouped[c][:, first * PACK : (first + QUARTER) * PACK].rearrange("p (n i t) -> p n t i", i=2, t=PACK),
                 h_bank[:].rearrange("p t (n i) -> p n t i", i=2),
-                rin_picked[piece][:, :, tokens.start - piece : tokens.stop - piece].rearrange("p t (n i) -> p n t i", i=2),
+                rin_picked[c][:, :, first : first + QUARTER].rearrange("p t (n i) -> p n t i", i=2),
                 MULT,
             )
 
@@ -169,7 +169,7 @@ def tile_picked_bens8_none_p_kernel(tc, x_words, x_scales, w1, rin, w2, so, offs
             if c == 0:
                 z_codes[c] = keep.tile([P, HALF], U32, name="z_codes0", align_bytes=64)
             else:
-                z_codes[c] = late.tile([P, HALF], U32, name="z_codes1", offset=HELD + PLANE_BYTES, align_bytes=64)
+                z_codes[c] = late.tile([P, HALF], U32, name="z_codes1", offset=HELD + 3 * PLANE_BYTES, align_bytes=64)
             quantize(nc, z_codes[c][:], z_scales[c][:], z_grouped[c][:])
 
         for q in range(3):

@@ -22,7 +22,7 @@ QUARTER = 128
 LIST_ROWS = 16
 SCALE_ROWS = 16
 PLANE_BYTES = 4 * U
-SCALAR_COLUMNS = 72
+SCALAR_COLUMNS = 56
 W1_AT = 2 * PLANE_BYTES
 PICKED = W1_AT + PLANE_BYTES // 4
 HELD = 10 * PLANE_BYTES
@@ -187,6 +187,7 @@ def tile_picked_bens8_none_p_kernel(tc, x_words, x_scales, w1, rin, w2, so, offs
         nc.vector.tensor_copy(target[:, SCALAR_COLUMNS:], source[:, SCALAR_COLUMNS:])
         quantize_pair(w2_codes, w2_scales, w2_grouped, 0)
         quantize_z(1)
+        quantize_pair(w2_codes, w2_scales, w2_grouped, 1)
 
         for t in (1, 2):
             fetch_on_scalar(so_picked[t][:], so_sb[t], 0, S)
@@ -206,16 +207,13 @@ def tile_picked_bens8_none_p_kernel(tc, x_words, x_scales, w1, rin, w2, so, offs
             o_half = psum.tile([P, HALF], F32, name=f"o_half{c}", tag=f"h_bank{c}")
             product(nc, o_half[:], w2_codes, w2_scales, 0, z_codes[c][:], z_scales[c][:])
             output_piece(0, o_half, c * HALF, c * HALF, HALF)
-            if c == 0:
-                quantize_pair(w2_codes, w2_scales, w2_grouped, 1)
         for t in range(1, PACK):
             o_bank = psum.tile([P, S], F32, name=f"o_bank{t}")
             for c in range(2):
                 product(nc, o_bank[:, c * HALF : (c + 1) * HALF], w2_codes, w2_scales, t, z_codes[c][:], z_scales[c][:])
             if t < PACK - 1:
                 output_piece(t, o_bank, 0, 0, S)
-        output_piece(t, o_bank, 0, 0, HALF)
-        last = keep.tile([P, HALF], F32, name="last")
-        for first, count in last_pieces[1:]:
-            nc.vector.tensor_tensor(last[:, first - HALF : first - HALF + count], o_bank[:, first : first + count], so_picked[t][:, first : first + count], MULT)
-        nc.sync.dma_start(out_rows[t][:, HALF:], last[:])
+        last = keep.tile([P, S], F32, name="last")
+        for first, count in last_pieces:
+            nc.vector.tensor_tensor(last[:, first : first + count], o_bank[:, first : first + count], so_picked[t][:, first : first + count], MULT)
+        nc.sync.dma_start(out_rows[t], last[:])

@@ -22,7 +22,7 @@ QUARTER = 128
 LIST_ROWS = 16
 SCALE_ROWS = 16
 PLANE_BYTES = 4 * U
-SCALAR_COLUMNS = 56
+SCALAR_COLUMNS = 84
 W1_AT = 2 * PLANE_BYTES
 PICKED = W1_AT + PLANE_BYTES // 4
 HELD = 10 * PLANE_BYTES
@@ -195,25 +195,21 @@ def tile_picked_bens8_none_p_kernel(tc, x_words, x_scales, w1, rin, w2, so, offs
         for first, count in last_pieces:
             fetch_on_scalar(so_picked[3][:, first : first + count], so_sb[3], first, count)
 
-        out_rows = out.rearrange("(p t) s -> t p s", t=PACK)
+        out_flat = out.rearrange("(p t) s -> p (t s)", t=PACK)
+        result = keep.tile([P, PACK * S], F32, name="result")
 
-        def output_piece(t, o_bank, bank_first, first, count):
-            tokens = slice(first, first + count)
-            result = keep.tile([P, count], F32, name=f"result{t}_{first}")
-            nc.vector.tensor_tensor(result[:], o_bank[:, first - bank_first : first - bank_first + count], so_picked[t][:, tokens], MULT)
-            nc.sync.dma_start(out_rows[t][:, tokens], result[:])
+        def multiply_half(t, c, width):
+            o_bank = psum.tile([P, HALF], F32, name=f"o_bank{t}{c}", tag=f"h_bank{2 * t + c}")
+            product(nc, o_bank[:], w2_codes, w2_scales, t, z_codes[c][:], z_scales[c][:])
+            for first in range(0, HALF, width):
+                token = c * HALF + first
+                nc.vector.tensor_tensor(result[:, t * S + token : t * S + token + width], o_bank[:, first : first + width], so_picked[t][:, token : token + width], MULT)
 
-        for c in range(2):
-            o_half = psum.tile([P, HALF], F32, name=f"o_half{c}", tag=f"h_bank{c}")
-            product(nc, o_half[:], w2_codes, w2_scales, 0, z_codes[c][:], z_scales[c][:])
-            output_piece(0, o_half, c * HALF, c * HALF, HALF)
-        for t in range(1, PACK):
-            o_bank = psum.tile([P, S], F32, name=f"o_bank{t}")
-            for c in range(2):
-                product(nc, o_bank[:, c * HALF : (c + 1) * HALF], w2_codes, w2_scales, t, z_codes[c][:], z_scales[c][:])
-            if t < PACK - 1:
-                output_piece(t, o_bank, 0, 0, S)
-        last = keep.tile([P, S], F32, name="last")
-        for first, count in last_pieces:
-            nc.vector.tensor_tensor(last[:, first : first + count], o_bank[:, first : first + count], so_picked[t][:, first : first + count], MULT)
-        nc.sync.dma_start(out_rows[t], last[:])
+        stored = 0
+        for half in range(2 * PACK):
+            t, c = divmod(half, 2)
+            multiply_half(t, c, QUARTER if half == 2 * PACK - 1 else HALF)
+            if half not in (3, 5):
+                done = (half + 1) * HALF
+                nc.sync.dma_start(out_flat[:, stored:done], result[:, stored:done])
+                stored = done

@@ -22,7 +22,7 @@ QUARTER = 128
 LIST_ROWS = 16
 SCALE_ROWS = 16
 PLANE_BYTES = 4 * U
-SCALAR_COLUMNS = 84
+SCALAR_COLUMNS = 100
 W1_AT = 2 * PLANE_BYTES
 PICKED = W1_AT + PLANE_BYTES // 4
 HELD = 10 * PLANE_BYTES

@@ -89,7 +89,7 @@ def tile_picked_bens8_none_p_kernel(tc, x_words, x_scales, w1, rin, w2, so, offs
 
         first_row = 32
         nc.vector.memset(xs_sb[:].bitcast(I32), 0)
-        nc.sync.dma_start(rin_sb[0][:], rin.rearrange("(p t) u -> p (t u)", t=PACK)[:, : 2 * U])
+        nc.scalar.dma_start(rin_sb[0][:], rin.rearrange("(p t) u -> p (t u)", t=PACK)[:, : 2 * U])
         nc.sync.dma_start(mem_sb[:], mem)
         nc.sync.dma_start(offs_sb[:], offs)
         nc.sync.dma_start(xs_sb[first_row : first_row + 4 * SCALE_ROWS : 4, :].bitcast(I32), x_scales[0].bitcast(I32))

@@ -20,12 +20,14 @@ PACK = 4
 HALF = 256
 QUARTER = 128
 LIST_ROWS = 16
-SCALE_ROWS = 16
+ALIGN = 256
 PLANE_BYTES = 4 * U
 SCALAR_COLUMNS = 100
 W1_AT = 2 * PLANE_BYTES
-PICKED = W1_AT + PLANE_BYTES // 4
-HELD = 10 * PLANE_BYTES
+PICKED_AT = W1_AT + PLANE_BYTES // 4
+SCALES_AT = 10 * PLANE_BYTES
+RIN_AT = 12 * PLANE_BYTES
+W2_AT = 15 * PLANE_BYTES
 
 
 def plane_rows(table, t):
@@ -80,33 +82,31 @@ def tile_picked_bens8_none_p_kernel(tc, x_words, x_scales, w1, rin, w2, so, offs
         def fetch_on_vector(target, window, first, count):
             nc.vector.tensor_copy(target, window[:].indirect(entries(mem_sb, first, count)))
 
-        rin_sb = [keep.tile([P, 2 * U], F32, name="rin_sb0")]
-        rin_sb.append(late.tile([P, U], F32, name="rin_sb1", offset=HELD + 3 * PLANE_BYTES))
-        rin_sb.append(keep.tile([P, U], F32, name="rin_sb2"))
-        xs_sb = late.tile([P, T], U8, name="xs_sb", offset=HELD)
+        rin_sb = [late.tile([P, 2 * U], F32, name="rin_sb0", offset=RIN_AT, align_bytes=ALIGN)]
+        rin_sb.append(late.tile([P, U], F32, name="rin_sb1", offset=W2_AT))
+        xs_sb = late.tile([P, T], U8, name="xs_sb", offset=SCALES_AT)
         w1_raw = late.tile([P, PACK, H], F32, name="w1_raw", offset=W1_AT)
-        xw_sb = keep.tile([P, T], I32, name="xw_sb")
+        xw_sb = keep.tile([P, T], I32, name="xw_sb", align_bytes=ALIGN)
 
-        first_row = 32
         nc.vector.memset(xs_sb[:].bitcast(I32), 0)
         nc.scalar.dma_start(rin_sb[0][:], rin.rearrange("(p t) u -> p (t u)", t=PACK)[:, : 2 * U])
         nc.sync.dma_start(mem_sb[:], mem)
         nc.sync.dma_start(offs_sb[:], offs)
-        nc.sync.dma_start(xs_sb[first_row : first_row + 4 * SCALE_ROWS : 4, :].bitcast(I32), x_scales[0].bitcast(I32))
+        nc.sync.dma_start(xs_sb[0:P:8, :].bitcast(I32), x_scales[0].bitcast(I32))
         nc.sync.dma_start(w1_raw[:], w1.rearrange("(p j) c -> p j c", j=PACK))
-        nc.sync.dma_start(rin_sb[2][:], plane_rows(rin, 2))
         nc.sync.dma_start(xw_sb[:], x_words[0].rearrange("p n r -> p (n r)").bitcast(I32))
 
-        xs_gathered = keep.tile([P, S], U8, name="xs_gathered", align_bytes=64)
+        xs_gathered = keep.tile([P, S], U8, name="xs_gathered", align_bytes=ALIGN)
         nc.vector.tensor_copy(xs_gathered[:], xs_sb[:].indirect(offs_sb[:]))
-        xs_picked = keep.tile([P, S], U8, name="xs_picked", align_bytes=64)
-        nc.vector.memset(xs_picked[:].bitcast(I32), 0)
-        for r in range(4):
-            nc.sync.dma_start(xs_picked[r:P:32, :].bitcast(I32), xs_gathered[first_row + 4 * r : first_row + 4 * SCALE_ROWS : 16, :].bitcast(I32))
-        rin_sb.append(late.tile([P, U], F32, name="rin_sb3", offset=HELD + PLANE_BYTES // 2))
-        nc.sync.dma_start(rin_sb[3][:], plane_rows(rin, 3))
+        xs_picked = keep.tile([P, S], U8, name="xs_picked", align_bytes=ALIGN)
+        nc.vector.tensor_copy(xs_picked[:].bitcast(I32), xs_gathered[:].bitcast(I32))
+        for r in range(1, 4):
+            nc.sync.dma_start(xs_picked[r:P:32, :].bitcast(I32), xs_gathered[8 * r : P : 32, :].bitcast(I32))
+        for t in (2, 3):
+            rin_sb.append(late.tile([P, U], F32, name=f"rin_sb{t}", offset=SCALES_AT + (2 * t - 5) * PLANE_BYTES // 2))
+            nc.sync.dma_start(rin_sb[t][:], plane_rows(rin, t))
 
-        pieces = ((0, QUARTER), (QUARTER, QUARTER), (HALF, HALF))
+        quarters = ((0, QUARTER), (QUARTER, QUARTER))
         halves = ((0, HALF), (HALF, HALF))
         rin_picked = [keep.tile([P, PACK, HALF], F32, name=f"rin_picked{c}") for c in range(2)]
 
@@ -116,13 +116,12 @@ def tile_picked_bens8_none_p_kernel(tc, x_words, x_scales, w1, rin, w2, so, offs
                 fetch(rin_picked[c][:, t, column : column + count], rin_sb[t], first, count)
 
         nc.scalar.copy(out=rin_sb[1][:], in_=rin_sb[0][:, U:])
-        fetch_rin(fetch_on_vector, 0, halves)
+        fetch_rin(fetch_on_scalar, 0, halves)
         fetch_rin(fetch_on_scalar, 1, halves)
-        fetch_rin(fetch_on_scalar, 2, halves)
 
-        so_sb = [late.tile([P, 2 * U], F32, name="so_sb0", offset=HELD - 3 * PLANE_BYTES // 2)]
+        so_sb = [late.tile([P, 2 * U], F32, name="so_sb0", offset=RIN_AT + PLANE_BYTES)]
         nc.sync.dma_start(so_sb[0][:, :U], plane_rows(so, 0))
-        w2_raw = late.tile([P, PACK, N], F32, name="w2_raw", offset=HELD + 3 * PLANE_BYTES)
+        w2_raw = late.tile([P, PACK, N], F32, name="w2_raw", offset=W2_AT)
         nc.sync.dma_start(w2_raw[:], w2.rearrange("(p j) c -> p j c", j=PACK))
 
         def quantize_pair(codes, scales, grouped, u):
@@ -137,13 +136,15 @@ def tile_picked_bens8_none_p_kernel(tc, x_words, x_scales, w1, rin, w2, so, offs
 
         for t in range(1, PACK):
             width = U if t == PACK - 1 else 2 * U
-            so_sb.append(late.tile([P, width], F32, name=f"so_sb{t}", offset=PICKED + (-2, 3, 2)[t - 1] * PLANE_BYTES))
+            so_sb.append(late.tile([P, width], F32, name=f"so_sb{t}", offset=PICKED_AT + (-2, 3, 2)[t - 1] * PLANE_BYTES))
             nc.sync.dma_start(so_sb[t][:, :U], plane_rows(so, t))
 
-        x_picked = late.tile([P, S], U32, name="x_picked", offset=PICKED, align_bytes=64)
-        for first, count in pieces:
+        x_picked = late.tile([P, S], U32, name="x_picked", offset=PICKED_AT, align_bytes=64)
+        for first, count in quarters + halves[1:]:
             nc.vector.tensor_copy(x_picked[:, first : first + count], xw_sb[:].bitcast(U32).indirect(entries(offs_sb, first, count)))
-        fetch_rin(fetch_on_scalar, 3, pieces)
+        fetch_rin(fetch_on_scalar, 2, halves[:1])
+        fetch_rin(fetch_on_vector, 2, halves[1:])
+        fetch_rin(fetch_on_scalar, 3, quarters + halves[1:])
 
         so_picked = [keep.tile([P, S], F32, name=f"so_picked{t}") for t in range(PACK)]
         fetch_on_scalar(so_picked[0][:], so_sb[0], 0, S)
@@ -155,7 +156,7 @@ def tile_picked_bens8_none_p_kernel(tc, x_words, x_scales, w1, rin, w2, so, offs
         def hidden_quarter(q):
             c, first = divmod(q * QUARTER, HALF)
             tokens = slice(q * QUARTER, (q + 1) * QUARTER)
-            h_bank = psum.tile([P, PACK, QUARTER], F32, name=f"h_bank{q}")
+            h_bank = psum.tile([P, PACK, QUARTER], F32, name=f"h_bank{q}", tag=f"bank{q % 3}")
             for t in range(PACK):
                 product(nc, h_bank[:, t, :], w1_codes, w1_scales, t, x_picked[:, tokens], xs_picked[:, tokens])
             nc.vector.tensor_tensor(
@@ -169,7 +170,7 @@ def tile_picked_bens8_none_p_kernel(tc, x_words, x_scales, w1, rin, w2, so, offs
             if c == 0:
                 z_codes[c] = keep.tile([P, HALF], U32, name="z_codes0", align_bytes=64)
             else:
-                z_codes[c] = late.tile([P, HALF], U32, name="z_codes1", offset=HELD + 3 * PLANE_BYTES, align_bytes=64)
+                z_codes[c] = late.tile([P, HALF], U32, name="z_codes1", offset=W2_AT, align_bytes=64)
             quantize(nc, z_codes[c][:], z_scales[c][:], z_grouped[c][:])
 
         for q in range(3):
@@ -196,10 +197,10 @@ def tile_picked_bens8_none_p_kernel(tc, x_words, x_scales, w1, rin, w2, so, offs
             fetch_on_scalar(so_picked[3][:, first : first + count], so_sb[3], first, count)
 
         out_flat = out.rearrange("(p t) s -> p (t s)", t=PACK)
-        result = keep.tile([P, PACK * S], F32, name="result")
+        result = keep.tile([P, PACK * S], F32, name="result", align_bytes=ALIGN)
 
         def multiply_half(t, c, width):
-            o_bank = psum.tile([P, HALF], F32, name=f"o_bank{t}{c}", tag=f"h_bank{2 * t + c}")
+            o_bank = psum.tile([P, HALF], F32, name=f"o_bank{t}{c}", tag=f"bank{(2 * t + c + 3) % 8}")
             product(nc, o_bank[:], w2_codes, w2_scales, t, z_codes[c][:], z_scales[c][:])
             for first in range(0, HALF, width):
                 token = c * HALF + first

@@ -22,12 +22,11 @@ QUARTER = 128
 LIST_ROWS = 16
 ALIGN = 256
 PLANE_BYTES = 4 * U
-SCALAR_COLUMNS = 100
 W1_AT = 2 * PLANE_BYTES
 PICKED_AT = W1_AT + PLANE_BYTES // 4
 SCALES_AT = 10 * PLANE_BYTES
 RIN_AT = 12 * PLANE_BYTES
-W2_AT = 15 * PLANE_BYTES
+W2_AT = 16 * PLANE_BYTES
 
 
 def plane_rows(table, t):
@@ -40,9 +39,9 @@ def cast_weight(nc, raw, grouped):
     nc.vector.tensor_copy(target, source)
 
 
-def weight_pair_views(raw, grouped, u):
+def weight_pair_views(raw, grouped, u, c):
     return (
-        grouped.rearrange("p (i m j) -> p m j i", i=2, j=PACK),
+        grouped.rearrange("p (i c m j) -> p c m j i", i=2, c=2, j=PACK)[:, c],
         raw[:].rearrange("p j (m u i) -> p u m j i", u=2, i=2)[:, u],
     )
 
@@ -83,7 +82,7 @@ def tile_picked_bens8_none_p_kernel(tc, x_words, x_scales, w1, rin, w2, so, offs
             nc.vector.tensor_copy(target, window[:].indirect(entries(mem_sb, first, count)))
 
         rin_sb = [late.tile([P, 2 * U], F32, name="rin_sb0", offset=RIN_AT, align_bytes=ALIGN)]
-        rin_sb.append(late.tile([P, U], F32, name="rin_sb1", offset=W2_AT))
+        rin_sb.append(late.tile([P, U], F32, name="rin_sb1", offset=W2_AT + 3 * PLANE_BYTES // 2))
         xs_sb = late.tile([P, T], U8, name="xs_sb", offset=SCALES_AT)
         w1_raw = late.tile([P, PACK, H], F32, name="w1_raw", offset=W1_AT)
         xw_sb = keep.tile([P, T], I32, name="xw_sb", align_bytes=ALIGN)
@@ -121,8 +120,10 @@ def tile_picked_bens8_none_p_kernel(tc, x_words, x_scales, w1, rin, w2, so, offs
 
         so_sb = [late.tile([P, 2 * U], F32, name="so_sb0", offset=RIN_AT + PLANE_BYTES)]
         nc.sync.dma_start(so_sb[0][:, :U], plane_rows(so, 0))
-        w2_raw = late.tile([P, PACK, N], F32, name="w2_raw", offset=W2_AT)
-        nc.sync.dma_start(w2_raw[:], w2.rearrange("(p j) c -> p j c", j=PACK))
+        w2_raw = []
+        for c in range(2):
+            w2_raw.append(late.tile([P, PACK, HALF], F32, name=f"w2_raw{c}", offset=W2_AT + 2 * c * PLANE_BYTES))
+            nc.sync.dma_start(w2_raw[c][:], w2.rearrange("(p j) c -> p j c", j=PACK)[:, :, c * HALF : (c + 1) * HALF])
 
         def quantize_pair(codes, scales, grouped, u):
             cols = slice(2 * u * P, 2 * (u + 1) * P)
@@ -170,7 +171,7 @@ def tile_picked_bens8_none_p_kernel(tc, x_words, x_scales, w1, rin, w2, so, offs
             if c == 0:
                 z_codes[c] = keep.tile([P, HALF], U32, name="z_codes0", align_bytes=64)
             else:
-                z_codes[c] = late.tile([P, HALF], U32, name="z_codes1", offset=W2_AT, align_bytes=64)
+                z_codes[c] = late.tile([P, HALF], U32, name="z_codes1", offset=W2_AT + 2 * PLANE_BYTES, align_bytes=64)
             quantize(nc, z_codes[c][:], z_scales[c][:], z_grouped[c][:])
 
         for q in range(3):
@@ -181,11 +182,11 @@ def tile_picked_bens8_none_p_kernel(tc, x_words, x_scales, w1, rin, w2, so, offs
         w2_grouped = [keep.tile([P, 2 * N], BF16, name=f"w2_grouped{u}", align_bytes=64) for u in range(2)]
         w2_codes = keep.tile([P, N], U32, name="w2_codes", align_bytes=64)
         w2_scales = keep.tile([P, N], U8, name="w2_scales", align_bytes=64)
-        target, source = weight_pair_views(w2_raw, w2_grouped[0][:], 0)
-        nc.vector.tensor_copy(target, source)
-        target, source = weight_pair_views(w2_raw, w2_grouped[1][:], 1)
-        nc.scalar.copy(out=target[:, :SCALAR_COLUMNS], in_=source[:, :SCALAR_COLUMNS])
-        nc.vector.tensor_copy(target[:, SCALAR_COLUMNS:], source[:, SCALAR_COLUMNS:])
+        for u in range(2):
+            target, source = weight_pair_views(w2_raw[0], w2_grouped[u][:], u, 0)
+            nc.scalar.copy(out=target, in_=source)
+            target, source = weight_pair_views(w2_raw[1], w2_grouped[u][:], u, 1)
+            nc.vector.tensor_copy(target, source)
         quantize_pair(w2_codes, w2_scales, w2_grouped, 0)
         quantize_z(1)
         quantize_pair(w2_codes, w2_scales, w2_grouped, 1)

@@ -13,6 +13,7 @@ U16 = mybir.dt.uint16
 U8 = mybir.dt.uint8
 FP8X4 = mybir.dt.float8_e4m3fn_x4
 MULT = mybir.AluOpType.mult
+ADD = mybir.AluOpType.add
 COPY = mybir.ActivationFunctionType.Copy
 
 P = 128
@@ -22,6 +23,8 @@ QUARTER = 128
 LIST_ROWS = 16
 ALIGN = 256
 PLANE_BYTES = 4 * U
+GPSIMD_COLUMNS = 48
+SCALAR_LATE_COLUMNS = 24
 W1_AT = 2 * PLANE_BYTES
 PICKED_AT = W1_AT + PLANE_BYTES // 4
 SCALES_AT = 10 * PLANE_BYTES
@@ -174,19 +177,23 @@ def tile_picked_bens8_none_p_kernel(tc, x_words, x_scales, w1, rin, w2, so, offs
                 z_codes[c] = late.tile([P, HALF], U32, name="z_codes1", offset=W2_AT + 2 * PLANE_BYTES, align_bytes=64)
             quantize(nc, z_codes[c][:], z_scales[c][:], z_grouped[c][:])
 
-        for q in range(3):
+        for q in range(PACK):
             hidden_quarter(q)
         quantize_z(0)
-        hidden_quarter(3)
 
         w2_grouped = [keep.tile([P, 2 * N], BF16, name=f"w2_grouped{u}", align_bytes=64) for u in range(2)]
         w2_codes = keep.tile([P, N], U32, name="w2_codes", align_bytes=64)
         w2_scales = keep.tile([P, N], U8, name="w2_scales", align_bytes=64)
-        for u in range(2):
-            target, source = weight_pair_views(w2_raw[0], w2_grouped[u][:], u, 0)
-            nc.scalar.copy(out=target, in_=source)
-            target, source = weight_pair_views(w2_raw[1], w2_grouped[u][:], u, 1)
-            nc.vector.tensor_copy(target, source)
+        target, source = weight_pair_views(w2_raw[0], w2_grouped[1][:], 1, 0)
+        nc.gpsimd.tensor_scalar(
+            target[:, :GPSIMD_COLUMNS].rearrange("p m j i -> p i m j"), source[:, :GPSIMD_COLUMNS].rearrange("p m j i -> p i m j"), 1.0, 0.0, MULT, ADD
+        )
+        nc.scalar.copy(*weight_pair_views(w2_raw[0], w2_grouped[0][:], 0, 0))
+        nc.scalar.copy(target[:, GPSIMD_COLUMNS:], source[:, GPSIMD_COLUMNS:])
+        nc.vector.tensor_copy(*weight_pair_views(w2_raw[1], w2_grouped[0][:], 0, 1))
+        target, source = weight_pair_views(w2_raw[1], w2_grouped[1][:], 1, 1)
+        nc.scalar.copy(target[:, :SCALAR_LATE_COLUMNS], source[:, :SCALAR_LATE_COLUMNS])
+        nc.vector.tensor_copy(target[:, SCALAR_LATE_COLUMNS:], source[:, SCALAR_LATE_COLUMNS:])
         quantize_pair(w2_codes, w2_scales, w2_grouped, 0)
         quantize_z(1)
         quantize_pair(w2_codes, w2_scales, w2_grouped, 1)

@@ -23,12 +23,11 @@ QUARTER = 128
 LIST_ROWS = 16
 ALIGN = 256
 PLANE_BYTES = 4 * U
-GPSIMD_COLUMNS = 48
-SCALAR_LATE_COLUMNS = 24
+SCALAR_GROUPS = 48
 W1_AT = 2 * PLANE_BYTES
 PICKED_AT = W1_AT + PLANE_BYTES // 4
 SCALES_AT = 10 * PLANE_BYTES
-RIN_AT = 12 * PLANE_BYTES
+RIN_AT = 13 * PLANE_BYTES
 W2_AT = 16 * PLANE_BYTES
 
 
@@ -85,7 +84,7 @@ def tile_picked_bens8_none_p_kernel(tc, x_words, x_scales, w1, rin, w2, so, offs
             nc.vector.tensor_copy(target, window[:].indirect(entries(mem_sb, first, count)))
 
         rin_sb = [late.tile([P, 2 * U], F32, name="rin_sb0", offset=RIN_AT, align_bytes=ALIGN)]
-        rin_sb.append(late.tile([P, U], F32, name="rin_sb1", offset=W2_AT + 3 * PLANE_BYTES // 2))
+        rin_sb.append(late.tile([P, U], F32, name="rin_sb1", offset=W2_AT))
         xs_sb = late.tile([P, T], U8, name="xs_sb", offset=SCALES_AT)
         w1_raw = late.tile([P, PACK, H], F32, name="w1_raw", offset=W1_AT)
         xw_sb = keep.tile([P, T], I32, name="xw_sb", align_bytes=ALIGN)
@@ -121,16 +120,13 @@ def tile_picked_bens8_none_p_kernel(tc, x_words, x_scales, w1, rin, w2, so, offs
         fetch_rin(fetch_on_scalar, 0, halves)
         fetch_rin(fetch_on_scalar, 1, halves)
 
+        w2_rows = w2.rearrange("(p j) c -> p j c", j=PACK)
+        w2_raw = [late.tile([P, PACK, HALF], F32, name="w2_raw0", offset=RIN_AT - 3 * PLANE_BYTES // 2)]
+        nc.sync.dma_start(w2_raw[0][:], w2_rows[:, :, :HALF])
         so_sb = [late.tile([P, 2 * U], F32, name="so_sb0", offset=RIN_AT + PLANE_BYTES)]
         nc.sync.dma_start(so_sb[0][:, :U], plane_rows(so, 0))
-        w2_raw = []
-        for c in range(2):
-            w2_raw.append(late.tile([P, PACK, HALF], F32, name=f"w2_raw{c}", offset=W2_AT + 2 * c * PLANE_BYTES))
-            nc.sync.dma_start(w2_raw[c][:], w2.rearrange("(p j) c -> p j c", j=PACK)[:, :, c * HALF : (c + 1) * HALF])
-
-        def quantize_pair(codes, scales, grouped, u):
-            cols = slice(2 * u * P, 2 * (u + 1) * P)
-            quantize(nc, codes[:, cols], scales[:, cols], grouped[u][:])
+        w2_raw.append(late.tile([P, PACK, HALF], F32, name="w2_raw1", offset=W2_AT))
+        nc.sync.dma_start(w2_raw[1][:], w2_rows[:, :, HALF:])
 
         w1_grouped = keep.tile([P, PACK * H], BF16, name="w1_grouped", align_bytes=64)
         w1_codes = keep.tile([P, H], U32, name="w1_codes", align_bytes=64)
@@ -139,7 +135,7 @@ def tile_picked_bens8_none_p_kernel(tc, x_words, x_scales, w1, rin, w2, so, offs
         quantize(nc, w1_codes[:], w1_scales[:], w1_grouped[:])
 
         for t in range(1, PACK):
-            width = U if t == PACK - 1 else 2 * U
+            width = 2 * U if t == 1 else U
             so_sb.append(late.tile([P, width], F32, name=f"so_sb{t}", offset=PICKED_AT + (-2, 3, 2)[t - 1] * PLANE_BYTES))
             nc.sync.dma_start(so_sb[t][:, :U], plane_rows(so, t))
 
@@ -151,10 +147,9 @@ def tile_picked_bens8_none_p_kernel(tc, x_words, x_scales, w1, rin, w2, so, offs
         fetch_rin(fetch_on_scalar, 3, quarters + halves[1:])
 
         so_picked = [keep.tile([P, S], F32, name=f"so_picked{t}") for t in range(PACK)]
-        fetch_on_scalar(so_picked[0][:], so_sb[0], 0, S)
 
         z_grouped = [keep.tile([P, PACK * HALF], BF16, name=f"z_grouped{c}", align_bytes=64) for c in range(2)]
-        z_codes = {}
+        z_codes = [keep.tile([P, HALF], U32, name=f"z_codes{c}", align_bytes=64) for c in range(2)]
         z_scales = [keep.tile([P, HALF], U8, name=f"z_scales{c}", align_bytes=64) for c in range(2)]
 
         def hidden_quarter(q):
@@ -170,46 +165,42 @@ def tile_picked_bens8_none_p_kernel(tc, x_words, x_scales, w1, rin, w2, so, offs
                 MULT,
             )
 
-        def quantize_z(c):
-            if c == 0:
-                z_codes[c] = keep.tile([P, HALF], U32, name="z_codes0", align_bytes=64)
-            else:
-                z_codes[c] = late.tile([P, HALF], U32, name="z_codes1", offset=W2_AT + 2 * PLANE_BYTES, align_bytes=64)
-            quantize(nc, z_codes[c][:], z_scales[c][:], z_grouped[c][:])
-
         for q in range(PACK):
             hidden_quarter(q)
-        quantize_z(0)
+        for c in range(2):
+            quantize(nc, z_codes[c][:], z_scales[c][:], z_grouped[c][:])
 
         w2_grouped = [keep.tile([P, 2 * N], BF16, name=f"w2_grouped{u}", align_bytes=64) for u in range(2)]
-        w2_codes = keep.tile([P, N], U32, name="w2_codes", align_bytes=64)
-        w2_scales = keep.tile([P, N], U8, name="w2_scales", align_bytes=64)
-        target, source = weight_pair_views(w2_raw[0], w2_grouped[1][:], 1, 0)
-        nc.gpsimd.tensor_scalar(
-            target[:, :GPSIMD_COLUMNS].rearrange("p m j i -> p i m j"), source[:, :GPSIMD_COLUMNS].rearrange("p m j i -> p i m j"), 1.0, 0.0, MULT, ADD
-        )
-        nc.scalar.copy(*weight_pair_views(w2_raw[0], w2_grouped[0][:], 0, 0))
-        nc.scalar.copy(target[:, GPSIMD_COLUMNS:], source[:, GPSIMD_COLUMNS:])
-        nc.vector.tensor_copy(*weight_pair_views(w2_raw[1], w2_grouped[0][:], 0, 1))
-        target, source = weight_pair_views(w2_raw[1], w2_grouped[1][:], 1, 1)
-        nc.scalar.copy(target[:, :SCALAR_LATE_COLUMNS], source[:, :SCALAR_LATE_COLUMNS])
-        nc.vector.tensor_copy(target[:, SCALAR_LATE_COLUMNS:], source[:, SCALAR_LATE_COLUMNS:])
-        quantize_pair(w2_codes, w2_scales, w2_grouped, 0)
-        quantize_z(1)
-        quantize_pair(w2_codes, w2_scales, w2_grouped, 1)
+        w2_scales = [keep.tile([P, 2 * P], U8, name=f"w2_scales{u}", align_bytes=64) for u in range(2)]
 
-        for t in (1, 2):
-            fetch_on_scalar(so_picked[t][:], so_sb[t], 0, S)
-        last_pieces = ((0, HALF), (HALF, QUARTER), (HALF + QUARTER, QUARTER))
-        for first, count in last_pieces:
-            fetch_on_scalar(so_picked[3][:, first : first + count], so_sb[3], first, count)
+        def cast_on_gpsimd(target, source):
+            nc.gpsimd.tensor_scalar(target.rearrange("p m j i -> p i m j"), source.rearrange("p m j i -> p i m j"), 1.0, 0.0, MULT, ADD)
+
+        target, source = weight_pair_views(w2_raw[0], w2_grouped[0][:], 0, 0)
+        nc.scalar.copy(target[:, :SCALAR_GROUPS], source[:, :SCALAR_GROUPS])
+        cast_on_gpsimd(target[:, SCALAR_GROUPS:], source[:, SCALAR_GROUPS:])
+        cast_on_gpsimd(*weight_pair_views(w2_raw[0], w2_grouped[1][:], 1, 0))
+        fetch_on_scalar(so_picked[0][:], so_sb[0], 0, S)
+        nc.scalar.copy(*weight_pair_views(w2_raw[1], w2_grouped[0][:], 0, 1))
+        nc.vector.tensor_copy(*weight_pair_views(w2_raw[1], w2_grouped[1][:], 1, 1))
+        w2_codes = [keep.tile([P, 2 * P], U32, name="w2_codes0", align_bytes=64)]
+        w2_codes.append(late.tile([P, 2 * P], U32, name="w2_codes1", offset=W2_AT, align_bytes=64))
+        for u in range(2):
+            quantize(nc, w2_codes[u][:], w2_scales[u][:], w2_grouped[u][:])
+
+        fetch_on_vector(so_picked[2][:, S - QUARTER :], so_sb[2], S - QUARTER, QUARTER)
+        fetch_on_scalar(so_picked[1][:], so_sb[1], 0, S)
+        pieces = ((0, HALF), (HALF, QUARTER), (HALF + QUARTER, QUARTER))
+        for t, cuts in ((2, pieces[:2]), (3, pieces)):
+            for first, count in cuts:
+                fetch_on_scalar(so_picked[t][:, first : first + count], so_sb[t], first, count)
 
         out_flat = out.rearrange("(p t) s -> p (t s)", t=PACK)
         result = keep.tile([P, PACK * S], F32, name="result", align_bytes=ALIGN)
 
         def multiply_half(t, c, width):
             o_bank = psum.tile([P, HALF], F32, name=f"o_bank{t}{c}", tag=f"bank{(2 * t + c + 3) % 8}")
-            product(nc, o_bank[:], w2_codes, w2_scales, t, z_codes[c][:], z_scales[c][:])
+            product(nc, o_bank[:], w2_codes[t // 2], w2_scales[t // 2], t % 2, z_codes[c][:], z_scales[c][:])
             for first in range(0, HALF, width):
                 token = c * HALF + first
                 nc.vector.tensor_tensor(result[:, t * S + token : t * S + token + width], o_bank[:, first : first + width], so_picked[t][:, token : token + width], MULT)

from contextlib import ExitStack

import concourse.mybir as mybir

K, T, S, H, N, U = 512, 2048, 512, 512, 512, 512
FLOPS = 2 * K * H * S + 2 * H * N * S

F32 = mybir.dt.float32
BF16 = mybir.dt.bfloat16
I32 = mybir.dt.int32
U32 = mybir.dt.uint32
U16 = mybir.dt.uint16
U8 = mybir.dt.uint8
FP8X4 = mybir.dt.float8_e4m3fn_x4
MULT = mybir.AluOpType.mult
ADD = mybir.AluOpType.add
COPY = mybir.ActivationFunctionType.Copy

P = 128
PACK = 4
HALF = 256
QUARTER = 128
LIST_ROWS = 16
ALIGN = 256
PLANE_BYTES = 4 * U
SCALAR_GROUPS = 48
W1_AT = 2 * PLANE_BYTES
PICKED_AT = W1_AT + PLANE_BYTES // 4
SCALES_AT = 10 * PLANE_BYTES
RIN_AT = 13 * PLANE_BYTES
W2_AT = 16 * PLANE_BYTES


def plane_rows(table, t):
    return table.rearrange("(p t) u -> t p u", t=PACK)[t]


def cast_weight(nc, raw, grouped):
    target = grouped[:].rearrange("p (t m j) -> p m j t", t=PACK, j=PACK)
    source = raw[:].rearrange("p j (m t) -> p m j t", t=PACK)
    nc.vector.tensor_copy(target, source)


def weight_pair_views(raw, grouped, u, c):
    return (
        grouped.rearrange("p (i c m j) -> p c m j i", i=2, c=2, j=PACK)[:, c],
        raw[:].rearrange("p j (m u i) -> p u m j i", u=2, i=2)[:, u],
    )


def quantize(nc, codes, scales, grouped):
    nc.vector.quantize_mx(out=codes.bitcast(FP8X4), scales=scales, in_=grouped)


def product(nc, target, w_codes, w_scales, t, codes, scales):
    nc.tensor.matmul_mx(
        out=target,
        lhsT=w_codes[:, t * P : (t + 1) * P].bitcast(FP8X4),
        lhsT_scale=w_scales[:, t * P : (t + 1) * P],
        rhs=codes.bitcast(FP8X4),
        rhs_scale=scales,
        start=True,
        stop=True,
    )


def tile_picked_bens8_none_p_kernel(tc, x_words, x_scales, w1, rin, w2, so, offs, mem, out):
    nc = tc.nc
    with ExitStack() as ctx:
        keep = ctx.enter_context(tc.tile_pool(name="keep", bufs=1))
        late = ctx.enter_context(tc.tile_pool(name="late", bufs=1))
        psum = ctx.enter_context(tc.psum_pool(name="psum", bufs=1))

        def entries(list_sb, first, count):
            return list_sb[:, first // LIST_ROWS : (first + count) // LIST_ROWS]

        mem_sb = keep.tile([P, S // LIST_ROWS], U16, name="mem_sb")
        offs_sb = keep.tile([P, S // LIST_ROWS], U16, name="offs_sb")

        def fetch_on_scalar(target, window, first, count):
            nc.scalar.activation(target, window[:].indirect(entries(mem_sb, first, count)), COPY)

        def fetch_on_vector(target, window, first, count):
            nc.vector.tensor_copy(target, window[:].indirect(entries(mem_sb, first, count)))

        rin_sb = [late.tile([P, 2 * U], F32, name="rin_sb0", offset=RIN_AT, align_bytes=ALIGN)]
        rin_sb.append(late.tile([P, U], F32, name="rin_sb1", offset=W2_AT))
        xs_sb = late.tile([P, T], U8, name="xs_sb", offset=SCALES_AT)
        w1_raw = late.tile([P, PACK, H], F32, name="w1_raw", offset=W1_AT)
        xw_sb = keep.tile([P, T], I32, name="xw_sb", align_bytes=ALIGN)

        nc.vector.memset(xs_sb[:].bitcast(I32), 0)
        nc.scalar.dma_start(rin_sb[0][:], rin.rearrange("(p t) u -> p (t u)", t=PACK)[:, : 2 * U])
        nc.sync.dma_start(mem_sb[:], mem)
        nc.sync.dma_start(offs_sb[:], offs)
        nc.sync.dma_start(xs_sb[0:P:8, :].bitcast(I32), x_scales[0].bitcast(I32))
        nc.sync.dma_start(w1_raw[:], w1.rearrange("(p j) c -> p j c", j=PACK))
        nc.sync.dma_start(xw_sb[:], x_words[0].rearrange("p n r -> p (n r)").bitcast(I32))

        xs_gathered = keep.tile([P, S], U8, name="xs_gathered", align_bytes=ALIGN)
        nc.vector.tensor_copy(xs_gathered[:], xs_sb[:].indirect(offs_sb[:]))
        xs_picked = keep.tile([P, S], U8, name="xs_picked", align_bytes=ALIGN)
        nc.vector.tensor_copy(xs_picked[:].bitcast(I32), xs_gathered[:].bitcast(I32))
        for r in range(1, 4):
            nc.sync.dma_start(xs_picked[r:P:32, :].bitcast(I32), xs_gathered[8 * r : P : 32, :].bitcast(I32))
        for t in (2, 3):
            rin_sb.append(late.tile([P, U], F32, name=f"rin_sb{t}", offset=SCALES_AT + (2 * t - 5) * PLANE_BYTES // 2))
            nc.sync.dma_start(rin_sb[t][:], plane_rows(rin, t))

        quarters = ((0, QUARTER), (QUARTER, QUARTER))
        halves = ((0, HALF), (HALF, HALF))
        rin_picked = [keep.tile([P, PACK, HALF], F32, name=f"rin_picked{c}") for c in range(2)]

        def fetch_rin(fetch, t, cuts):
            for first, count in cuts:
                c, column = divmod(first, HALF)
                fetch(rin_picked[c][:, t, column : column + count], rin_sb[t], first, count)

        nc.scalar.copy(out=rin_sb[1][:], in_=rin_sb[0][:, U:])
        fetch_rin(fetch_on_scalar, 0, halves)
        fetch_rin(fetch_on_scalar, 1, halves)

        w2_rows = w2.rearrange("(p j) c -> p j c", j=PACK)
        w2_raw = [late.tile([P, PACK, HALF], F32, name="w2_raw0", offset=RIN_AT - 3 * PLANE_BYTES // 2)]
        nc.sync.dma_start(w2_raw[0][:], w2_rows[:, :, :HALF])
        so_sb = [late.tile([P, 2 * U], F32, name="so_sb0", offset=RIN_AT + PLANE_BYTES)]
        nc.sync.dma_start(so_sb[0][:, :U], plane_rows(so, 0))
        w2_raw.append(late.tile([P, PACK, HALF], F32, name="w2_raw1", offset=W2_AT))
        nc.sync.dma_start(w2_raw[1][:], w2_rows[:, :, HALF:])

        w1_grouped = keep.tile([P, PACK * H], BF16, name="w1_grouped", align_bytes=64)
        w1_codes = keep.tile([P, H], U32, name="w1_codes", align_bytes=64)
        w1_scales = keep.tile([P, H], U8, name="w1_scales", align_bytes=64)
        cast_weight(nc, w1_raw, w1_grouped)
        quantize(nc, w1_codes[:], w1_scales[:], w1_grouped[:])

        for t in range(1, PACK):
            width = 2 * U if t == 1 else U
            so_sb.append(late.tile([P, width], F32, name=f"so_sb{t}", offset=PICKED_AT + (-2, 3, 2)[t - 1] * PLANE_BYTES))
            nc.sync.dma_start(so_sb[t][:, :U], plane_rows(so, t))

        x_picked = late.tile([P, S], U32, name="x_picked", offset=PICKED_AT, align_bytes=64)
        for first, count in quarters + halves[1:]:
            nc.vector.tensor_copy(x_picked[:, first : first + count], xw_sb[:].bitcast(U32).indirect(entries(offs_sb, first, count)))
        fetch_rin(fetch_on_scalar, 2, halves[:1])
        fetch_rin(fetch_on_vector, 2, halves[1:])
        fetch_rin(fetch_on_scalar, 3, quarters + halves[1:])

        so_picked = [keep.tile([P, S], F32, name=f"so_picked{t}") for t in range(PACK)]

        z_grouped = [keep.tile([P, PACK * HALF], BF16, name=f"z_grouped{c}", align_bytes=64) for c in range(2)]
        z_codes = [keep.tile([P, HALF], U32, name=f"z_codes{c}", align_bytes=64) for c in range(2)]
        z_scales = [keep.tile([P, HALF], U8, name=f"z_scales{c}", align_bytes=64) for c in range(2)]

        def hidden_quarter(q):
            c, first = divmod(q * QUARTER, HALF)
            tokens = slice(q * QUARTER, (q + 1) * QUARTER)
            h_bank = psum.tile([P, PACK, QUARTER], F32, name=f"h_bank{q}", tag=f"bank{q % 3}")
            for t in range(PACK):
                product(nc, h_bank[:, t, :], w1_codes, w1_scales, t, x_picked[:, tokens], xs_picked[:, tokens])
            nc.vector.tensor_tensor(
                z_grouped[c][:, first * PACK : (first + QUARTER) * PACK].rearrange("p (n i t) -> p n t i", i=2, t=PACK),
                h_bank[:].rearrange("p t (n i) -> p n t i", i=2),
                rin_picked[c][:, :, first : first + QUARTER].rearrange("p t (n i) -> p n t i", i=2),
                MULT,
            )

        for q in range(PACK):
            hidden_quarter(q)
        for c in range(2):
            quantize(nc, z_codes[c][:], z_scales[c][:], z_grouped[c][:])

        w2_grouped = [keep.tile([P, 2 * N], BF16, name=f"w2_grouped{u}", align_bytes=64) for u in range(2)]
        w2_scales = [keep.tile([P, 2 * P], U8, name=f"w2_scales{u}", align_bytes=64) for u in range(2)]

        def cast_on_gpsimd(target, source):
            nc.gpsimd.tensor_scalar(target.rearrange("p m j i -> p i m j"), source.rearrange("p m j i -> p i m j"), 1.0, 0.0, MULT, ADD)

        target, source = weight_pair_views(w2_raw[0], w2_grouped[0][:], 0, 0)
        nc.scalar.copy(target[:, :SCALAR_GROUPS], source[:, :SCALAR_GROUPS])
        cast_on_gpsimd(target[:, SCALAR_GROUPS:], source[:, SCALAR_GROUPS:])
        cast_on_gpsimd(*weight_pair_views(w2_raw[0], w2_grouped[1][:], 1, 0))
        fetch_on_scalar(so_picked[0][:], so_sb[0], 0, S)
        nc.scalar.copy(*weight_pair_views(w2_raw[1], w2_grouped[0][:], 0, 1))
        nc.vector.tensor_copy(*weight_pair_views(w2_raw[1], w2_grouped[1][:], 1, 1))
        w2_codes = [keep.tile([P, 2 * P], U32, name="w2_codes0", align_bytes=64)]
        w2_codes.append(late.tile([P, 2 * P], U32, name="w2_codes1", offset=W2_AT, align_bytes=64))
        for u in range(2):
            quantize(nc, w2_codes[u][:], w2_scales[u][:], w2_grouped[u][:])

        fetch_on_vector(so_picked[2][:, S - QUARTER :], so_sb[2], S - QUARTER, QUARTER)
        fetch_on_scalar(so_picked[1][:], so_sb[1], 0, S)
        pieces = ((0, HALF), (HALF, QUARTER), (HALF + QUARTER, QUARTER))
        for t, cuts in ((2, pieces[:2]), (3, pieces)):
            for first, count in cuts:
                fetch_on_scalar(so_picked[t][:, first : first + count], so_sb[t], first, count)

        out_flat = out.rearrange("(p t) s -> p (t s)", t=PACK)
        result = keep.tile([P, PACK * S], F32, name="result", align_bytes=ALIGN)

        def multiply_half(t, c, width):
            o_bank = psum.tile([P, HALF], F32, name=f"o_bank{t}{c}", tag=f"bank{(2 * t + c + 3) % 8}")
            product(nc, o_bank[:], w2_codes[t // 2], w2_scales[t // 2], t % 2, z_codes[c][:], z_scales[c][:])
            for first in range(0, HALF, width):
                token = c * HALF + first
                nc.vector.tensor_tensor(result[:, t * S + token : t * S + token + width], o_bank[:, first : first + width], so_picked[t][:, token : token + width], MULT)

        stored = 0
        for half in range(2 * PACK):
            t, c = divmod(half, 2)
            multiply_half(t, c, QUARTER if half == 2 * PACK - 1 else HALF)
            if half not in (3, 5):
                done = (half + 1) * HALF
                nc.sync.dma_start(out_flat[:, stored:done], result[:, stored:done])
                stored = done
